import numpy as np, ml_dtypes
CORES = [10,34,74,98]
N = 4
BF = ml_dtypes.bfloat16
def gentries(a):
    return np.ascontiguousarray(a.reshape(8, 16, -1).transpose(0, 2, 1)).reshape(8, -1)
def gtable(e):
    e = np.asarray(e); return np.ascontiguousarray(e.reshape(8, -1, 16).transpose(0, 2, 1)).reshape(128, -1).astype(np.int32)
V, P, T, TL, Q, M = 3584, 256, 8, 4, 9, 4096
def money(rng, base):
    v = base + rng.integers(-3, 4, base.shape[:2] + (16, base.shape[-1]))
    return np.clip(np.floor(v), 0, 15).astype(np.int64)
def parts(rng):
    x = money(rng, 16 * rng.random((N, 8, 1, V)) ** rng.choice(np.array([2.0, 3.0, 5.0]), (N, 8, 1, 1)))
    price = money(rng, 16 * rng.random((N, 8, 1, P)))
    pool = rng.integers(0, V, (N, 8, 64))
    pop = np.take_along_axis(pool, rng.integers(0, 64, (N, 8, 16 * V)), 2).reshape(N, 8, 16, V)
    kin = np.where(rng.random((N, 8, 16, V)) < 0.15, pop, rng.integers(0, V, (N, 8, 16, V)))
    few = np.take_along_axis(pool, rng.integers(0, 48, (N, 8, P)), 2)
    own = np.where(rng.random((N, 8, P)) < 0.5, few, rng.integers(0, V, (N, 8, P)))
    hold = rng.integers(0, V, (N, 8, P)); wall = rng.integers(0, 2, (N, 8, P)); wt = rng.integers(0, 256, (N, 8, 16))
    return x, kin, own, hold, wall, price, wt
def pack(x, kin, own, hold, wall, price, wt):
    return {"x": np.ascontiguousarray(x.reshape(N, 128, V)).astype(np.float32).astype(BF), "kin": np.ascontiguousarray(kin.reshape(N, 128, V)).astype(np.int32),
            "own": np.stack([gtable(a) for a in own]), "hold": np.stack([gtable(a) for a in hold]), "wall": np.stack([gtable(a) for a in wall]),
            "price": np.ascontiguousarray(price.reshape(N, 128, P)).astype(np.float32).astype(BF), "wt": np.ascontiguousarray(wt.reshape(N, 128, 1)).astype(np.int32)}
def setup_inputs(rng):
    return pack(*parts(rng))
def setup_inputs_alike(rng):
    x, kin, own, hold, wall, price, wt = parts(rng)
    kin[:, 0] = kin[:, 0, :, :1].copy()
    kin[:, 1] = kin[:, 1, :1, :].copy()
    own[:, 2] = own[:, 2, :1].copy()
    kin[:, 3] = rng.integers(0, V, (N, 1, 1))
    own[:, 4] = np.take_along_axis(rng.integers(0, V, (N, 3)), rng.integers(0, 3, (N, P)), 1)
    own[:, 5] = np.argsort(rng.random((N, V)), axis=-1)[:, :P]; price[:, 5] = 15; x[:, 5] = 0; x[:, 5, 3] = rng.integers(0, 2, (N, V))
    own[1::2, 5, P - 1] = own[1::2, 5, 0]; price[1::2, 5, 3, P - 1] = 0
    x[:, 6] = x[:, 6, :, :1].copy(); hold[:, 6] = hold[:, 6, :1].copy()
    kin[:, 7] = rng.choice(np.array([0, 1, V - 2, V - 1]), (N, 16, V)); own[:, 7] = rng.choice(np.array([0, V - 1]), (N, P))
    return pack(x, kin, own, hold, wall, price, wt)
def setup_inputs_corners(rng):
    x, kin, own, hold, wall, price, wt = parts(rng); q = rng.permutation(8); a = np.arange(V)
    for r in range(N):
        g = q[0]; x[r, g] = 0; price[r, g] = 15; kin[r, g] = np.minimum(a + 1, V - 1); own[r, g, ::8] = V - 1; own[r, g, 1::8] = 0; own[r, g, 2::8] = V - 2
        g = q[1]; kin[r, g] = a; own[r, g, :2] = 0; own[r, g, P - 2:] = V - 1
        g = q[2]; price[r, g] = 0; wt[r, g] = 255 * (r % 2)
        g = q[3]; x[r, g] = 15; price[r, g] = 15; wt[r, g] = 255; wall[r, g] = 1; hold[r, g, ::2] = V - 1; hold[r, g, 1::4] = 0
        kin[r, g, 0] = rng.permutation(V); own[r, g] = rng.permutation(V)[:P]
        if r % 2 == 1: own[r, g, P - 1] = own[r, g, 0]; price[r, g, :, P - 1] = 7
        g = q[4 + r % 4]; kin[r, g] = rng.integers(0, 2, (16, V)) * (V - 1); own[r, g] = rng.integers(0, 2, P) * (V - 1)
        g = q[4 + (r + 1) % 4]; wall[r, g] = 0; wt[r, g] = 0
        g = q[4 + (r + 2) % 4]; x[r, g] = 0; x[r, g, :, 0] = 15; price[r, g] = 15; kin[r, g] = np.maximum(a - 1, 0); own[r, g] = rng.integers(0, 2 * T, P)
        g = q[4 + (r + 3) % 4]; wall[r, g] = 1; hold[r, g] = rng.integers(0, 2, P) * (V - 1); kin[r, g, :, V - 1] = 0; kin[r, g, :, 0] = V - 1
    return pack(x, kin, own, hold, wall, price, wt)
def setup_inputs_ends(rng):
    def rec(n):
        k = rng.random((N, 8, 1, n)); el = rng.integers(0, 2, (N, 8, 16, n))
        return 15 * np.where(k < 0.35, 0, np.where(k < 0.7, 1, el))
    x = rec(V); price = rec(P)
    kin = np.where(rng.random((N, 8, 1, V)) < 0.7, rng.integers(0, 2, (N, 8, 16, V)) * (V - 1), rng.integers(0, V, (N, 8, 16, V)))
    own = np.where(rng.random((N, 8, P)) < 0.7, rng.integers(0, 2, (N, 8, P)) * (V - 1), rng.integers(0, V, (N, 8, P)))
    hold = np.where(rng.random((N, 8, P)) < 0.75, rng.integers(0, 2, (N, 8, P)) * (V - 1), rng.integers(0, V, (N, 8, P)))
    wall = rng.integers(0, 2, (N, 8, P)); wt = 255 * rng.integers(0, 2, (N, 8, 16)); wt[N - 1, 7] = 255; wt[N - 1, 0, 0] = 0
    for g in range(8):
        x[:, g, :, 0] = (0, 15, 0, 15)[g % 4]; x[:, g, :, V - 1] = (15, 0, 0, 15)[g % 4]
    x[:, 7, :, 0] = 0; x[:, 7, :, 4] = 0; x[:, 7, :, V - 1] = 15
    kin[:, 7, :, V - 1] = V - 1; kin[:, 7, :, 0] = 0; kin[:, 7, 0::2, 2] = 4; kin[:, 7, 1::2, 2] = 0
    own[:, 7, 0] = V - 1; price[:, 7, :, 0] = 0; wall[:, 7, 0] = 0
    own[:, 7, P - 8:] = V - 1; hold[:, 7, P - 8:] = V - 1; wall[:, 7, P - 8:] = 1
    own[:, 7, P - 16:P - 8] = 0; own[:, 7, P - 24:P - 16] = 2; price[:, 7, :, P - 24:] = 15
    x[:, 5, :, V - 2] = 0; kin[:, 5, :, V - 2] = V - 2; own[:, 5, P - 2:] = V - 2; wall[:, 5, P - 2:] = 0; price[:, 5, :, P - 2:] = 15
    y = 15 >> (T // TL); s = [a for a in range(V, 61201, M) if a % y == 0][0] // y
    for r in range(N):
        wt[r, 5] = rng.permutation(np.array([255] * (s // 255) + [s % 255] + [0] * (15 - s // 255)))
    return pack(x, kin, own, hold, wall, price, wt)
def setup_inputs_spread(rng):
    def skew(top, p, *shape):
        return np.minimum(np.floor(top * rng.random(shape) ** p), top - 1).astype(np.int64)
    x = skew(16, np.exp2(rng.integers(-2, 4, (N, 8, 1, V)) + rng.integers(0, 2, (N, 8, 16, 1))), N, 8, 16, V)
    price = skew(16, np.exp2(rng.integers(-3, 3, (N, 8, 1, P)) + rng.integers(0, 2, (N, 8, 16, 1))), N, 8, 16, P)
    kin = skew(V, np.exp2(rng.integers(-1, 4, (N, 8, 16, 1))), N, 8, 16, V)
    own = skew(V, np.exp2(rng.integers(-2, 4, (N, 8, 1))), N, 8, P); hold = skew(V, np.exp2(rng.integers(-3, 4, (N, 8, 1))), N, 8, P)
    wall = (rng.random((N, 8, P)) < rng.choice(np.array([0.1, 0.5, 0.9]), (N, 8, 1))).astype(np.int64)
    wt = np.minimum(np.floor(np.exp2(8.02 * rng.random((N, 8, 16)))).astype(np.int64) - 1, 255)
    return pack(x, kin, own, hold, wall, price, wt)
def setup_inputs_ties(rng):
    x, kin, own, hold, wall, price, wt = parts(rng)
    n = Q - 2 + rng.integers(0, 2, (N, 8, 1, V)) + (rng.random((N, 8, 1, V)) < 0.03) + (np.arange(8) % 2).reshape(1, 8, 1, 1)
    x = 6 + (np.argsort(rng.random((N, 8, 16, V)), axis=2) < n).astype(np.int64)
    price = np.broadcast_to(rng.choice(np.array([6, 7, 7, 7, 7, 7, 7, 8]), (N, 8, 1, P)), (N, 8, 16, P)).copy()
    i = int(rng.integers(0, 16)); x[:, 6, :, V - 1] = 11; x[:, 6, i, V - 1] = 1
    k6 = kin[:, 6]; k6[k6 == V - 1] = V - 2; kin[:, 6, :, V - 1] = V - 1
    o6 = own[:, 6]; o6[o6 == V - 1] = 0; own[:, 6, P - 2:] = V - 1; wall[:, 6] = 0; price[:, 6, :, P - 2:] = 15
    ya, yz = 15, 15
    for _ in range(T // TL):
        ya, yz = (ya + 11) >> 1, (yz + 1) >> 1
    for r in range(N):
        s = 32768 if r % 2 == 0 else 7 * M
        c = [a for a in range(256) if (s - yz * a) % ya == 0][0]; rest = (s - yz * c) // ya
        wt[r, 6] = np.insert(rng.permutation(np.array([255] * (rest // 255) + [rest % 255] + [0] * (14 - rest // 255))), i, c)
    return pack(x, kin, own, hold, wall, price, wt)
def check_inputs(d):
    bad = []
    for k, hi in (("x", 15), ("kin", V - 1), ("own", V - 1), ("hold", V - 1), ("wall", 1), ("price", 15), ("wt", 255)):
        a = np.asarray(d[k]).astype(np.float64)
        if not (np.min(a) >= 0 and np.max(a) <= hi): bad.append("range of " + k)
        elif np.any(a != np.floor(a)): bad.append("whole numbers in " + k)
    return bad
def reference(x, kin, own, hold, wall, price, wt):
    X = x.astype(np.float32).astype(np.int32).reshape(N, 8, 16, V); K = kin.astype(np.int64).reshape(N, 8, 16, V)
    heir = np.tile(np.arange(V), (N, 8, 1)); lane = np.arange(P)
    e = np.stack([gentries(a) for a in own]).astype(np.int64); h = np.stack([gentries(a) for a in hold]).astype(np.int64); wl = np.stack([gentries(a) for a in wall])
    y = price.astype(np.float32).astype(np.int32).reshape(N, 8, 16, P); w = wt.astype(np.int64).reshape(N, 8, 16, 1)
    for t in range(T):
        for r in range(N):
            s = (r + t) % N; XS, KS, HS, ys, hs, es = X[s], K[s], heir[s], y[r], h[r], e[r].copy()
            c = np.take_along_axis(KS, es[:, None, :], 2)
            d = np.take_along_axis(XS, c.reshape(8, 1, 16 * P), 2).reshape(8, 16, 16, P) - ys[:, :, None, :]
            solvent = np.add.reduce((d >= 0).astype(np.int32), axis=1) >= Q; score = np.add.reduce(np.abs(d), axis=1)
            offers = np.any(solvent, axis=1)
            k = np.where(offers, np.argmax(solvent, axis=1), np.argmin(score, axis=1))
            b = np.take_along_axis(c, k[:, None, :], 1)[:, 0]
            key = np.where(offers, b, V + es)
            first = np.argmax(key[:, :, None] == key[:, None, :], axis=2) == lane
            fg, fp = np.nonzero(first & ~offers); ef, f = es[fg, fp], b[fg, fp]
            KS[fg, 1::2, ef] = KS[fg, 1::2, f]
            HS[fg, ef] = f
            wg, wp = np.nonzero(first & offers); cw = b[wg, wp]
            XS[wg, :, cw] = np.maximum(XS[wg, :, cw] - (ys[wg, :, wp] >> 2), 0)
            ys[wg, :, wp] = np.minimum(ys[wg, :, wp] + 1, 15); hs[wg, wp] = cw
            es = np.take_along_axis(HS, es, 1)
            if t % TL == TL - 1:
                es = np.where(wl[r] == 1, hs, es)
                y[r] = (ys + np.take_along_axis(XS, es[:, None, :], 2)) >> 1
                u = np.add.reduce(w[s] * y[r], axis=1) & (M - 1)
                h[r] = np.where(u >= V, u - V, u)
            e[r] = es
    yk = np.add.reduce(K * np.arange(1, 17).reshape(1, 1, 16, 1), axis=2)
    return {"yx": X.reshape(N, 128, V).astype(np.float32).astype(BF), "yk": yk.astype(np.float32), "yh": heir.astype(np.float32), "yo": e.astype(np.float32), "yt": h.astype(np.float32)}

@@ -1,0 +1,504 @@
+from concourse.bass import DstId, RemoteDMATransfer
+from concourse.mybir import dt, AluOpType, AxisListType, ActivationFunctionType
+
+V, NP, NT, TERM = 3584, 256, 8, 4
+W = 2 * V + NP
+CH = 64
+NCH = NP // CH
+RDF = True
+NE = 11
+BIG = float(2 ** 28)
+
+_S = {}
+
+
+def _sb(n, w, d):
+    _S[n] = ("sbuf", [128, w], d)
+
+
+F, B, I, U = "float32", "bfloat16", "int32", "uint16"
+for _n, _w, _d in [
+        ("K", W, F), ("KI", V, I), ("X", W, B), ("H", W, F), ("YK", W, F),
+        ("OWN", 16, I), ("WL", 16, I), ("WR", 16, I), ("HI0", 16, I), ("WTI", 1, I),
+        ("RE", 16 * NT, U), ("RP", NP * NT, B), ("RH", 16 * NT, F), ("FIN", 32, F),
+        ("EN", 16 * NT, U), ("PO", NP * NT, B), ("HO", 16 * NT, F), ("FO", 32, F),
+        ("CU", NP, U), ("KC0", NP, F), ("PR", 16 * NP, B), ("D", 16 * NP, B), ("AB", 16 * NP, B), ("GE", 16 * NP, B),
+        ("KB", NP, F), ("KEY", NP, F), ("T1", NP, F), ("SC", NP, F),
+        ("MI", 16, I), ("BI", 16, I), ("FB", 16, F), ("KT", 16, F), ("KL", 16, F), ("EV", 16, F),
+        ("KLT", 16, F), ("OF1", 16, F), ("OF2", 16, F), ("OFS", 16, U),
+        ("BU", 16, U), ("EXK", NP, F), ("EXB", NP, F), ("KR", NP, U), ("E", 16 * NP, B), ("FD", NP, B), ("FS", NP, F),
+        ("BR", NP, F), ("EG", NP, F), ("ES", NP, F), ("T4", NP, B), ("XG", NP, B), ("XV", NP, B),
+        ("SKF", NP, F), ("SCE", NP, F), ("THO", NP, F), ("RD", NP, B), ("PN", NP, B), ("EA", NP * 2, F),
+        ("RL", 16, F), ("BH", 16, F), ("BH2", 16, F), ("HN", 16, F), ("DW", 16, F), ("DW2", 16, F), ("EJ", 16, F), ("WF", 16, F),
+        ("PJ1", NP, B), ("PJ2", NP, B), ("HI", 16, I), ("HA", 16, I), ("HG", 16, F), ("YF", NP, F), ("YO", NP, F), ("YT", NP, F),
+        ("IP", 1, I), ("ICF", NP, F), ("CMF", NP, F), ("CGF", 128, F), ("TRB", 16, F),
+        ("PMI", 1, I), ("PAI", 1, I), ("ODI", 1, I), ("COL", 16, F),
+        ("IDF", 128, F), ("BDF", 128, F), ("YW", 128, F), ("LUS", 512, F), ("WS", 144, F), ("WA", 144, B), ("WB", 144, B), ("WH", 144, B),
+        ("BD17", 128, B), ("W1", 128, B), ("IDB", 128, B), ("NIDB", 128, B), ("DIAG", NP, F), ("RS", NP, F), ("SEG", NP, F),
+        ("PWD", 16, F), ("TH", NP, B), ("THD", NP, F), ("TR", 16, F), ("SOFF", NP, U)]:
+    _sb(_n, _w, _d)
+COLS = ["PF", "PM", "PG", "PG15", "PAR", "PA1", "ODD", "EVN", "KCOL", "KEV", "K1", "POW", "WTF", "PFM", "PFP", "POH"]
+for _n in ["pA0", "pB0", "pA1", "pB1", "pL", "pR", "pR2", "pD"]:
+    _S[_n] = ("psum", [128, 512], F)
+SCRATCH = _S
+NDMA = 24
+SEMAPHORES = (["qV", "qS", "qT", "qG", "loc", "aW", "aF"] + ["aE%d" % t for t in range(NT)] + ["aP%d" % t for t in range(NT)]
+              + ["aH%d" % t for t in range(NT)] + ["d%d" % k for k in range(NDMA)])
+
+
+def rank_program(g, core, T, topo):
+    rank = T.rank_of(core)
+    if rank is None:
+        return
+    nxt, prv = T.cores[(rank + 1) % 4], T.cores[(rank + 3) % 4]
+    op = AluOpType
+    AF = ActivationFunctionType
+    queues = {"V": g.vector, "S": g.scalar, "T": g.tensor, "G": g, "Y": g.sync}
+    count = {}
+    known = {q: {} for q in queues}
+    log = {}
+    order = [0]
+    ndma = [0]
+    nloc = [0]
+
+    def A(n, a=0, b=None, s=1):
+        if n in COLS:
+            return ("COL", COLS.index(n), COLS.index(n) + 1, 1)
+        return (n, a, _S[n][1][1] if b is None else b, s)
+
+    def IND(w, o):
+        return ("ind", w, o)
+
+    def ap(x):
+        if not isinstance(x, tuple):
+            return x
+        if x[0] == "ind":
+            return ap(x[1]).indirect(ap(x[2]))
+        n, a, b, s = x
+        return T[n][:, a:b] if s == 1 else T[n][:, a:b:s]
+
+    def regs(x):
+        if not isinstance(x, tuple):
+            return []
+        return [x[1], x[2]] if x[0] == "ind" else [x]
+
+    def psum(n):
+        return _S[n][0] == "psum"
+
+    def need(q, reads, writes):
+        ev = []
+        for lst, wr in ((reads, False), (writes, True)):
+            for r in lst:
+                for e in log.get(r[0], []):
+                    if psum(r[0]):
+                        if e[3] == q and (q == "T" or not (wr or e[2])):
+                            continue
+                        ev.append(e[4])
+                    elif e[0] < r[2] and r[1] < e[1] and (wr or e[2]):
+                        ev.append(e[4])
+        ev.sort(key=lambda e: -e[0])
+        for e in ev:
+            if known[q].get(e[1], 0) >= e[2]:
+                continue
+            queues[q].wait_ge(T.sem[e[1]], e[2])
+            for k, v in e[3].items():
+                known[q][k] = max(known[q].get(k, 0), v)
+
+    def note(q, reads, writes, event):
+        for r in writes:
+            l = log.setdefault(r[0], [])
+            if r[3] == 1 or psum(r[0]):
+                lo, hi = (0, 1 << 20) if psum(r[0]) and q != "T" else (r[1], r[2])
+                l[:] = [e for e in l if not (lo <= e[0] and e[1] <= hi)]
+            l.append((r[1], r[2], True, q, event))
+        for r in reads:
+            l = log.setdefault(r[0], [])
+            l[:] = [e for e in l if not (not e[2] and e[3] == q and r[1] <= e[0] and e[1] <= r[2])]
+            l.append((r[1], r[2], False, q, event))
+
+    def event(q, sem, val):
+        order[0] += 1
+        c = dict(known[q])
+        c[sem] = val
+        return (order[0], sem, val, c)
+
+    def emit(q, reads, writes, fn):
+        need(q, reads, writes)
+        sem = "q" + q
+        count[sem] = count.get(sem, 0) + 1
+        fn().then_inc(T.sem[sem], 1)
+        note(q, reads, writes, event(q, sem, count[sem]))
+
+    def external(x, sem, val):
+        order[0] += 1
+        log.setdefault(x[0], []).append((x[1], x[2], True, "X", (order[0], sem, val, {sem: val})))
+
+    def tt(out, a, b, o, q="V"):
+        wr = [out[1]] if out[0] == "ind" else [out]
+        rd = regs(a) + regs(b) + ([out[2]] if out[0] == "ind" else [])
+        emit(q, rd, wr, lambda: g.vector.tensor_tensor(ap(out), ap(a), ap(b), o))
+
+    def ts(out, a, s1, o1, s2=None, o2=None):
+        rd = regs(a) + regs(s1) + regs(s2)
+        if o2 is None:
+            emit("V", rd, [out], lambda: g.vector.tensor_scalar(ap(out), ap(a), ap(s1), None, o1))
+        else:
+            emit("V", rd, [out], lambda: g.vector.tensor_scalar(ap(out), ap(a), ap(s1), ap(s2), o1, o2))
+
+    def cp(out, a):
+        wr = [out[1]] if out[0] == "ind" else [out]
+        emit("V", regs(a) + ([out[2]] if out[0] == "ind" else []), wr, lambda: g.vector.tensor_copy(ap(out), ap(a)))
+
+    def scan(out, d0, d1, init, o0, o1):
+        emit("V", [d0, d1], [out], lambda: g.vector.tensor_tensor_scan(ap(out), ap(d0), ap(d1), init, o0, o1))
+
+    def vtr(out, a):
+        emit("V", [a], [out], lambda: g.vector.transpose(ap(out), ap(a)))
+
+    def fill(out, c):
+        emit("V", [], [out], lambda: g.vector.memset(ap(out), c))
+
+    def act(out, a, f, bias=0.0, scale=1.0):
+        emit("S", regs(a) + regs(bias) + regs(scale), [out],
+             lambda: g.scalar.activation(ap(out), ap(a), f, bias=ap(bias), scale=ap(scale)))
+
+    def mm(out, l, r, start, stop):
+        emit("T", [l, r], [out], lambda: g.tensor.matmul(ap(out), ap(l), ap(r), start, stop))
+
+    def dma(q, out, in_, reads, writes):
+        need(q, reads, writes)
+        sem = "d%d" % ndma[0]
+        ndma[0] += 1
+        queues[q].dma_start(out, in_).then_inc(T.sem[sem], 16)
+        note(q, reads, writes, event(q, sem, 16))
+        return sem
+
+    def send(dst, out, in_, sem):
+        need("G", [in_], [])
+        rid, pid = topo.addr(dst)[:2]
+        m = topo.engines(core, dst)[:8]
+        mask = sum(1 << e for e in m)
+        g.remote_dma(ap(out), ap(in_), T.sem[sem], T.sem.loc, pid, rid, mask)
+        nloc[0] += len(m)
+
+    def arrives(src, x, sem):
+        external(x, sem, len(topo.engines(src, core)[:8]))
+
+    for q, n, src in (("Y", "OWN", T.own), ("Y", "WL", T.wall), ("Y", "HI0", T.hold), ("Y", "WTI", T.wt)):
+        dma(q, T[n][:, :], src[:, :], [], [A(n)])
+    dma("S", T.PN[:, :], T.price[:, :], [], [A("PN")])
+    for k in range(4):
+        a, b = 896 * k, 896 * k + 896
+        dma("YS"[k % 2], T.KI[:, a:b], T.kin[:, a:b], [], [A("KI", a, b)])
+    for k in range(2):
+        a, b = 1792 * k, 1792 * k + 1792
+        dma("YS"[k % 2], T.X[:, a:b], T.x[:, a:b], [], [A("X", a, b)])
+
+    def iota(x, pattern, base=0, per=0):
+        flag = {"allow_small_or_imprecise_dtypes": True} if _S[x[0]][2] == F else {}
+        emit("G", [], [x], lambda: g.iota(ap(x), pattern, base, per, **flag))
+
+    iota(A("IP"), [[1, 1]], 0, 1)
+    iota(A("PF"), [[1, 1]], 0, 1)
+    iota(A("CMF"), [[0, 16], [1, 16]])
+    iota(A("ICF"), [[1, NP]])
+    iota(A("CGF"), [[16, 8], [0, 16]])
+    iota(A("TRB"), [[16, 16]], 2 * V)
+    send(prv, A("WR"), A("WL"), "aW")
+    arrives(nxt, A("WR"), "aW")
+    iota(A("H", V, 2 * V), [[1, V]])
+    ts(A("PMI"), A("IP"), 15, op.bitwise_and)
+    ts(A("PAI"), A("IP"), 4, op.arith_shift_right, 1, op.bitwise_and)
+    ts(A("ODI"), A("IP"), 1, op.bitwise_and)
+    cp(A("PM"), A("PMI"))
+    cp(A("PAR"), A("PAI"))
+    cp(A("ODD"), A("ODI"))
+    tt(A("PG"), A("PF"), A("PM"), op.subtract)
+    ts(A("PG15"), A("PG"), 15.0, op.add)
+    ts(A("KCOL"), A("PM"), 4096.0, op.mult)
+    ts(A("DIAG"), A("CMF"), A("PM"), op.is_equal)
+    ts(A("RS"), A("CMF"), 0.0, op.is_equal, float(2 ** 25), op.mult)
+    ts(A("SEG"), A("CMF"), 0.0, op.not_equal)
+    cp(A("SOFF"), A("ICF"))
+    ts(A("WS"), A("ICF", 0, 144), A("PG15"), op.is_equal)
+    act(A("WA"), A("WS"), AF.Identity, scale=65536.0)
+    act(A("WB"), A("WS"), AF.Identity, scale=-BIG)
+    ts(A("RP", 0, NP), A("PN"), -1.0, op.mult, 15.0, op.add)
+    cp(A("RE", 0, 16), A("OWN"))
+    ts(A("IDF"), A("ICF", 0, 128), A("PF"), op.is_equal)
+    act(A("IDB"), A("IDF"), AF.Identity)
+    act(A("NIDB"), A("IDF"), AF.Identity, scale=-1.0)
+    ts(A("BDF"), A("CGF"), A("PG"), op.is_equal)
+    act(A("BD17"), A("BDF"), AF.Identity, scale=-float(2 ** 17))
+    ts(A("PA1"), A("PAR"), -1.0, op.mult, 1.0, op.add)
+    ts(A("PFM"), A("PF"), -16.0, op.add)
+    ts(A("PFP"), A("PF"), 16.0, op.add)
+    for u in range(2):
+        for s in range(2):
+            j = 2 * u + s
+            ts(A("LUS", 128 * j, 128 * j + 128), A("ICF", 0, 128), A(("PFM", "PF", "PFP")[s - u + 1]), op.is_equal, A("PAR" if u else "PA1"), op.mult)
+    ts(A("KB"), A("CMF"), 0.0, op.is_equal, 65536.0, op.mult)
+    ts(A("KEY"), A("SEG"), 0.5, op.mult)
+    scan(A("TH"), A("KEY"), A("KB"), 0.0, op.mult, op.add)
+    act(A("THD"), A("DIAG"), AF.Identity, bias=float(2 ** 17), scale=-float(2 ** 17))
+    tt(A("PWD"), A("TH", 0, 16), A("DIAG", 0, 16), op.mult)
+    emit("V", [A("PWD")], [A("POW")], lambda: g.vector.tensor_reduce(ap(A("POW")), T.PWD[:, :], AxisListType.X, op.add))
+    ts(A("POH"), A("POW"), -0.5, op.mult)
+    act(A("W1"), A("BDF"), AF.Identity, scale=A("POH"))
+    ts(A("TR"), A("TRB"), A("PM"), op.add)
+    ts(A("EVN"), A("ODD"), -1.0, op.mult, 1.0, op.add)
+    ts(A("KEV"), A("KCOL"), -1.0, op.mult, A("EVN"), op.mult)
+    ts(A("K1"), A("PM"), 1.0, op.add)
+    act(A("YW"), A("BDF"), AF.Identity, scale=A("K1"))
+    cp(A("WTF"), A("WTI"))
+    act(A("WH"), A("WS"), AF.Identity, scale=A("WTF"))
+    cp(A("RH", 0, 16), A("HI0"))
+    for k in range(4):
+        a, b = 896 * k, 896 * k + 896
+        cp(A("K", V + a, V + b), A("KI", a, b))
+    pend = []
+
+    def pa(c):
+        return ("pA0", "pB0") if c < NCH - 1 else ("pA1", "pB1")
+
+    for t in range(NT):
+        e = A("RE", 16 * t, 16 * t + 16)
+        price = A("RP", NP * t, NP * t + NP)
+        hold = A("RH", 16 * t, 16 * t + 16)
+        jub = t % TERM == TERM - 1
+        last = t == NT - 1
+        if t:
+            arrives(prv, price, "aP%d" % t)
+            arrives(prv, e, "aE%d" % t)
+            arrives(prv, hold, "aH%d" % t)
+        Kg, Xg = A("K", V, 2 * V), A("X", 0, V)
+
+        def rep(c):
+            act(A("PR", 1024 * c, 1024 * c + 1024), IND(price, A("SOFF", CH * c, CH * c + CH)), AF.Identity)
+
+        def part(n, c):
+            w = 1024 if c < NCH - 1 else 512
+            return A(n, int(1024 * c), int(1024 * c) + w)
+
+        def dif(c):
+            x = part("D", c)
+            tt(x, IND(Xg, A("CU", x[1] // 16, x[2] // 16)), part("PR", c), op.add)
+
+        def cmp(c):
+            ts(part("GE", c), part("D", c), 15.0, op.is_ge, -0.53125, op.add)
+
+        def absd(c):
+            act(part("AB", c), part("D", c), AF.Abs, bias=-15.0)
+
+        def sums(c):
+            a, b = pa(c)
+            lo, hi = CH * c, CH * c + CH
+            if c == 0:
+                mm(A("pA0", 0, NP - CH), A("IDF"), A("KC0", 0, NP - CH), True, False)
+                mm(A("pA1", NP - CH, NP), A("IDF"), A("KC0", NP - CH, NP), True, False)
+            for k in range(16):
+                mm(A(b, lo, hi), A("WB", 15 - k, 143 - k), A("GE", 1024 * c + k, 1024 * c + 1024, 16), k == 0, k == 15)
+            for k in range(16):
+                mm(A(a, lo, hi), A("WA", 15 - k, 143 - k), A("AB", 1024 * c + k, 1024 * c + 1024, 16), False, k == 15 and c >= NCH - 2)
+
+        def best(c0, c1):
+            lo, hi = CH * c0, CH * c1
+            a, b = pa(c0)
+            tt(A("KB", lo, hi), A(b, lo, hi), A("KC0", lo, hi), op.max)
+            tt(A("KEY", lo, hi), A(a, lo, hi), A("KB", lo, hi), op.min)
+            vtr(A("T1", lo, hi), A("KEY", lo, hi))
+            scan(A("SC", lo, hi), A("RS", lo, hi), A("T1", lo, hi), float(2 ** 25), op.add, op.min)
+
+        rep(0)
+        rep(1)
+        cp(A("CU"), IND(Kg, e))
+        dif(0)
+        ts(A("KC0"), A("CU"), A("KCOL"), op.add)
+        cmp(0)
+        absd(0)
+        rep(2)
+        sums(0)
+        dif(1)
+        cmp(1)
+        absd(1)
+        rep(3)
+        sums(1)
+        dif(2)
+        cmp(2)
+        absd(2)
+        sums(2)
+        dif(3)
+        absd(3)
+        dif(3.5)
+        cmp(3)
+        absd(3.5)
+        cmp(3.5)
+        sums(3)
+        best(0, NCH - 1)
+        best(NCH - 1, NCH)
+        ts(A("EV"), e, float(V), op.add)
+        if t == 0:
+            cp(A("WF"), A("WR"))
+        while pend:
+            pend.pop(0)()
+        act(A("T4"), price, AF.Identity, bias=163.375, scale=-0.25)
+        act(A("SCE"), A("KC0"), AF.Identity, bias=A("KEV"), scale=A("EVN"))
+        for u in range(2):
+            for s in range(2):
+                j = 2 * u + s
+                mm(A("pL", u, 16, 2), A("LUS", 128 * j, 128 * j + 128), A("SC", 15 + 16 * s, NP, 32), s == 0, s == 1)
+        mm(A("pD", 0, NP), A("IDB"), A("TH"), True, False)
+        cp(A("MI"), A("pL", 0, 16))
+        ts(A("FB"), A("pL", 0, 16), 65536.0, op.is_ge, 8192.0, op.mult)
+        ts(A("BI"), A("MI"), 4095, op.bitwise_and)
+        tt(A("KT"), A("BI"), A("FB"), op.add)
+        tt(A("KL"), A("KT"), A("EV"), op.min)
+        tt(A("EXK"), IND(A("KL"), A("SOFF", 0, 16)), A("DIAG"), op.mult)
+        mm(A("pR", 0, NP), A("BDF"), A("EXK"), True, True)
+        cp(A("BU"), A("BI"))
+        tt(A("KLT"), A("KL"), A("TR"), op.subtract)
+        act(A("XG"), IND(Xg, A("BU")), AF.Identity)
+        cp(A("KR"), A("pR", 0, NP))
+        ea = 0
+        for j in range(NE, 16):
+            w = NP - 16 * j
+            act(A("EA", ea, ea + w), A("pR", 16 * j, NP), AF.Abs, bias=A("KL", j, j + 1), scale=-1.0)
+            ea += w
+        act(A("E", NP * NE, NP * NE + ea), A("EA", 0, ea), AF.Relu, bias=1.0, scale=-1.0)
+        act(A("THO"), A("pR", 0, NP), AF.Relu, bias=-float(2 ** 17 * (V - 1)), scale=float(2 ** 17))
+        ea = NP * NE
+        for j in range(16):
+            lo = 16 * j
+            if j < NE:
+                x = A("E", NP * j + lo, NP * j + NP)
+                ts(x, A("KR", lo, NP), A("KL", j, j + 1), op.is_equal)
+            else:
+                x = A("E", ea, ea + NP - lo)
+                ea += NP - lo
+            mm(A("pD", lo, lo + 16), A("W1"), A("E", x[1], x[1] + 16), False, j == 15)
+            if j < 15:
+                mm(A("pD", lo + 16, NP), A("BD17"), A("E", x[1] + 16, x[2]), False, False)
+        tt(A("EXB"), IND(A("BI"), A("SOFF", 0, 16)), A("DIAG"), op.mult)
+        mm(A("pR2", 0, NP), A("BDF"), A("EXB"), True, True)
+        act(A("BR"), A("pR2", 0, NP), AF.Identity)
+        mm(A("pB1", 0, NP), A("IDB"), A("XG"), True, False)
+        mm(A("pB1", 0, NP), A("NIDB"), A("T4"), False, True)
+        tt(A("FD"), A("pD", 0, NP), A("THD"), op.is_gt)
+        if RDF:
+            tt(A("RD"), A("pD", 0, NP), A("THO"), op.is_gt)
+        scan(A("FS"), A("SEG"), A("FD"), 0.0, op.mult, op.add)
+        fl = A("FS", 15, NP, 16)
+        tt(A("OF1"), fl, A("KLT"), op.mult)
+        if not RDF:
+            tt(A("RD"), A("pD", 0, NP), A("THO"), op.is_gt)
+        tt(A("OF2"), A("OF1"), A("TR"), op.add)
+        cp(A("OFS"), A("OF2"))
+        pn = A("PN") if jub else A("PO", NP * t, NP * t + NP)
+        mm(A("pA1", 0, NP), A("IDB"), price, True, False)
+        mm(A("pA1", 0, NP), A("NIDB"), A("RD"), False, True)
+        act(pn, A("pA1", 0, NP), AF.Relu)
+        if not jub:
+            send(nxt, A("RP", NP * t + NP, NP * t + 2 * NP), pn, "aP%d" % (t + 1))
+        act(A("SKF"), IND(Kg, A("BU")), AF.Identity, scale=A("ODD"))
+        act(A("XV"), A("pB1", 0, NP), AF.Relu, bias=160.0)
+        if last:
+            ybase(g, T, A, mm, act, AF, range(3, 7))
+            mm(A("pA1", 0, NP), A("YW"), A("SKF"), True, False)
+            mm(A("pA1", 0, NP), A("YW"), A("SCE"), False, True)
+            act(A("YF"), A("pA1", 0, NP), AF.Identity)
+        cp(IND(A("H"), A("OFS")), A("BR"))
+        tt(A("EG"), IND(A("H", V, 2 * V), e), A("DIAG"), op.mult)
+
+        def xpart():
+            cp(IND(A("X"), A("OFS")), A("XV"))
+
+        def hpart(out, hold=hold):
+            ts(A("RL"), A("OF2"), float(V), op.is_lt)
+            tt(A("BH"), A("OF2"), hold, op.subtract)
+            tt(A("BH2"), A("RL"), A("BH"), op.mult)
+            tt(out, A("BH2"), hold, op.add)
+
+        def kpart():
+            tt(IND(A("K"), A("OFS")), A("SKF"), A("SCE"), op.add)
+
+        el = A("ES", 15, NP, 16)
+        scan(A("ES"), A("SEG"), A("EG"), 0.0, op.mult, op.add)
+        if not jub:
+            en = A("EN", 16 * t, 16 * t + 16)
+            cp(en, el)
+            send(nxt, A("RE", 16 * t + 16, 16 * t + 32), en, "aE%d" % (t + 1))
+            kpart()
+            xpart()
+
+            def hsend(t=t, hpart=hpart):
+                ho = A("HO", 16 * t, 16 * t + 16)
+                hpart(ho)
+                send(nxt, A("RH", 16 * t + 16, 16 * t + 32), ho, "aH%d" % (t + 1))
+            pend.append(hsend)
+        else:
+            hpart(A("HN"))
+            tt(A("DW"), A("HN"), el, op.subtract)
+            tt(A("DW2"), A("DW"), A("WF"), op.mult)
+            tt(A("EJ"), A("DW2"), el, op.add)
+            en = A("EN", 16 * t, 16 * t + 16)
+            cp(en, A("EJ"))
+            if not last:
+                send(nxt, A("RE", 16 * t + 16, 16 * t + 32), en, "aE%d" % (t + 1))
+            else:
+                cp(A("FO", 0, 16), A("EJ"))
+            xpart()
+            tt(A("PJ1"), IND(Xg, en), A("PN"), op.subtract)
+            ts(A("PJ2"), A("PJ1"), 0.5, op.mult, 167.25, op.add)
+            po = A("PO", NP * t, NP * t + NP)
+            if not last:
+                ts(po, A("PJ2"), -1.0, op.mult, 175.0, op.add)
+            ts(A("PJ1"), A("PJ2"), -160.0, op.add)
+            if not last:
+                send(nxt, A("RP", NP * t + NP, NP * t + 2 * NP), po, "aP%d" % (t + 1))
+                kpart()
+            for j in range(16):
+                mm(A("pL", 0, 16), A("WH", 15 - j, 143 - j), A("PJ1", j, NP, 16), j == 0, j == 15)
+            cp(A("HI"), A("pL", 0, 16))
+
+            def hnew(t=t, ho=A("FO", 16, 32) if last else A("HO", 16 * t, 16 * t + 16)):
+                ts(A("HA"), A("HI"), 4095, op.bitwise_and)
+                ts(A("HG"), A("HA"), float(V), op.is_ge, -float(V), op.mult)
+                tt(ho, A("HA"), A("HG"), op.add)
+                if t < NT - 1:
+                    send(nxt, A("RH", 16 * t + 16, 16 * t + 32), ho, "aH%d" % (t + 1))
+                else:
+                    send(nxt, A("FIN"), A("FO"), "aF")
+            if last:
+                hnew()
+            else:
+                pend.append(hnew)
+        if t == NT - 2:
+            ybase(g, T, A, mm, act, AF, range(0, 3))
+        if last:
+            outs = []
+            outs.append(("Y", dma("Y", T.yh[:, :], T.H[0:128:16, V:2 * V], [A("H", V, 2 * V)], [])))
+            outs.append(("Y", dma("Y", T.yx[:, :], T.X[:, 0:V], [A("X", 0, V)], [])))
+            cp(IND(A("YK"), A("OFS")), A("YF"))
+            outs.append(("Y", dma("Y", T.yk[:, :], T.YK[0:128:16, V:2 * V], [A("YK", V, 2 * V)], [])))
+            arrives(prv, A("FIN"), "aF")
+            for k, (x, p, y, o) in enumerate((("EXK", "pR", "YO", T.yo), ("EXB", "pR2", "YT", T.yt))):
+                tt(A(x), IND(A("FIN", 16 * k, 16 * k + 16), A("SOFF", 0, 16)), A("DIAG"), op.mult)
+                mm(A(p, 0, NP), A("BDF"), A(x), True, True)
+                if k:
+                    act(A(y), A(p, 0, NP), AF.Identity)
+                else:
+                    cp(A(y), A(p, 0, NP))
+                outs.append(("YS"[k], dma("YS"[k], o[:, :], T[y][0:128:16, :], [A(y)], [])))
+            for q, s in outs:
+                queues[q].wait_ge(T.sem[s], 16)
+            g.wait_ge(T.sem.loc, nloc[0])
+            for s, n in count.items():
+                g.wait_ge(T.sem[s], n)
+
+
+def ybase(g, T, A, mm, act, AF, blocks):
+    for k in blocks:
+        p = ("pA0", "pB0", "pB1")[k % 3]
+        a, b = V + 512 * k, V + 512 * k + 512
+        mm(A(p, 0, 512), A("YW"), A("K", a, b), True, True)
+        act(A("YK", a, b), A(p, 0, 512), AF.Identity)

@@ -1,44 +1,38 @@
-from concourse.bass import DstId, RemoteDMATransfer
-from concourse.mybir import dt, AluOpType, AxisListType, ActivationFunctionType
+from concourse.mybir import AluOpType, AxisListType, ActivationFunctionType
 
 V, NP, NT, TERM = 3584, 256, 8, 4
 W = 2 * V + NP
-CH = 64
-NCH = NP // CH
-RDF = True
-NE = 11
-BIG = float(2 ** 28)
+MID = V // 2
+NV = 9
+VG = (32, 64)
+C19 = float(3 * 2 ** 18)
+C0 = C19 + MID
 
 _S = {}
-
-
-def _sb(n, w, d):
-    _S[n] = ("sbuf", [128, w], d)
-
-
-F, B, I, U = "float32", "bfloat16", "int32", "uint16"
+F, B, I, U, Hf = "float32", "bfloat16", "int32", "uint16", "float16"
 for _n, _w, _d in [
-        ("K", W, F), ("KI", V, I), ("X", W, B), ("H", W, F), ("YK", W, F),
+        ("K", W, F), ("KI", V, I), ("X", W, B), ("H", W, F), ("YK", W, F), ("IOTA", W, F),
         ("OWN", 16, I), ("WL", 16, I), ("WR", 16, I), ("HI0", 16, I), ("WTI", 1, I),
-        ("RE", 16 * NT, U), ("RP", NP * NT, B), ("RH", 16 * NT, F), ("FIN", 32, F),
-        ("EN", 16 * NT, U), ("PO", NP * NT, B), ("HO", 16 * NT, F), ("FO", 32, F),
-        ("CU", NP, U), ("KC0", NP, F), ("PR", 16 * NP, B), ("D", 16 * NP, B), ("AB", 16 * NP, B), ("GE", 16 * NP, B),
-        ("KB", NP, F), ("KEY", NP, F), ("T1", NP, F), ("SC", NP, F),
-        ("MI", 16, I), ("BI", 16, I), ("FB", 16, F), ("KT", 16, F), ("KL", 16, F), ("EV", 16, F),
-        ("KLT", 16, F), ("OF1", 16, F), ("OF2", 16, F), ("OFS", 16, U),
-        ("BU", 16, U), ("EXK", NP, F), ("EXB", NP, F), ("KR", NP, U), ("E", 16 * NP, B), ("FD", NP, B), ("FS", NP, F),
+        ("RE", 16 * NT, U), ("RP", NP * NT, B), ("RH", 16 * NT, F), ("FIN", 32, U),
+        ("EN", 16 * NT, U), ("PO", NP * NT, B), ("HO", 16 * NT, F), ("FO", 32, U),
+        ("CU", NP, U), ("KC", NP, Hf), ("G", 16 * NP, B), ("M", 16 * NP, Hf),
+        ("R1", NP, F), ("UU", NP, F), ("KEY", NP, F), ("SC", NP, F), ("EXP", NP, F),
+        ("RB", 16, B), ("R4", 16, F), ("BP", 16, F), ("KT", 16, F), ("KL", 16, F), ("KF", 16, F), ("EV", 16, F),
+        ("KU", 16, U), ("BU", 16, U), ("OF2", 16, F), ("OFS", 16, U),
+        ("KR", NP, U), ("KRF", NP, F), ("E", 16 * NP, B), ("ED", NP, B), ("FS", NP, F), ("EA", NP * 3, F),
         ("BR", NP, F), ("EG", NP, F), ("ES", NP, F), ("T4", NP, B), ("XG", NP, B), ("XV", NP, B),
-        ("SKF", NP, F), ("SCE", NP, F), ("THO", NP, F), ("RD", NP, B), ("PN", NP, B), ("EA", NP * 2, F),
+        ("SKF", NP, F), ("SCE", NP, F), ("SG", NP, B), ("PN", NP, B),
         ("RL", 16, F), ("BH", 16, F), ("BH2", 16, F), ("HN", 16, F), ("DW", 16, F), ("DW2", 16, F), ("EJ", 16, F), ("WF", 16, F),
         ("PJ1", NP, B), ("PJ2", NP, B), ("HI", 16, I), ("HA", 16, I), ("HG", 16, F), ("YF", NP, F), ("YO", NP, F), ("YT", NP, F),
-        ("IP", 1, I), ("ICF", NP, F), ("CMF", NP, F), ("CGF", 128, F), ("TRB", 16, F),
-        ("PMI", 1, I), ("PAI", 1, I), ("ODI", 1, I), ("COL", 16, F),
-        ("IDF", 128, F), ("BDF", 128, F), ("YW", 128, F), ("LUS", 512, F), ("WS", 144, F), ("WA", 144, B), ("WB", 144, B), ("WH", 144, B),
-        ("BD17", 128, B), ("W1", 128, B), ("IDB", 128, B), ("NIDB", 128, B), ("DIAG", NP, F), ("RS", NP, F), ("SEG", NP, F),
-        ("PWD", 16, F), ("TH", NP, B), ("THD", NP, F), ("TR", 16, F), ("SOFF", NP, U)]:
-    _sb(_n, _w, _d)
-COLS = ["PF", "PM", "PG", "PG15", "PAR", "PA1", "ODD", "EVN", "KCOL", "KEV", "K1", "POW", "WTF", "PFM", "PFP", "POH"]
-for _n in ["pA0", "pB0", "pA1", "pB1", "pL", "pR", "pR2", "pD"]:
+        ("IP", 1, I), ("ICF", NP, F), ("CMF", NP, F), ("CGF", 128, F), ("TMP", NP, F), ("TMQ", NP, F),
+        ("PMI", 1, I), ("ODI", 1, I), ("COL", 16, F),
+        ("BDF", 128, F), ("YW", 128, F), ("WS", 144, F), ("WH", 144, B), ("A8", 8, F), ("BG8", 8, B), ("BM8", 8, Hf),
+        ("IDB", 128, B), ("NIDB", 128, B), ("ID4", 128, B), ("IDHF", 128, B), ("IDH", 128, Hf), ("EVD", 128, Hf),
+        ("BDQ", 128, B), ("BDB", 128, B), ("LOW", 128, B), ("CY", 128, B), ("CK", 128, B), ("C16", 512, B), ("MASK", NP, B),
+        ("DIAG", NP, F), ("RS", 128, F), ("SEG", NP, F), ("TRM", NP, F), ("SOFF", 16, U), ("LOFF", 8, U)]:
+    _S[_n] = ("sbuf", [128, _w], _d)
+COLS = ["PF", "PM", "PG", "PG15", "ODD", "EVN", "EVM", "K1", "WTF", "PMW"]
+for _n in ["pP", "pY0", "pY1", "pK", "pL", "pD", "pX", "pQ"]:
     _S[_n] = ("psum", [128, 512], F)
 SCRATCH = _S
 NDMA = 24
@@ -90,11 +84,11 @@ def rank_program(g, core, T, topo):
         for lst, wr in ((reads, False), (writes, True)):
             for r in lst:
                 for e in log.get(r[0], []):
+                    meet = e[0] < r[2] and r[1] < e[1] and (wr or e[2])
                     if psum(r[0]):
-                        if e[3] == q and (q == "T" or not (wr or e[2])):
-                            continue
-                        ev.append(e[4])
-                    elif e[0] < r[2] and r[1] < e[1] and (wr or e[2]):
+                        if e[3] != q or (q != "T" and meet):
+                            ev.append(e[4])
+                    elif meet:
                         ev.append(e[4])
         ev.sort(key=lambda e: -e[0])
         for e in ev:
@@ -107,14 +101,17 @@ def rank_program(g, core, T, topo):
     def note(q, reads, writes, event):
         for r in writes:
             l = log.setdefault(r[0], [])
-            if r[3] == 1 or psum(r[0]):
-                lo, hi = (0, 1 << 20) if psum(r[0]) and q != "T" else (r[1], r[2])
-                l[:] = [e for e in l if not (lo <= e[0] and e[1] <= hi)]
+            if r[3] == 1:
+                l[:] = [e for e in l if not (r[1] <= e[0] and e[1] <= r[2])]
             l.append((r[1], r[2], True, q, event))
         for r in reads:
             l = log.setdefault(r[0], [])
             l[:] = [e for e in l if not (not e[2] and e[3] == q and r[1] <= e[0] and e[1] <= r[2])]
             l.append((r[1], r[2], False, q, event))
+        for r in reads + writes:
+            l = log[r[0]]
+            if len(l) > 64:
+                l[:] = [e for e in l if not all(known[k].get(e[4][1], 0) >= e[4][2] for k in "VST")] if psum(r[0]) else l
 
     def event(q, sem, val):
         order[0] += 1
@@ -151,9 +148,6 @@ def rank_program(g, core, T, topo):
 
     def scan(out, d0, d1, init, o0, o1):
         emit("V", [d0, d1], [out], lambda: g.vector.tensor_tensor_scan(ap(out), ap(d0), ap(d1), init, o0, o1))
-
-    def vtr(out, a):
-        emit("V", [a], [out], lambda: g.vector.transpose(ap(out), ap(a)))
 
     def fill(out, c):
         emit("V", [], [out], lambda: g.vector.memset(ap(out), c))
@@ -200,67 +194,75 @@ def rank_program(g, core, T, topo):
 
     iota(A("IP"), [[1, 1]], 0, 1)
     iota(A("PF"), [[1, 1]], 0, 1)
-    iota(A("CMF"), [[0, 16], [1, 16]])
     iota(A("ICF"), [[1, NP]])
+    iota(A("CMF"), [[0, 16], [1, 16]])
     iota(A("CGF"), [[16, 8], [0, 16]])
-    iota(A("TRB"), [[16, 16]], 2 * V)
     send(prv, A("WR"), A("WL"), "aW")
     arrives(nxt, A("WR"), "aW")
     iota(A("H", V, 2 * V), [[1, V]])
+    act(A("IOTA", 0, NP), A("ICF"), AF.Identity)
+    n = NP
+    while n < W:
+        m = min(n, W - n)
+        act(A("IOTA", n, n + m), A("IOTA", 0, m), AF.Identity, bias=float(n))
+        n += m
+    fill(A("C16"), 1.0 / 16)
+    fill(A("CY"), -8.5 * 2048)
     ts(A("PMI"), A("IP"), 15, op.bitwise_and)
-    ts(A("PAI"), A("IP"), 4, op.arith_shift_right, 1, op.bitwise_and)
     ts(A("ODI"), A("IP"), 1, op.bitwise_and)
     cp(A("PM"), A("PMI"))
-    cp(A("PAR"), A("PAI"))
     cp(A("ODD"), A("ODI"))
     tt(A("PG"), A("PF"), A("PM"), op.subtract)
     ts(A("PG15"), A("PG"), 15.0, op.add)
-    ts(A("KCOL"), A("PM"), 4096.0, op.mult)
-    ts(A("DIAG"), A("CMF"), A("PM"), op.is_equal)
-    ts(A("RS"), A("CMF"), 0.0, op.is_equal, float(2 ** 25), op.mult)
-    ts(A("SEG"), A("CMF"), 0.0, op.not_equal)
-    cp(A("SOFF"), A("ICF"))
-    ts(A("WS"), A("ICF", 0, 144), A("PG15"), op.is_equal)
-    act(A("WA"), A("WS"), AF.Identity, scale=65536.0)
-    act(A("WB"), A("WS"), AF.Identity, scale=-BIG)
+    ts(A("EVN"), A("ODD"), -1.0, op.mult, 1.0, op.add)
+    ts(A("PMW"), A("PM"), float(2 * V), op.add)
+    ts(A("K1"), A("PM"), 1.0, op.add)
+    ts(A("EVM"), A("EVN"), float(MID), op.mult)
+    cp(A("SOFF"), A("ICF", 0, 16))
+    ts(A("LOFF"), A("ICF", 0, 8), 16.0, op.mult, 15.0, op.add)
     ts(A("RP", 0, NP), A("PN"), -1.0, op.mult, 15.0, op.add)
     cp(A("RE", 0, 16), A("OWN"))
-    ts(A("IDF"), A("ICF", 0, 128), A("PF"), op.is_equal)
-    act(A("IDB"), A("IDF"), AF.Identity)
-    act(A("NIDB"), A("IDF"), AF.Identity, scale=-1.0)
+    idn = A("ICF", 0, 128)
+    ts(A("IDB"), idn, A("PF"), op.is_equal)
+    ts(A("IDH"), idn, A("PF"), op.is_equal)
+    ts(A("ID4"), idn, A("PF"), op.is_equal, 4.0, op.mult)
+    ts(A("NIDB"), idn, A("PF"), op.is_equal, -1.0, op.mult)
+    ts(A("IDHF"), idn, A("PF"), op.is_equal, 0.5, op.mult)
+    ts(A("EVD"), idn, A("PF"), op.is_equal, A("EVN"), op.mult)
     ts(A("BDF"), A("CGF"), A("PG"), op.is_equal)
-    act(A("BD17"), A("BDF"), AF.Identity, scale=-float(2 ** 17))
-    ts(A("PA1"), A("PAR"), -1.0, op.mult, 1.0, op.add)
-    ts(A("PFM"), A("PF"), -16.0, op.add)
-    ts(A("PFP"), A("PF"), 16.0, op.add)
-    for u in range(2):
-        for s in range(2):
-            j = 2 * u + s
-            ts(A("LUS", 128 * j, 128 * j + 128), A("ICF", 0, 128), A(("PFM", "PF", "PFP")[s - u + 1]), op.is_equal, A("PAR" if u else "PA1"), op.mult)
-    ts(A("KB"), A("CMF"), 0.0, op.is_equal, 65536.0, op.mult)
-    ts(A("KEY"), A("SEG"), 0.5, op.mult)
-    scan(A("TH"), A("KEY"), A("KB"), 0.0, op.mult, op.add)
-    act(A("THD"), A("DIAG"), AF.Identity, bias=float(2 ** 17), scale=-float(2 ** 17))
-    tt(A("PWD"), A("TH", 0, 16), A("DIAG", 0, 16), op.mult)
-    emit("V", [A("PWD")], [A("POW")], lambda: g.vector.tensor_reduce(ap(A("POW")), T.PWD[:, :], AxisListType.X, op.add))
-    ts(A("POH"), A("POW"), -0.5, op.mult)
-    act(A("W1"), A("BDF"), AF.Identity, scale=A("POH"))
-    ts(A("TR"), A("TRB"), A("PM"), op.add)
-    ts(A("EVN"), A("ODD"), -1.0, op.mult, 1.0, op.add)
-    ts(A("KEV"), A("KCOL"), -1.0, op.mult, A("EVN"), op.mult)
-    ts(A("K1"), A("PM"), 1.0, op.add)
-    act(A("YW"), A("BDF"), AF.Identity, scale=A("K1"))
+    ts(A("BDQ"), A("CGF"), A("PG"), op.is_equal, 65536.0, op.mult)
+    ts(A("BDB"), A("CGF"), A("PG"), op.is_equal, 8192.0, op.mult)
+    cg8 = A("CGF", 0, 128, 16)
+    ts(A("A8"), cg8, A("PG"), op.is_equal)
+    ts(A("BG8"), cg8, A("PG"), op.is_equal, 16384.0, op.mult)
+    ts(A("BM8"), cg8, A("PG"), op.is_equal, -32768.0, op.mult)
+    ts(A("CK"), A("CMF", 0, 128), 4096.0, op.mult)
+    ts(A("DIAG"), A("CMF"), A("PM"), op.is_equal)
+    ts(A("MASK"), A("CMF"), A("PM"), op.not_equal, 8192.0, op.mult)
+    ts(A("RS"), A("CMF", 0, 128), 0.0, op.is_equal, float(2 ** 25), op.mult)
+    ts(A("SEG"), A("CMF"), 0.0, op.not_equal)
+    ts(A("TMP", 0, 128), A("CMF", 0, 128), A("PM"), op.is_gt, 8192.0, op.mult)
+    tt(A("LOW"), A("TMP", 0, 128), A("BDF"), op.mult)
+    ts(A("TMQ"), A("ICF"), A("PMW"), op.add)
+    ts(A("TMP"), A("CMF"), 0.0, op.is_equal)
+    tt(A("TRM"), A("TMP"), A("TMQ"), op.mult)
+    ts(A("WS"), A("ICF", 0, 144), A("PG15"), op.is_equal)
+    ts(A("YW"), A("BDF"), A("K1"), op.mult)
     cp(A("WTF"), A("WTI"))
-    act(A("WH"), A("WS"), AF.Identity, scale=A("WTF"))
+    ts(A("WH"), A("WS"), A("WTF"), op.mult)
     cp(A("RH", 0, 16), A("HI0"))
     for k in range(4):
         a, b = 896 * k, 896 * k + 896
         cp(A("K", V + a, V + b), A("KI", a, b))
+
+    def ybase(blocks):
+        for k in blocks:
+            p = ("pX", "pQ")[k % 2]
+            a, b = V + 512 * k, V + 512 * k + 512
+            mm(A(p, 0, 512), A("YW"), A("K", a, b), True, True)
+            act(A("YK", a, b), A(p, 0, 512), AF.Identity)
+
     pend = []
-
-    def pa(c):
-        return ("pA0", "pB0") if c < NCH - 1 else ("pA1", "pB1")
-
     for t in range(NT):
         e = A("RE", 16 * t, 16 * t + 16)
         price = A("RP", NP * t, NP * t + NP)
@@ -273,139 +275,128 @@ def rank_program(g, core, T, topo):
             arrives(prv, hold, "aH%d" % t)
         Kg, Xg = A("K", V, 2 * V), A("X", 0, V)
 
-        def rep(c):
-            act(A("PR", 1024 * c, 1024 * c + 1024), IND(price, A("SOFF", CH * c, CH * c + CH)), AF.Identity)
+        def kin(a, b):
+            cp(A("CU", a, b), IND(Kg, A("RE", 16 * t + a // 16, 16 * t + b // 16)))
 
-        def part(n, c):
-            w = 1024 if c < NCH - 1 else 512
-            return A(n, int(1024 * c), int(1024 * c) + w)
+        def wealth(a, b):
+            x, src = A("G", 16 * a, 16 * b), IND(Xg, A("CU", a, b))
+            if VG[0] <= a < VG[1]:
+                ts(x, src, -4.0, op.mult, 60.0, op.add)
+            else:
+                act(x, src, AF.Identity, bias=60.0, scale=-4.0)
 
-        def dif(c):
-            x = part("D", c)
-            tt(x, IND(Xg, A("CU", x[1] // 16, x[2] // 16)), part("PR", c), op.add)
-
-        def cmp(c):
-            ts(part("GE", c), part("D", c), 15.0, op.is_ge, -0.53125, op.add)
-
-        def absd(c):
-            act(part("AB", c), part("D", c), AF.Abs, bias=-15.0)
-
-        def sums(c):
-            a, b = pa(c)
-            lo, hi = CH * c, CH * c + CH
-            if c == 0:
-                mm(A("pA0", 0, NP - CH), A("IDF"), A("KC0", 0, NP - CH), True, False)
-                mm(A("pA1", NP - CH, NP), A("IDF"), A("KC0", NP - CH, NP), True, False)
+        def gsum(h):
             for k in range(16):
-                mm(A(b, lo, hi), A("WB", 15 - k, 143 - k), A("GE", 1024 * c + k, 1024 * c + 1024, 16), k == 0, k == 15)
-            for k in range(16):
-                mm(A(a, lo, hi), A("WA", 15 - k, 143 - k), A("AB", 1024 * c + k, 1024 * c + 1024, 16), False, k == 15 and c >= NCH - 2)
+                mm(A("pY%d" % h, k, 128, 16), A("G", 2048 * h + k, 2048 * h + 2048, 16), A("BG8"), False, False)
 
-        def best(c0, c1):
-            lo, hi = CH * c0, CH * c1
-            a, b = pa(c0)
-            tt(A("KB", lo, hi), A(b, lo, hi), A("KC0", lo, hi), op.max)
-            tt(A("KEY", lo, hi), A(a, lo, hi), A("KB", lo, hi), op.min)
-            vtr(A("T1", lo, hi), A("KEY", lo, hi))
-            scan(A("SC", lo, hi), A("RS", lo, hi), A("T1", lo, hi), float(2 ** 25), op.add, op.min)
+        def least(a, b):
+            h = a // 128
+            for s in range(8):
+                o = 2048 * h + 256 * s
+                tt(A("M", o + 2 * (a % 128), o + 2 * (a % 128) + 2 * (b - a)), A("G", 16 * a + s, 16 * b, 8), A("pP", 2 * a, 2 * b), op.min)
+                if b % 128 == 0:
+                    for u in range(2):
+                        mm(A("pY%d" % h, s + 8 * u, 128, 16), A("M", o + u, o + 256, 2), A("BM8"), False, s == 7 and u == 1)
 
-        rep(0)
-        rep(1)
-        cp(A("CU"), IND(Kg, e))
-        dif(0)
-        ts(A("KC0"), A("CU"), A("KCOL"), op.add)
-        cmp(0)
-        absd(0)
-        rep(2)
-        sums(0)
-        dif(1)
-        cmp(1)
-        absd(1)
-        rep(3)
-        sums(1)
-        dif(2)
-        cmp(2)
-        absd(2)
-        sums(2)
-        dif(3)
-        absd(3)
-        dif(3.5)
-        cmp(3)
-        absd(3.5)
-        cmp(3.5)
-        sums(3)
-        best(0, NCH - 1)
-        best(NCH - 1, NCH)
-        ts(A("EV"), e, float(V), op.add)
+        def best(h):
+            y, lo, hi = "pY%d" % h, 128 * h, 128 * h + 128
+            big = 1.5 * 2.0 ** 39
+            ts(A("R1", lo, hi), A(y, 0, 128), big, op.add, -big, op.add)
+            tt(A(y, 128, 256), A(y, 0, 128), A("R1", lo, hi), op.is_gt)
+            tt(A("UU", lo, hi), A(y, 128, 256), A("R1", lo, hi), op.mult)
+            tt(A("KEY", lo, hi), A("pK", lo, hi), A("UU", lo, hi), op.add)
+            scan(A("SC", lo, hi), A("RS"), A("KEY", lo, hi), float(2 ** 25), op.add, op.min)
+            tt(A("EXP", lo, hi), IND(A("SC", lo, hi), A("LOFF")), A("DIAG", 0, 128), op.mult)
+            mm(A("pL", 8 * h, 8 * h + 8), A("EXP", lo, hi), A("A8"), True, True)
+
+        mm(A("pP"), A("IDB"), A("C16"), True, False)
+        for h in range(2):
+            mm(A("pY%d" % h, 0, 128), A("IDB"), A("CY"), True, False)
+        for u in range(2):
+            mm(A("pP", u, 512, 2), A("ID4"), price, False, u == 1)
+        for h in range(2):
+            mm(A("pY%d" % h, 0, 128), A("RP", NP * t + 128 * h, NP * t + 128 * h + 128), A("BDQ"), False, False)
+        kin(0, 64)
+        wealth(0, 32)
+        kin(64, NP)
+        wealth(32, 64)
+        wealth(64, 128)
+        ts(A("KC"), A("CU"), -float(MID), op.add)
+        for h in range(2):
+            mm(A("pK", 128 * h, 128 * h + 128), A("IDB"), A("CK"), True, False)
+            mm(A("pK", 128 * h, 128 * h + 128), A("KC", 128 * h, 128 * h + 128), A("IDH"), False, True)
+        mm(A("pL", 256, 512), A("EVD"), A("KC"), True, True)
+        least(0, 64)
+        wealth(128, 192)
+        gsum(0)
+        least(64, 128)
+        wealth(192, NP)
+        best(0)
+        least(128, 192)
+        act(A("SCE"), A("pL", 256, 512), AF.Identity, bias=A("EVM"))
+        act(A("T4"), price, AF.Identity, bias=163.375, scale=-0.25)
+        gsum(1)
+        least(192, NP)
+        if last:
+            ybase(range(0, 2))
+        mm(A("pD", 0, NP), A("IDB"), A("MASK"), True, False)
+        best(1)
+        ts(A("EV"), e, V - C0, op.add)
         if t == 0:
             cp(A("WF"), A("WR"))
         while pend:
             pend.pop(0)()
-        act(A("T4"), price, AF.Identity, bias=163.375, scale=-0.25)
-        act(A("SCE"), A("KC0"), AF.Identity, bias=A("KEV"), scale=A("EVN"))
-        for u in range(2):
-            for s in range(2):
-                j = 2 * u + s
-                mm(A("pL", u, 16, 2), A("LUS", 128 * j, 128 * j + 128), A("SC", 15 + 16 * s, NP, 32), s == 0, s == 1)
-        mm(A("pD", 0, NP), A("IDB"), A("TH"), True, False)
-        cp(A("MI"), A("pL", 0, 16))
-        ts(A("FB"), A("pL", 0, 16), 65536.0, op.is_ge, 8192.0, op.mult)
-        ts(A("BI"), A("MI"), 4095, op.bitwise_and)
-        tt(A("KT"), A("BI"), A("FB"), op.add)
+        key = A("pL", 0, 16)
+        big = 1.5 * 2.0 ** 35
+        ts(A("RB"), key, 131072.0, op.min, C19, op.add)
+        ts(A("R4"), key, big, op.add, -big, op.add)
+        tt(A("KT"), key, A("RB"), op.subtract)
+        tt(A("BP"), key, A("R4"), op.subtract)
         tt(A("KL"), A("KT"), A("EV"), op.min)
-        tt(A("EXK"), IND(A("KL"), A("SOFF", 0, 16)), A("DIAG"), op.mult)
-        mm(A("pR", 0, NP), A("BDF"), A("EXK"), True, True)
-        cp(A("BU"), A("BI"))
-        tt(A("KLT"), A("KL"), A("TR"), op.subtract)
-        act(A("XG"), IND(Xg, A("BU")), AF.Identity)
-        cp(A("KR"), A("pR", 0, NP))
+        ts(A("BU"), A("BP"), float(MID), op.add)
+        ts(A("KU"), A("KL"), C0, op.add)
+        act(A("KRF"), IND(A("IOTA"), A("KU")), AF.Identity, bias=-C0)
+        cp(A("KR"), IND(A("IOTA"), A("KU")))
         ea = 0
-        for j in range(NE, 16):
-            w = NP - 16 * j
-            act(A("EA", ea, ea + w), A("pR", 16 * j, NP), AF.Abs, bias=A("KL", j, j + 1), scale=-1.0)
-            ea += w
-        act(A("E", NP * NE, NP * NE + ea), A("EA", 0, ea), AF.Relu, bias=1.0, scale=-1.0)
-        act(A("THO"), A("pR", 0, NP), AF.Relu, bias=-float(2 ** 17 * (V - 1)), scale=float(2 ** 17))
-        ea = NP * NE
-        for j in range(16):
-            lo = 16 * j
-            if j < NE:
+        for j in range(NV, 15):
+            lo = 16 * j + 16
+            act(A("EA", ea, ea + NP - lo), A("KRF", lo, NP), AF.Abs, bias=A("KL", j, j + 1), scale=-1.0)
+            ea += NP - lo
+        act(A("E", NP * NV, NP * NV + ea), A("EA", 0, ea), AF.Relu, bias=1.0, scale=-1.0)
+        act(A("BR"), IND(A("IOTA"), A("BU")), AF.Identity)
+        act(A("XG"), IND(Xg, A("BU")), AF.Identity)
+        tt(A("ED"), IND(A("KL"), A("SOFF")), A("KRF"), op.is_equal)
+        mm(A("pD", 0, NP), A("LOW"), A("ED"), False, False)
+        ea = NP * NV
+        for j in range(15):
+            lo = 16 * j + 16
+            if j < NV:
                 x = A("E", NP * j + lo, NP * j + NP)
-                ts(x, A("KR", lo, NP), A("KL", j, j + 1), op.is_equal)
+                ts(x, A("KR", lo, NP), -C0, op.add, A("KL", j, j + 1), op.is_equal)
             else:
                 x = A("E", ea, ea + NP - lo)
                 ea += NP - lo
-            mm(A("pD", lo, lo + 16), A("W1"), A("E", x[1], x[1] + 16), False, j == 15)
-            if j < 15:
-                mm(A("pD", lo + 16, NP), A("BD17"), A("E", x[1] + 16, x[2]), False, False)
-        tt(A("EXB"), IND(A("BI"), A("SOFF", 0, 16)), A("DIAG"), op.mult)
-        mm(A("pR2", 0, NP), A("BDF"), A("EXB"), True, True)
-        act(A("BR"), A("pR2", 0, NP), AF.Identity)
-        mm(A("pB1", 0, NP), A("IDB"), A("XG"), True, False)
-        mm(A("pB1", 0, NP), A("NIDB"), A("T4"), False, True)
-        tt(A("FD"), A("pD", 0, NP), A("THD"), op.is_gt)
-        if RDF:
-            tt(A("RD"), A("pD", 0, NP), A("THO"), op.is_gt)
-        scan(A("FS"), A("SEG"), A("FD"), 0.0, op.mult, op.add)
-        fl = A("FS", 15, NP, 16)
-        tt(A("OF1"), fl, A("KLT"), op.mult)
-        if not RDF:
-            tt(A("RD"), A("pD", 0, NP), A("THO"), op.is_gt)
-        tt(A("OF2"), A("OF1"), A("TR"), op.add)
+            mm(A("pD", lo, NP), A("BDB"), x, False, j == 14)
+        ts(A("KF"), A("KL"), C0, op.add)
+        mm(A("pX", 0, NP), A("IDB"), A("XG"), True, False)
+        mm(A("pX", 0, NP), A("NIDB"), A("T4"), False, True)
+        mm(A("pQ", 0, NP), A("IDB"), price, True, False)
+        act(A("SKF"), IND(Kg, A("BU")), AF.Identity, scale=A("ODD"))
+        scan(A("FS"), A("TRM"), A("pD", 0, NP), 0.0, op.max, op.min)
+        tt(A("OF2"), A("FS", 15, NP, 16), A("KF"), op.max)
         cp(A("OFS"), A("OF2"))
         pn = A("PN") if jub else A("PO", NP * t, NP * t + NP)
-        mm(A("pA1", 0, NP), A("IDB"), price, True, False)
-        mm(A("pA1", 0, NP), A("NIDB"), A("RD"), False, True)
-        act(pn, A("pA1", 0, NP), AF.Relu)
+        act(A("SG"), IND(A("IOTA"), A("OFS")), AF.Sign, bias=0.5 - V)
+        mm(A("pQ", 0, NP), A("IDHF"), A("SG"), False, True)
+        act(pn, A("pQ", 0, NP), AF.Relu, bias=-0.5)
         if not jub:
             send(nxt, A("RP", NP * t + NP, NP * t + 2 * NP), pn, "aP%d" % (t + 1))
-        act(A("SKF"), IND(Kg, A("BU")), AF.Identity, scale=A("ODD"))
-        act(A("XV"), A("pB1", 0, NP), AF.Relu, bias=160.0)
+        act(A("XV"), A("pX", 0, NP), AF.Relu, bias=160.0)
         if last:
-            ybase(g, T, A, mm, act, AF, range(3, 7))
-            mm(A("pA1", 0, NP), A("YW"), A("SKF"), True, False)
-            mm(A("pA1", 0, NP), A("YW"), A("SCE"), False, True)
-            act(A("YF"), A("pA1", 0, NP), AF.Identity)
+            mm(A("pK", 0, NP), A("YW"), A("SKF"), True, False)
+            mm(A("pK", 0, NP), A("YW"), A("SCE"), False, True)
+            ybase(range(2, 7))
+            act(A("YF"), A("pK", 0, NP), AF.Identity)
         cp(IND(A("H"), A("OFS")), A("BR"))
         tt(A("EG"), IND(A("H", V, 2 * V), e), A("DIAG"), op.mult)
 
@@ -460,20 +451,20 @@ def rank_program(g, core, T, topo):
                 mm(A("pL", 0, 16), A("WH", 15 - j, 143 - j), A("PJ1", j, NP, 16), j == 0, j == 15)
             cp(A("HI"), A("pL", 0, 16))
 
-            def hnew(t=t, ho=A("FO", 16, 32) if last else A("HO", 16 * t, 16 * t + 16)):
+            def hnew(t=t):
+                ho = A("HO", 16 * t, 16 * t + 16)
                 ts(A("HA"), A("HI"), 4095, op.bitwise_and)
                 ts(A("HG"), A("HA"), float(V), op.is_ge, -float(V), op.mult)
                 tt(ho, A("HA"), A("HG"), op.add)
                 if t < NT - 1:
                     send(nxt, A("RH", 16 * t + 16, 16 * t + 32), ho, "aH%d" % (t + 1))
                 else:
+                    cp(A("FO", 16, 32), ho)
                     send(nxt, A("FIN"), A("FO"), "aF")
             if last:
                 hnew()
             else:
                 pend.append(hnew)
-        if t == NT - 2:
-            ybase(g, T, A, mm, act, AF, range(0, 3))
         if last:
             outs = []
             outs.append(("Y", dma("Y", T.yh[:, :], T.H[0:128:16, V:2 * V], [A("H", V, 2 * V)], [])))
@@ -481,24 +472,12 @@ def rank_program(g, core, T, topo):
             cp(IND(A("YK"), A("OFS")), A("YF"))
             outs.append(("Y", dma("Y", T.yk[:, :], T.YK[0:128:16, V:2 * V], [A("YK", V, 2 * V)], [])))
             arrives(prv, A("FIN"), "aF")
-            for k, (x, p, y, o) in enumerate((("EXK", "pR", "YO", T.yo), ("EXB", "pR2", "YT", T.yt))):
-                tt(A(x), IND(A("FIN", 16 * k, 16 * k + 16), A("SOFF", 0, 16)), A("DIAG"), op.mult)
-                mm(A(p, 0, NP), A("BDF"), A(x), True, True)
-                if k:
-                    act(A(y), A(p, 0, NP), AF.Identity)
-                else:
-                    cp(A(y), A(p, 0, NP))
+            cp(A("YO"), IND(A("IOTA"), A("FIN", 0, 16)))
+            act(A("YT"), IND(A("IOTA"), A("FIN", 16, 32)), AF.Identity)
+            for k, (y, o) in enumerate((("YO", T.yo), ("YT", T.yt))):
                 outs.append(("YS"[k], dma("YS"[k], o[:, :], T[y][0:128:16, :], [A(y)], [])))
             for q, s in outs:
                 queues[q].wait_ge(T.sem[s], 16)
             g.wait_ge(T.sem.loc, nloc[0])
             for s, n in count.items():
                 g.wait_ge(T.sem[s], n)
-
-
-def ybase(g, T, A, mm, act, AF, blocks):
-    for k in blocks:
-        p = ("pA0", "pB0", "pB1")[k % 3]
-        a, b = V + 512 * k, V + 512 * k + 512
-        mm(A(p, 0, 512), A("YW"), A("K", a, b), True, True)
-        act(A("YK", a, b), A(p, 0, 512), AF.Identity)

@@ -4,7 +4,8 @@ V, NP, NT, TERM = 3584, 256, 8, 4
 W = 2 * V + NP
 MID = V // 2
 NV = 9
-VG = (32, 64)
+LAST = 224
+VG = (16, 64)
 C19 = float(3 * 2 ** 18)
 C0 = C19 + MID
 
@@ -16,11 +17,12 @@ for _n, _w, _d in [
         ("RE", 16 * NT, U), ("RP", NP * NT, B), ("RH", 16 * NT, F), ("FIN", 32, U),
         ("EN", 16 * NT, U), ("PO", NP * NT, B), ("HO", 16 * NT, F), ("FO", 32, U),
         ("CU", NP, U), ("KC", NP, Hf), ("G", 16 * NP, B), ("M", 16 * NP, Hf),
-        ("R1", NP, F), ("UU", NP, F), ("KEY", NP, F), ("SC", NP, F), ("EXP", NP, F),
+        ("R0", 128, F), ("R1", NP, F), ("R2", NP, B), ("U0", 128, B), ("UU", NP, F), ("KEY", 128, F),
+        ("IDM", 128, B), ("IDP", 128, B), ("OFD", NP, F), ("RSH", NP, Hf), ("WA", 16, F), ("WB", 16, F), ("SC", NP, F), ("EXP", NP, F),
         ("RB", 16, B), ("R4", 16, F), ("BP", 16, F), ("KT", 16, F), ("KL", 16, F), ("KF", 16, F), ("EV", 16, F),
         ("KU", 16, U), ("BU", 16, U), ("OF2", 16, F), ("OFS", 16, U),
         ("KR", NP, U), ("KRF", NP, F), ("E", 16 * NP, B), ("ED", NP, B), ("FS", NP, F), ("EA", NP * 3, F),
-        ("BR", NP, F), ("EG", NP, F), ("ES", NP, F), ("T4", NP, B), ("XG", NP, B), ("XV", NP, B),
+        ("BR", NP, F), ("EG", NP, Hf), ("ES", NP, Hf), ("T4", NP, B), ("XG", NP, B), ("XV", NP, B),
         ("SKF", NP, F), ("SCE", NP, F), ("SG", NP, B), ("PN", NP, B),
         ("RL", 16, F), ("BH", 16, F), ("BH2", 16, F), ("HN", 16, F), ("DW", 16, F), ("DW2", 16, F), ("EJ", 16, F), ("WF", 16, F),
         ("PJ1", NP, B), ("PJ2", NP, B), ("HI", 16, I), ("HA", 16, I), ("HG", 16, F), ("YF", NP, F), ("YO", NP, F), ("YT", NP, F),
@@ -68,8 +70,9 @@ def rank_program(g, core, T, topo):
             return x
         if x[0] == "ind":
             return ap(x[1]).indirect(ap(x[2]))
-        n, a, b, s = x
-        return T[n][:, a:b] if s == 1 else T[n][:, a:b:s]
+        n, a, b, s = x[:4]
+        p = slice(*x[4]) if len(x) > 4 else slice(None)
+        return T[n][p, a:b] if s == 1 else T[n][p, a:b:s]
 
     def regs(x):
         if not isinstance(x, tuple):
@@ -240,7 +243,10 @@ def rank_program(g, core, T, topo):
     ts(A("DIAG"), A("CMF"), A("PM"), op.is_equal)
     ts(A("MASK"), A("CMF"), A("PM"), op.not_equal, 8192.0, op.mult)
     ts(A("RS"), A("CMF", 0, 128), 0.0, op.is_equal, float(2 ** 25), op.mult)
-    ts(A("SEG"), A("CMF"), 0.0, op.not_equal)
+    ts(A("RSH"), A("CMF"), 0.0, op.is_equal, -32768.0, op.mult)
+    ts(A("OFD"), A("MASK"), float(MID), op.add)
+    ts(A("IDM"), idn, A("PF"), op.is_equal, -255.0, op.mult)
+    ts(A("IDP"), idn, A("PF"), op.is_equal, 256.0, op.mult)
     ts(A("TMP", 0, 128), A("CMF", 0, 128), A("PM"), op.is_gt, 8192.0, op.mult)
     tt(A("LOW"), A("TMP", 0, 128), A("BDF"), op.mult)
     ts(A("TMQ"), A("ICF"), A("PMW"), op.add)
@@ -255,12 +261,11 @@ def rank_program(g, core, T, topo):
         a, b = 896 * k, 896 * k + 896
         cp(A("K", V + a, V + b), A("KI", a, b))
 
-    def ybase(blocks):
-        for k in blocks:
-            p = ("pX", "pQ")[k % 2]
-            a, b = V + 512 * k, V + 512 * k + 512
-            mm(A(p, 0, 512), A("YW"), A("K", a, b), True, True)
-            act(A("YK", a, b), A(p, 0, 512), AF.Identity)
+    def ymm(k, p):
+        mm(A(p), A("YW"), A("K", V + 512 * k, V + 512 * k + 512), True, True)
+
+    def ycopy(k, p):
+        act(A("YK", V + 512 * k, V + 512 * k + 512), A(p), AF.Identity)
 
     pend = []
     for t in range(NT):
@@ -285,67 +290,105 @@ def rank_program(g, core, T, topo):
             else:
                 act(x, src, AF.Identity, bias=60.0, scale=-4.0)
 
-        def gsum(h):
-            for k in range(16):
-                mm(A("pY%d" % h, k, 128, 16), A("G", 2048 * h + k, 2048 * h + 2048, 16), A("BG8"), False, False)
+        def ysum(k, a, b):
+            return A("pY%d" % (a // 128), k, 128, 16) + ((a % 128, (b - 1) % 128 + 1),)
 
-        def least(a, b):
-            h = a // 128
+        def gsum(a, b, ks=range(16)):
+            for k in ks:
+                mm(ysum(k, a, b), A("G", 16 * a + k, 16 * b, 16), A("BG8"), False, False)
+
+        def least(a, b, a0=None):
             for s in range(8):
-                o = 2048 * h + 256 * s
+                o = 2048 * (a // 128) + 256 * s
                 tt(A("M", o + 2 * (a % 128), o + 2 * (a % 128) + 2 * (b - a)), A("G", 16 * a + s, 16 * b, 8), A("pP", 2 * a, 2 * b), op.min)
-                if b % 128 == 0:
+                if a >= 192:
+                    gsum(a, b, (s, s + 8))
+                if a0 is not None:
+                    o += 2 * (a0 % 128)
                     for u in range(2):
-                        mm(A("pY%d" % h, s + 8 * u, 128, 16), A("M", o + u, o + 256, 2), A("BM8"), False, s == 7 and u == 1)
+                        mm(ysum(s + 8 * u, a0, b), A("M", o + u, o + 2 * (b - a0), 2), A("BM8"), False, s == 7 and u == 1)
 
-        def best(h):
-            y, lo, hi = "pY%d" % h, 128 * h, 128 * h + 128
-            big = 1.5 * 2.0 ** 39
-            ts(A("R1", lo, hi), A(y, 0, 128), big, op.add, -big, op.add)
-            tt(A(y, 128, 256), A(y, 0, 128), A("R1", lo, hi), op.is_gt)
-            tt(A("UU", lo, hi), A(y, 128, 256), A("R1", lo, hi), op.mult)
-            tt(A("KEY", lo, hi), A("pK", lo, hi), A("UU", lo, hi), op.add)
-            scan(A("SC", lo, hi), A("RS"), A("KEY", lo, hi), float(2 ** 25), op.add, op.min)
+        big = 1.5 * 2.0 ** 39
+        keys = (A("pX", 256, 384), A("pK", 0, 128))
+
+        def least_key(h, key):
+            scan(A("SC", 128 * h, 128 * h + 128), A("RS"), key, float(2 ** 25), op.add, op.min)
+
+        def to_list(h):
+            lo, hi = 128 * h, 128 * h + 128
             tt(A("EXP", lo, hi), IND(A("SC", lo, hi), A("LOFF")), A("DIAG", 0, 128), op.mult)
             mm(A("pL", 8 * h, 8 * h + 8), A("EXP", lo, hi), A("A8"), True, True)
 
+        def fillers(n):
+            for _ in range(min(n, len(pend))):
+                pend.pop(0)()
+
+        pend.append(lambda e=e: ts(A("EV"), e, V - C0, op.add))
+        if t == 0:
+            pend.append(lambda: cp(A("WF"), A("WR")))
+            pend.append(lambda: ts(A("WB"), A("WF"), -1.0, op.mult, 1.0, op.add))
         mm(A("pP"), A("IDB"), A("C16"), True, False)
         for h in range(2):
             mm(A("pY%d" % h, 0, 128), A("IDB"), A("CY"), True, False)
+        for h in range(2):
+            mm(keys[h], A("IDB"), A("CK"), True, False)
         for u in range(2):
             mm(A("pP", u, 512, 2), A("ID4"), price, False, u == 1)
         for h in range(2):
             mm(A("pY%d" % h, 0, 128), A("RP", NP * t + 128 * h, NP * t + 128 * h + 128), A("BDQ"), False, False)
+        if last:
+            ymm(2, "pQ")
         kin(0, 64)
-        wealth(0, 32)
+        wealth(0, VG[0])
         kin(64, NP)
-        wealth(32, 64)
-        wealth(64, 128)
+        wealth(*VG)
+        wealth(VG[1], 128)
         ts(A("KC"), A("CU"), -float(MID), op.add)
         for h in range(2):
-            mm(A("pK", 128 * h, 128 * h + 128), A("IDB"), A("CK"), True, False)
-            mm(A("pK", 128 * h, 128 * h + 128), A("KC", 128 * h, 128 * h + 128), A("IDH"), False, True)
+            mm(keys[h], A("KC", 128 * h, 128 * h + 128), A("IDH"), False, h == 1)
         mm(A("pL", 256, 512), A("EVD"), A("KC"), True, True)
         least(0, 64)
         wealth(128, 192)
-        gsum(0)
-        least(64, 128)
-        wealth(192, NP)
-        best(0)
-        least(128, 192)
+        gsum(0, 128)
+        least(64, 128, 0)
+        wealth(192, LAST)
+        wealth(LAST, NP)
+        gsum(128, 192)
+        least(128, 192, 128)
+        act(A("R0"), A("pY0", 0, 128), AF.Identity, bias=16.5 * 2048)
+        act(A("R1", 0, 128), A("pY0", 0, 128), AF.Identity, bias=big)
+        act(A("R1", 128, 256), A("R0"), AF.Identity, bias=big)
+        act(A("R2"), A("R1"), AF.Identity, bias=-big)
         act(A("SCE"), A("pL", 256, 512), AF.Identity, bias=A("EVM"))
-        act(A("T4"), price, AF.Identity, bias=163.375, scale=-0.25)
-        gsum(1)
-        least(192, NP)
+        least(192, LAST, 192)
+        least(LAST, NP, LAST)
+        mm(A("pY0", 128, 256), A("IDM"), A("R2", 0, 128), True, False)
+        mm(A("pY0", 128, 256), A("IDP"), A("R2", 128, 256), False, True)
+        act(A("U0"), A("pY0", 128, 256), AF.Relu, bias=-float(2 ** 24))
+        mm(keys[0], A("IDB"), A("U0"), False, True)
         if last:
-            ybase(range(0, 2))
+            ymm(3, "pY0")
+        y1 = A("pY1", 0, 128)
+        fillers(1)
+        ts(A("UU", 0, 128), y1, big, op.add, -big, op.add)
+        fillers(1)
+        tt(A("pY1", 128, 256), y1, A("UU", 0, 128), op.is_gt)
+        fillers(1)
+        tt(A("UU", 128, 256), A("pY1", 128, 256), A("UU", 0, 128), op.mult)
+        fillers(1)
+        tt(A("KEY", 0, 128), keys[1], A("UU", 128, 256), op.add)
+        least_key(0, keys[0])
+        least_key(1, A("KEY", 0, 128))
+        to_list(0)
+        to_list(1)
+        act(A("T4"), price, AF.Identity, bias=163.375, scale=-0.25)
+        if last:
+            ycopy(1, "pD")
+            ycopy(2, "pQ")
+            ycopy(3, "pY0")
+            ymm(4, "pY1")
         mm(A("pD", 0, NP), A("IDB"), A("MASK"), True, False)
-        best(1)
-        ts(A("EV"), e, V - C0, op.add)
-        if t == 0:
-            cp(A("WF"), A("WR"))
-        while pend:
-            pend.pop(0)()
+        fillers(99)
         key = A("pL", 0, 16)
         big = 1.5 * 2.0 ** 35
         ts(A("RB"), key, 131072.0, op.min, C19, op.add)
@@ -365,8 +408,6 @@ def rank_program(g, core, T, topo):
         act(A("E", NP * NV, NP * NV + ea), A("EA", 0, ea), AF.Relu, bias=1.0, scale=-1.0)
         act(A("BR"), IND(A("IOTA"), A("BU")), AF.Identity)
         act(A("XG"), IND(Xg, A("BU")), AF.Identity)
-        tt(A("ED"), IND(A("KL"), A("SOFF")), A("KRF"), op.is_equal)
-        mm(A("pD", 0, NP), A("LOW"), A("ED"), False, False)
         ea = NP * NV
         for j in range(15):
             lo = 16 * j + 16
@@ -376,67 +417,78 @@ def rank_program(g, core, T, topo):
             else:
                 x = A("E", ea, ea + NP - lo)
                 ea += NP - lo
-            mm(A("pD", lo, NP), A("BDB"), x, False, j == 14)
+            mm(A("pD", lo, NP), A("BDB"), x, False, False)
+        tt(A("ED"), IND(A("KL"), A("SOFF")), A("KRF"), op.is_equal)
+        mm(A("pD", 0, NP), A("LOW"), A("ED"), False, True)
         ts(A("KF"), A("KL"), C0, op.add)
-        mm(A("pX", 0, NP), A("IDB"), A("XG"), True, False)
-        mm(A("pX", 0, NP), A("NIDB"), A("T4"), False, True)
         mm(A("pQ", 0, NP), A("IDB"), price, True, False)
-        act(A("SKF"), IND(Kg, A("BU")), AF.Identity, scale=A("ODD"))
+        mm(A("pX", 0, NP), A("NIDB"), A("T4"), True, False)
+        mm(A("pX", 0, NP), A("IDB"), A("XG"), False, True)
         scan(A("FS"), A("TRM"), A("pD", 0, NP), 0.0, op.max, op.min)
         tt(A("OF2"), A("FS", 15, NP, 16), A("KF"), op.max)
         cp(A("OFS"), A("OF2"))
         pn = A("PN") if jub else A("PO", NP * t, NP * t + NP)
         act(A("SG"), IND(A("IOTA"), A("OFS")), AF.Sign, bias=0.5 - V)
         mm(A("pQ", 0, NP), A("IDHF"), A("SG"), False, True)
+        act(A("XV"), A("pX", 0, NP), AF.Relu, bias=160.0)
         act(pn, A("pQ", 0, NP), AF.Relu, bias=-0.5)
         if not jub:
             send(nxt, A("RP", NP * t + NP, NP * t + 2 * NP), pn, "aP%d" % (t + 1))
-        act(A("XV"), A("pX", 0, NP), AF.Relu, bias=160.0)
+        act(A("SKF"), IND(Kg, A("BU")), AF.Identity, scale=A("ODD"))
         if last:
-            mm(A("pK", 0, NP), A("YW"), A("SKF"), True, False)
-            mm(A("pK", 0, NP), A("YW"), A("SCE"), False, True)
-            ybase(range(2, 7))
+            ymm(5, "pP")
+            mm(A("pK", 0, NP), A("YW"), A("SCE"), True, False)
+            mm(A("pK", 0, NP), A("YW"), A("SKF"), False, True)
+            ymm(6, "pY0")
+            ycopy(4, "pY1")
+            ycopy(5, "pP")
             act(A("YF"), A("pK", 0, NP), AF.Identity)
+            ycopy(6, "pY0")
+        ho = A("HO", 16 * t, 16 * t + 16)
+        pend.append(lambda: ts(A("RL"), A("OF2"), float(V), op.is_lt))
+        pend.append(lambda hold=hold: tt(A("BH"), A("OF2"), hold, op.subtract))
+        pend.append(lambda: tt(A("BH2"), A("RL"), A("BH"), op.mult))
+        if not jub:
+            def hsend(t=t, ho=ho, hold=hold):
+                tt(ho, A("BH2"), hold, op.add)
+                send(nxt, A("RH", 16 * t + 16, 16 * t + 32), ho, "aH%d" % (t + 1))
+            pend.append(hsend)
+        else:
+            pend.append(lambda: tt(A("HN"), A("BH2"), hold, op.add))
+            pend.append(lambda: ts(A("HG"), A("HN"), -float(MID), op.add))
+            pend.append(lambda: tt(A("WA"), A("HG"), A("WF"), op.mult))
+        nf = 2 if jub else 1
+        fillers(nf)
         cp(IND(A("H"), A("OFS")), A("BR"))
-        tt(A("EG"), IND(A("H", V, 2 * V), e), A("DIAG"), op.mult)
+        fillers(nf)
+        tt(A("EG"), IND(A("H", V, 2 * V), e), A("OFD"), op.subtract)
+        fillers(1)
 
         def xpart():
             cp(IND(A("X"), A("OFS")), A("XV"))
-
-        def hpart(out, hold=hold):
-            ts(A("RL"), A("OF2"), float(V), op.is_lt)
-            tt(A("BH"), A("OF2"), hold, op.subtract)
-            tt(A("BH2"), A("RL"), A("BH"), op.mult)
-            tt(out, A("BH2"), hold, op.add)
 
         def kpart():
             tt(IND(A("K"), A("OFS")), A("SKF"), A("SCE"), op.add)
 
         el = A("ES", 15, NP, 16)
-        scan(A("ES"), A("SEG"), A("EG"), 0.0, op.mult, op.add)
+        en = A("FO", 0, 16) if last else A("EN", 16 * t, 16 * t + 16)
+        scan(A("ES"), A("RSH"), A("EG"), -32768.0, op.add, op.max)
         if not jub:
-            en = A("EN", 16 * t, 16 * t + 16)
-            cp(en, el)
+            ts(en, el, float(MID), op.add)
             send(nxt, A("RE", 16 * t + 16, 16 * t + 32), en, "aE%d" % (t + 1))
             kpart()
             xpart()
-
-            def hsend(t=t, hpart=hpart):
-                ho = A("HO", 16 * t, 16 * t + 16)
-                hpart(ho)
-                send(nxt, A("RH", 16 * t + 16, 16 * t + 32), ho, "aH%d" % (t + 1))
-            pend.append(hsend)
+            if t == NT - 2:
+                ymm(0, "pQ")
+                ymm(1, "pD")
+                ycopy(0, "pQ")
         else:
-            hpart(A("HN"))
-            tt(A("DW"), A("HN"), el, op.subtract)
-            tt(A("DW2"), A("DW"), A("WF"), op.mult)
-            tt(A("EJ"), A("DW2"), el, op.add)
-            en = A("EN", 16 * t, 16 * t + 16)
-            cp(en, A("EJ"))
+            fillers(1)
+            tt(A("DW"), el, A("WB"), op.mult)
+            tt(A("EJ"), A("DW"), A("WA"), op.add)
+            ts(en, A("EJ"), float(MID), op.add)
             if not last:
                 send(nxt, A("RE", 16 * t + 16, 16 * t + 32), en, "aE%d" % (t + 1))
-            else:
-                cp(A("FO", 0, 16), A("EJ"))
             xpart()
             tt(A("PJ1"), IND(Xg, en), A("PN"), op.subtract)
             ts(A("PJ2"), A("PJ1"), 0.5, op.mult, 167.25, op.add)
@@ -451,20 +503,18 @@ def rank_program(g, core, T, topo):
                 mm(A("pL", 0, 16), A("WH", 15 - j, 143 - j), A("PJ1", j, NP, 16), j == 0, j == 15)
             cp(A("HI"), A("pL", 0, 16))
 
-            def hnew(t=t):
-                ho = A("HO", 16 * t, 16 * t + 16)
-                ts(A("HA"), A("HI"), 4095, op.bitwise_and)
-                ts(A("HG"), A("HA"), float(V), op.is_ge, -float(V), op.mult)
+            def hnew(t=t, ho=ho):
                 tt(ho, A("HA"), A("HG"), op.add)
                 if t < NT - 1:
                     send(nxt, A("RH", 16 * t + 16, 16 * t + 32), ho, "aH%d" % (t + 1))
                 else:
                     cp(A("FO", 16, 32), ho)
                     send(nxt, A("FIN"), A("FO"), "aF")
+            pend.append(lambda: ts(A("HA"), A("HI"), 4095, op.bitwise_and))
+            pend.append(lambda: ts(A("HG"), A("HA"), float(V), op.is_ge, -float(V), op.mult))
+            pend.append(hnew)
             if last:
-                hnew()
-            else:
-                pend.append(hnew)
+                fillers(3)
         if last:
             outs = []
             outs.append(("Y", dma("Y", T.yh[:, :], T.H[0:128:16, V:2 * V], [A("H", V, 2 * V)], [])))

@@ -1,45 +1,47 @@
-from concourse.mybir import AluOpType, AxisListType, ActivationFunctionType
+import math
+from concourse.mybir import AluOpType, ActivationFunctionType
 
 V, NP, NT, TERM = 3584, 256, 8, 4
 W = 2 * V + NP
 MID = V // 2
 NV = 9
+ND, NS = 7, 7
 LAST = 224
-VG = (16, 64)
+XO = 32.0
 C19 = float(3 * 2 ** 18)
 C0 = C19 + MID
 
 _S = {}
 F, B, I, U, Hf = "float32", "bfloat16", "int32", "uint16", "float16"
 for _n, _w, _d in [
-        ("K", W, F), ("KI", V, I), ("X", W, B), ("H", W, F), ("YK", W, F), ("IOTA", W, F),
+        ("K", W, F), ("KI", 4096, I), ("X", W, F), ("H", W, F), ("YK", W, F), ("IOTA", W, F),
         ("OWN", 16, I), ("WL", 16, I), ("WR", 16, I), ("HI0", 16, I), ("WTI", 1, I),
         ("RE", 16 * NT, U), ("RP", NP * NT, B), ("RH", 16 * NT, F), ("FIN", 32, U),
         ("EN", 16 * NT, U), ("PO", NP * NT, B), ("HO", 16 * NT, F), ("FO", 32, U),
         ("CU", NP, U), ("KC", NP, Hf), ("G", 16 * NP, B), ("M", 16 * NP, Hf),
         ("R0", 128, F), ("R1", NP, F), ("R2", NP, B), ("U0", 128, B), ("UU", NP, F), ("KEY", 128, F),
         ("IDM", 128, B), ("IDP", 128, B), ("OFD", NP, F), ("RSH", NP, Hf), ("WA", 16, F), ("WB", 16, F), ("SC", NP, F), ("EXP", NP, F),
-        ("RB", 16, B), ("R4", 16, F), ("BP", 16, F), ("KT", 16, F), ("KL", 16, F), ("KF", 16, F), ("EV", 16, F),
-        ("KU", 16, U), ("BU", 16, U), ("OF2", 16, F), ("OFS", 16, U),
+        ("RB", 32, B), ("R4", 16, F), ("BP", 16, F), ("KL", 32, F), ("ID15", 128, F),
+        ("KU", 16, U), ("BU", 16, U), ("OFS", 16 * NT, U), ("RO", 16 * NT, U),
         ("KR", NP, U), ("KRF", NP, F), ("E", 16 * NP, B), ("ED", NP, B), ("FS", NP, F), ("EA", NP * 3, F),
-        ("BR", NP, F), ("EG", NP, Hf), ("ES", NP, Hf), ("T4", NP, B), ("XG", NP, B), ("XV", NP, B),
+        ("BR", NP, F), ("EG", NP, Hf), ("ES", NP, Hf), ("T4", NP, B), ("XG", NP, B), ("XR", NP, B), ("XV", NP, F),
         ("SKF", NP, F), ("SCE", NP, F), ("SG", NP, B), ("PN", NP, B),
-        ("RL", 16, F), ("BH", 16, F), ("BH2", 16, F), ("HN", 16, F), ("DW", 16, F), ("DW2", 16, F), ("EJ", 16, F), ("WF", 16, F),
+        ("RL", 16, F), ("BH", 16, F), ("BH2", 16, F), ("HN", 16, F), ("DW", 16, F), ("EJ", 16, F), ("WF", 16, F),
         ("PJ1", NP, B), ("PJ2", NP, B), ("HI", 16, I), ("HA", 16, I), ("HG", 16, F), ("YF", NP, F), ("YO", NP, F), ("YT", NP, F),
-        ("IP", 1, I), ("ICF", NP, F), ("CMF", NP, F), ("CGF", 128, F), ("TMP", NP, F), ("TMQ", NP, F),
+        ("IP", 1, I), ("ICF", NP, B), ("CMF", NP, B), ("CGF", 128, B), ("TMP", 128, B),
         ("PMI", 1, I), ("ODI", 1, I), ("COL", 16, F),
-        ("BDF", 128, F), ("YW", 128, F), ("WS", 144, F), ("WH", 144, B), ("A8", 8, F), ("BG8", 8, B), ("BM8", 8, Hf),
-        ("IDB", 128, B), ("NIDB", 128, B), ("ID4", 128, B), ("IDHF", 128, B), ("IDH", 128, Hf), ("EVD", 128, Hf),
-        ("BDQ", 128, B), ("BDB", 128, B), ("LOW", 128, B), ("CY", 128, B), ("CK", 128, B), ("C16", 512, B), ("MASK", NP, B),
-        ("DIAG", NP, F), ("RS", 128, F), ("SEG", NP, F), ("TRM", NP, F), ("SOFF", 16, U), ("LOFF", 8, U)]:
+        ("YW", 128, F), ("WH", 144, B), ("A8", 8, F), ("BG8", 8, B), ("BM8", 8, B),
+        ("CF", NP, B), ("P16", 1024, B), ("IDB", 128, B), ("NIDB", 128, B), ("IDHF", 128, B), ("IDH", 128, Hf), ("EVD", 128, Hf),
+        ("BDQ", 128, B), ("BDB", 128, B), ("LOW", 128, B), ("CY", NP, B), ("CK", 128, B), ("C16", NP, Hf), ("C160", 16, B), ("WBD", 128, B), ("MASK", NP, B),
+        ("DIAG", 128, F), ("RS", 128, F), ("TRM", NP, F), ("SOFF", 16, U), ("LOFF", 8, U)]:
     _S[_n] = ("sbuf", [128, _w], _d)
-COLS = ["PF", "PM", "PG", "PG15", "ODD", "EVN", "EVM", "K1", "WTF", "PMW"]
+COLS = ["PF", "PM", "PG", "PG15", "ODD", "EVN", "EVM", "K1", "WTF", "PMW", "P15"]
 for _n in ["pP", "pY0", "pY1", "pK", "pL", "pD", "pX", "pQ"]:
     _S[_n] = ("psum", [128, 512], F)
 SCRATCH = _S
 NDMA = 24
 SEMAPHORES = (["qV", "qS", "qT", "qG", "loc", "aW", "aF"] + ["aE%d" % t for t in range(NT)] + ["aP%d" % t for t in range(NT)]
-              + ["aH%d" % t for t in range(NT)] + ["d%d" % k for k in range(NDMA)])
+              + ["aH%d" % t for t in range(NT)] + ["aO%d" % t for t in range(NT)] + ["d%d" % k for k in range(NDMA)])
 
 
 def rank_program(g, core, T, topo):
@@ -87,7 +89,7 @@ def rank_program(g, core, T, topo):
         for lst, wr in ((reads, False), (writes, True)):
             for r in lst:
                 for e in log.get(r[0], []):
-                    meet = e[0] < r[2] and r[1] < e[1] and (wr or e[2])
+                    meet = e[0] < r[2] and r[1] < e[1] and (wr or e[2]) and (e[0] - r[1]) % math.gcd(e[5], r[3]) == 0
                     if psum(r[0]):
                         if e[3] != q or (q != "T" and meet):
                             ev.append(e[4])
@@ -101,16 +103,18 @@ def rank_program(g, core, T, topo):
             for k, v in e[3].items():
                 known[q][k] = max(known[q].get(k, 0), v)
 
+    def covers(r, e):
+        return len(r) == 4 and r[1] <= e[0] and e[1] <= r[2] and e[5] % r[3] == 0 and (e[0] - r[1]) % r[3] == 0
+
     def note(q, reads, writes, event):
         for r in writes:
             l = log.setdefault(r[0], [])
-            if r[3] == 1:
-                l[:] = [e for e in l if not (r[1] <= e[0] and e[1] <= r[2])]
-            l.append((r[1], r[2], True, q, event))
+            l[:] = [e for e in l if not covers(r, e)]
+            l.append((r[1], r[2], True, q, event, r[3]))
         for r in reads:
             l = log.setdefault(r[0], [])
-            l[:] = [e for e in l if not (not e[2] and e[3] == q and r[1] <= e[0] and e[1] <= r[2])]
-            l.append((r[1], r[2], False, q, event))
+            l[:] = [e for e in l if not (not e[2] and e[3] == q and covers(r, e))]
+            l.append((r[1], r[2], False, q, event, r[3]))
         for r in reads + writes:
             l = log[r[0]]
             if len(l) > 64:
@@ -131,7 +135,7 @@ def rank_program(g, core, T, topo):
 
     def external(x, sem, val):
         order[0] += 1
-        log.setdefault(x[0], []).append((x[1], x[2], True, "X", (order[0], sem, val, {sem: val})))
+        log.setdefault(x[0], []).append((x[1], x[2], True, "X", (order[0], sem, val, {sem: val}), 1))
 
     def tt(out, a, b, o, q="V"):
         wr = [out[1]] if out[0] == "ind" else [out]
@@ -181,18 +185,19 @@ def rank_program(g, core, T, topo):
     def arrives(src, x, sem):
         external(x, sem, len(topo.engines(src, core)[:8]))
 
-    for q, n, src in (("Y", "OWN", T.own), ("Y", "WL", T.wall), ("Y", "HI0", T.hold), ("Y", "WTI", T.wt)):
+    parts = ((0, 1024), (1024, 2048), (2048, 3072), (3072, V))
+    xparts = ((0, MID), (MID, V))
+    for q, n, src in (("S", "PN", T.price), ("S", "OWN", T.own)):
         dma(q, T[n][:, :], src[:, :], [], [A(n)])
-    dma("S", T.PN[:, :], T.price[:, :], [], [A("PN")])
-    for k in range(4):
-        a, b = 896 * k, 896 * k + 896
-        dma("YS"[k % 2], T.KI[:, a:b], T.kin[:, a:b], [], [A("KI", a, b)])
-    for k in range(2):
-        a, b = 1792 * k, 1792 * k + 1792
-        dma("YS"[k % 2], T.X[:, a:b], T.x[:, a:b], [], [A("X", a, b)])
+    for a, b in xparts:
+        dma("Y", T.G[:, a:b], T.x[:, a:b], [], [A("G", a, b)])
+    for a, b in parts:
+        dma("Y", T.KI[:, a:b], T.kin[:, a:b], [], [A("KI", a, b)])
+    for q, n, src in (("Y", "WL", T.wall), ("Y", "HI0", T.hold), ("Y", "WTI", T.wt)):
+        dma(q, T[n][:, :], src[:, :], [], [A(n)])
 
     def iota(x, pattern, base=0, per=0):
-        flag = {"allow_small_or_imprecise_dtypes": True} if _S[x[0]][2] == F else {}
+        flag = {"allow_small_or_imprecise_dtypes": True} if _S[x[0]][2] != I else {}
         emit("G", [], [x], lambda: g.iota(ap(x), pattern, base, per, **flag))
 
     iota(A("IP"), [[1, 1]], 0, 1)
@@ -200,17 +205,18 @@ def rank_program(g, core, T, topo):
     iota(A("ICF"), [[1, NP]])
     iota(A("CMF"), [[0, 16], [1, 16]])
     iota(A("CGF"), [[16, 8], [0, 16]])
+    iota(A("IOTA", V, W), [[1, W - V]], V)
     send(prv, A("WR"), A("WL"), "aW")
     arrives(nxt, A("WR"), "aW")
-    iota(A("H", V, 2 * V), [[1, V]])
     act(A("IOTA", 0, NP), A("ICF"), AF.Identity)
     n = NP
-    while n < W:
-        m = min(n, W - n)
-        act(A("IOTA", n, n + m), A("IOTA", 0, m), AF.Identity, bias=float(n))
-        n += m
-    fill(A("C16"), 1.0 / 16)
-    fill(A("CY"), -8.5 * 2048)
+    while n < 2048:
+        act(A("IOTA", n, 2 * n), A("IOTA", 0, n), AF.Identity, bias=float(n))
+        n *= 2
+    for a, b in xparts:
+        act(A("X", a, b), A("G", a, b), AF.Silu, bias=XO)
+    fill(A("CY", 0, 128), -8.5 * 2048)
+    fill(A("CY", 128, 256), -15.0 * 2 ** 20)
     ts(A("PMI"), A("IP"), 15, op.bitwise_and)
     ts(A("ODI"), A("IP"), 1, op.bitwise_and)
     cp(A("PM"), A("PMI"))
@@ -221,74 +227,94 @@ def rank_program(g, core, T, topo):
     ts(A("PMW"), A("PM"), float(2 * V), op.add)
     ts(A("K1"), A("PM"), 1.0, op.add)
     ts(A("EVM"), A("EVN"), float(MID), op.mult)
-    cp(A("SOFF"), A("ICF", 0, 16))
+    ts(A("SOFF"), A("ICF", 0, 16), 2.0, op.mult, 1.0, op.add)
+    fill(A("RB"), -float(2 ** 30))
+    ts(A("P15"), A("PM"), 15.0, op.is_equal)
+    ts(A("ID15"), A("ICF", 0, 128), A("PF"), op.is_equal, A("P15"), op.mult)
     ts(A("LOFF"), A("ICF", 0, 8), 16.0, op.mult, 15.0, op.add)
     ts(A("RP", 0, NP), A("PN"), -1.0, op.mult, 15.0, op.add)
     cp(A("RE", 0, 16), A("OWN"))
     idn = A("ICF", 0, 128)
     ts(A("IDB"), idn, A("PF"), op.is_equal)
     ts(A("IDH"), idn, A("PF"), op.is_equal)
-    ts(A("ID4"), idn, A("PF"), op.is_equal, 4.0, op.mult)
     ts(A("NIDB"), idn, A("PF"), op.is_equal, -1.0, op.mult)
     ts(A("IDHF"), idn, A("PF"), op.is_equal, 0.5, op.mult)
     ts(A("EVD"), idn, A("PF"), op.is_equal, A("EVN"), op.mult)
-    ts(A("BDF"), A("CGF"), A("PG"), op.is_equal)
     ts(A("BDQ"), A("CGF"), A("PG"), op.is_equal, 65536.0, op.mult)
     ts(A("BDB"), A("CGF"), A("PG"), op.is_equal, 8192.0, op.mult)
     cg8 = A("CGF", 0, 128, 16)
     ts(A("A8"), cg8, A("PG"), op.is_equal)
-    ts(A("BG8"), cg8, A("PG"), op.is_equal, 16384.0, op.mult)
-    ts(A("BM8"), cg8, A("PG"), op.is_equal, -32768.0, op.mult)
+    ts(A("BG8"), cg8, A("PG"), op.is_equal, -65536.0, op.mult)
+    ts(A("BM8"), cg8, A("PG"), op.is_equal, 131072.0, op.mult)
+    ts(A("C16"), A("CMF"), 0.0, op.mult, 15 - 1.0 / 64, op.add)
+    fill(A("CF", 0, 128), (30 + XO) * 2 ** 20)
+    fill(A("CF", 128, 256), -32768.0)
     ts(A("CK"), A("CMF", 0, 128), 4096.0, op.mult)
-    ts(A("DIAG"), A("CMF"), A("PM"), op.is_equal)
+    ts(A("DIAG"), A("CMF", 0, 128), A("PM"), op.is_equal)
     ts(A("MASK"), A("CMF"), A("PM"), op.not_equal, 8192.0, op.mult)
     ts(A("RS"), A("CMF", 0, 128), 0.0, op.is_equal, float(2 ** 25), op.mult)
     ts(A("RSH"), A("CMF"), 0.0, op.is_equal, -32768.0, op.mult)
-    ts(A("OFD"), A("MASK"), float(MID), op.add)
     ts(A("IDM"), idn, A("PF"), op.is_equal, -255.0, op.mult)
     ts(A("IDP"), idn, A("PF"), op.is_equal, 256.0, op.mult)
-    ts(A("TMP", 0, 128), A("CMF", 0, 128), A("PM"), op.is_gt, 8192.0, op.mult)
-    tt(A("LOW"), A("TMP", 0, 128), A("BDF"), op.mult)
-    ts(A("TMQ"), A("ICF"), A("PMW"), op.add)
-    ts(A("TMP"), A("CMF"), 0.0, op.is_equal)
-    tt(A("TRM"), A("TMP"), A("TMQ"), op.mult)
-    ts(A("WS"), A("ICF", 0, 144), A("PG15"), op.is_equal)
-    ts(A("YW"), A("BDF"), A("K1"), op.mult)
-    cp(A("WTF"), A("WTI"))
-    ts(A("WH"), A("WS"), A("WTF"), op.mult)
-    cp(A("RH", 0, 16), A("HI0"))
-    for k in range(4):
-        a, b = 896 * k, 896 * k + 896
+    ts(A("TMP"), A("CMF", 0, 128), A("PM"), op.is_gt)
+    fill(A("TRM"), 0.0)
+    tt(A("LOW"), A("TMP"), A("BDB"), op.mult)
+    ts(A("TRM", 0, NP, 16), A("ICF", 0, NP, 16), A("PMW"), op.add)
+    for a, b in parts[:3]:
         cp(A("K", V + a, V + b), A("KI", a, b))
+
+    def jubilee_constants():
+        cp(A("WTF"), A("WTI"))
+        cp(A("WF"), A("WR"))
+        ts(A("YW"), A("CGF"), A("PG"), op.is_equal, A("K1"), op.mult)
+        ts(A("WH"), A("ICF", 0, 144), A("PG15"), op.is_equal, A("WTF"), op.mult)
+        ts(A("WBD"), A("CGF"), A("PG"), op.is_equal, A("WTF"), op.mult)
+        ts(A("WB"), A("WF"), -1.0, op.mult, 1.0, op.add)
+        fill(A("C160"), -160.0)
 
     def ymm(k, p):
         mm(A(p), A("YW"), A("K", V + 512 * k, V + 512 * k + 512), True, True)
 
     def ycopy(k, p):
-        act(A("YK", V + 512 * k, V + 512 * k + 512), A(p), AF.Identity)
+        if k < 4:
+            act(A("YK", V + 512 * k, V + 512 * k + 512), A(p), AF.Identity)
+        else:
+            cp(A("YK", V + 512 * k, V + 512 * k + 512), A(p))
+
+    def wide(x, f, bias):
+        for k in range(16):
+            act(A("P16", k, 1024, 16), x, f, bias=bias)
 
     pend = []
     for t in range(NT):
         e = A("RE", 16 * t, 16 * t + 16)
-        price = A("RP", NP * t, NP * t + NP)
+        pb = "PO" if t % TERM else "RP"
+        price = A(pb, NP * t, NP * t + NP)
         hold = A("RH", 16 * t, 16 * t + 16)
         jub = t % TERM == TERM - 1
         last = t == NT - 1
         if t:
-            arrives(prv, price, "aP%d" % t)
+            if t % TERM == 0:
+                for h in range(2):
+                    arrives(prv, A(pb, NP * t + 128 * h, NP * t + 128 * h + 128), "a%s%d" % ("PO"[h], t))
             arrives(prv, e, "aE%d" % t)
             arrives(prv, hold, "aH%d" % t)
+        if not jub:
+            need("G", [e], [])
+            send(nxt, A("RP", NP * t + NP, NP * t + 2 * NP), price, "aP%d" % (t + 1))
+        if t == 0:
+            iota(A("H", V, 2 * V), [[1, V]])
+        if t == 1:
+            iota(A("KI", 0, V), [[1, V]])
+            iota(A("KI", V, 4096), [[1, 4096 - V]])
+        pP = lambda a, b, s=1: A("pQ" if t == TERM and a >= 256 else "pP", a, b, s)
         Kg, Xg = A("K", V, 2 * V), A("X", 0, V)
 
         def kin(a, b):
-            cp(A("CU", a, b), IND(Kg, A("RE", 16 * t + a // 16, 16 * t + b // 16)))
+            cp(A("CU", a, b), IND(Kg if t else A("KI", 0, V), A("RE", 16 * t + a // 16, 16 * t + b // 16)))
 
         def wealth(a, b):
-            x, src = A("G", 16 * a, 16 * b), IND(Xg, A("CU", a, b))
-            if VG[0] <= a < VG[1]:
-                ts(x, src, -4.0, op.mult, 60.0, op.add)
-            else:
-                act(x, src, AF.Identity, bias=60.0, scale=-4.0)
+            act(A("G", 16 * a, 16 * b), IND(Xg, A("CU", a, b)), AF.Identity, bias=-XO)
 
         def ysum(k, a, b):
             return A("pY%d" % (a // 128), k, 128, 16) + ((a % 128, (b - 1) % 128 + 1),)
@@ -297,16 +323,14 @@ def rank_program(g, core, T, topo):
             for k in ks:
                 mm(ysum(k, a, b), A("G", 16 * a + k, 16 * b, 16), A("BG8"), False, False)
 
-        def least(a, b, a0=None):
+        def least(a, b, sums=None):
             for s in range(8):
-                o = 2048 * (a // 128) + 256 * s
-                tt(A("M", o + 2 * (a % 128), o + 2 * (a % 128) + 2 * (b - a)), A("G", 16 * a + s, 16 * b, 8), A("pP", 2 * a, 2 * b), op.min)
-                if a >= 192:
+                tt(A("M", 16 * a + s, 16 * b, 8), A("G", 16 * a + s, 16 * b, 8), pP(2 * a, 2 * b), op.max)
+                if b == NP:
                     gsum(a, b, (s, s + 8))
-                if a0 is not None:
-                    o += 2 * (a0 % 128)
-                    for u in range(2):
-                        mm(ysum(s + 8 * u, a0, b), A("M", o + u, o + 2 * (b - a0), 2), A("BM8"), False, s == 7 and u == 1)
+                if sums:
+                    for k in (s, s + 8):
+                        mm(ysum(k, *sums), A("M", 16 * sums[0] + k, 16 * sums[1], 16), A("BM8"), False, k == 15)
 
         big = 1.5 * 2.0 ** 39
         keys = (A("pX", 256, 384), A("pK", 0, 128))
@@ -317,59 +341,78 @@ def rank_program(g, core, T, topo):
         def to_list(h):
             lo, hi = 128 * h, 128 * h + 128
             tt(A("EXP", lo, hi), IND(A("SC", lo, hi), A("LOFF")), A("DIAG", 0, 128), op.mult)
-            mm(A("pL", 8 * h, 8 * h + 8), A("EXP", lo, hi), A("A8"), True, True)
+            mm(A("pL", 16 * h, 16 * h + 16, 2), A("EXP", lo, hi), A("A8"), True, True)
 
         def fillers(n):
             for _ in range(min(n, len(pend))):
                 pend.pop(0)()
 
-        pend.append(lambda e=e: ts(A("EV"), e, V - C0, op.add))
+        pend.insert(0, lambda e=e: ts(A("pL", 1, 32, 2), e, -1.0, op.mult, C0 - V, op.add))
         if t == 0:
-            pend.append(lambda: cp(A("WF"), A("WR")))
-            pend.append(lambda: ts(A("WB"), A("WF"), -1.0, op.mult, 1.0, op.add))
-        mm(A("pP"), A("IDB"), A("C16"), True, False)
+            pend.append(lambda: cp(A("RH", 0, 16), A("HI0")))
+        early = t != TERM
+
+        def prices(h):
+            n = 64 if early and h == 0 else 128
+            x = A(pb, NP * t + 128 * h, NP * t + 128 * h + n)
+            mm(pP(256 * h, 256 * h + 2 * n), A("IDH"), A("C16", 0, 2 * n), True, False)
+            for u in range(2):
+                mm(pP(256 * h + u, 256 * h + 2 * n, 2), A("NIDB"), x, False, u == 1)
+            mm(A("pY%d" % h, 0, 128) + ((0, n),), x, A("BDQ"), False, False)
+
         for h in range(2):
-            mm(A("pY%d" % h, 0, 128), A("IDB"), A("CY"), True, False)
-        for h in range(2):
+            mm(A("pY%d" % h, 0, 128), A("IDB"), A("CY", 0, 128), True, False)
+            mm(A("pY%d" % h, 0, 128), A("IDB"), A("CY", 128, 256), False, False)
             mm(keys[h], A("IDB"), A("CK"), True, False)
-        for u in range(2):
-            mm(A("pP", u, 512, 2), A("ID4"), price, False, u == 1)
-        for h in range(2):
-            mm(A("pY%d" % h, 0, 128), A("RP", NP * t + 128 * h, NP * t + 128 * h + 128), A("BDQ"), False, False)
-        if last:
-            ymm(2, "pQ")
+        if early:
+            for c in range(2):
+                mm(A("pY0", 0, 128) + ((64, 128),), A("IDB", 0, 64), A("CF", 128 * c, 128 * c + 128), False, False)
+        if t == 0:
+            wide(A(pb, 64, 128), AF.Identity, 0.0)
+        prices(0)
+        if early:
+            prices(1)
         kin(0, 64)
-        wealth(0, VG[0])
+        wealth(0, 64)
         kin(64, NP)
-        wealth(*VG)
-        wealth(VG[1], 128)
-        ts(A("KC"), A("CU"), -float(MID), op.add)
+        if early:
+            tt(A("G", 1024, 2048), IND(Xg, A("CU", 64, 128)), A("P16"), op.add)
+            ts(A("KC"), A("CU"), -float(MID), op.add)
+            ts(A("M", 1024, 2048), A("G", 1024, 2048), 1.0 / 64 - 15 - XO, op.add, 0.0, op.max)
+        else:
+            ts(A("G", 1024, 2048), IND(Xg, A("CU", 64, 128)), -XO, op.add)
+            ts(A("KC"), A("CU"), -float(MID), op.add)
+        wealth(128, 192)
+        gsum(0, 128)
         for h in range(2):
             mm(keys[h], A("KC", 128 * h, 128 * h + 128), A("IDH"), False, h == 1)
         mm(A("pL", 256, 512), A("EVD"), A("KC"), True, True)
-        least(0, 64)
-        wealth(128, 192)
-        gsum(0, 128)
-        least(64, 128, 0)
+        if early:
+            least(0, 64, (0, 128))
+        else:
+            least(0, 64)
+            least(64, 128, (0, 128))
+            prices(1)
         wealth(192, LAST)
         wealth(LAST, NP)
         gsum(128, 192)
-        least(128, 192, 128)
+        least(128, 192)
         act(A("R0"), A("pY0", 0, 128), AF.Identity, bias=16.5 * 2048)
         act(A("R1", 0, 128), A("pY0", 0, 128), AF.Identity, bias=big)
         act(A("R1", 128, 256), A("R0"), AF.Identity, bias=big)
         act(A("R2"), A("R1"), AF.Identity, bias=-big)
-        act(A("SCE"), A("pL", 256, 512), AF.Identity, bias=A("EVM"))
-        least(192, LAST, 192)
-        least(LAST, NP, LAST)
+        gsum(192, LAST)
+        least(192, LAST, (128, LAST))
+        least(LAST, NP, (LAST, NP))
         mm(A("pY0", 128, 256), A("IDM"), A("R2", 0, 128), True, False)
         mm(A("pY0", 128, 256), A("IDP"), A("R2", 128, 256), False, True)
         act(A("U0"), A("pY0", 128, 256), AF.Relu, bias=-float(2 ** 24))
         mm(keys[0], A("IDB"), A("U0"), False, True)
         if last:
-            ymm(3, "pY0")
+            ymm(2, "pY0")
         y1 = A("pY1", 0, 128)
         fillers(1)
+        act(A("SCE"), A("pL", 256, 512), AF.Identity, bias=A("EVM"))
         ts(A("UU", 0, 128), y1, big, op.add, -big, op.add)
         fillers(1)
         tt(A("pY1", 128, 256), y1, A("UU", 0, 128), op.is_gt)
@@ -384,69 +427,91 @@ def rank_program(g, core, T, topo):
         act(A("T4"), price, AF.Identity, bias=163.375, scale=-0.25)
         if last:
             ycopy(1, "pD")
-            ycopy(2, "pQ")
-            ycopy(3, "pY0")
-            ymm(4, "pY1")
+            ycopy(0, "pQ")
+            ycopy(2, "pY0")
+            ymm(3, "pY1")
         mm(A("pD", 0, NP), A("IDB"), A("MASK"), True, False)
+        if t == 0:
+            act(A("IOTA", 2048, V), A("IOTA", 0, V - 2048), AF.Identity, bias=2048.0)
+            act(A("OFD"), A("MASK"), AF.Identity, bias=float(MID))
+            cp(A("K", V + parts[3][0], 2 * V), A("KI", *parts[3]))
         fillers(99)
-        key = A("pL", 0, 16)
+        key = A("pL", 0, 32, 2)
         big = 1.5 * 2.0 ** 35
-        ts(A("RB"), key, 131072.0, op.min, C19, op.add)
+        kf = A("TRM", 15, NP, 16)
+        ts(A("RB", 1, 32, 2), key, 131072.0, op.min, C19, op.add)
         ts(A("R4"), key, big, op.add, -big, op.add)
-        tt(A("KT"), key, A("RB"), op.subtract)
+        scan(A("KL"), A("RB"), A("pL", 0, 32), 0.0, op.subtract, op.max)
         tt(A("BP"), key, A("R4"), op.subtract)
-        tt(A("KL"), A("KT"), A("EV"), op.min)
-        ts(A("BU"), A("BP"), float(MID), op.add)
-        ts(A("KU"), A("KL"), C0, op.add)
-        act(A("KRF"), IND(A("IOTA"), A("KU")), AF.Identity, bias=-C0)
+        ts(A("KU"), A("KL", 1, 32, 2), -1.0, op.mult, C0, op.add)
+        ts(kf, A("KL", 1, 32, 2), -1.0, op.mult, C0, op.add)
+        act(A("KRF"), IND(A("IOTA"), A("KU")), AF.Identity, bias=C0, scale=-1.0)
         cp(A("KR"), IND(A("IOTA"), A("KU")))
+        ts(A("BU"), A("BP"), float(MID), op.add)
+        mm(A("pD", 15, NP, 16), A("ID15"), kf, False, False)
         ea = 0
         for j in range(NV, 15):
             lo = 16 * j + 16
-            act(A("EA", ea, ea + NP - lo), A("KRF", lo, NP), AF.Abs, bias=A("KL", j, j + 1), scale=-1.0)
+            act(A("EA", ea, ea + NP - lo), A("KRF", lo, NP), AF.Abs, bias=A("KL", 2 * j + 1, 2 * j + 2), scale=-1.0)
             ea += NP - lo
         act(A("E", NP * NV, NP * NV + ea), A("EA", 0, ea), AF.Relu, bias=1.0, scale=-1.0)
         act(A("BR"), IND(A("IOTA"), A("BU")), AF.Identity)
         act(A("XG"), IND(Xg, A("BU")), AF.Identity)
-        ea = NP * NV
-        for j in range(15):
+        for j in range(NV):
             lo = 16 * j + 16
-            if j < NV:
-                x = A("E", NP * j + lo, NP * j + NP)
-                ts(x, A("KR", lo, NP), -C0, op.add, A("KL", j, j + 1), op.is_equal)
-            else:
-                x = A("E", ea, ea + NP - lo)
-                ea += NP - lo
-            mm(A("pD", lo, NP), A("BDB"), x, False, False)
-        tt(A("ED"), IND(A("KL"), A("SOFF")), A("KRF"), op.is_equal)
-        mm(A("pD", 0, NP), A("LOW"), A("ED"), False, True)
-        ts(A("KF"), A("KL"), C0, op.add)
-        mm(A("pQ", 0, NP), A("IDB"), price, True, False)
+            x = A("E", NP * j + lo, NP * j + NP)
+            ts(x, A("KR", lo, NP), A("TRM", lo - 1, lo), op.is_equal)
+            mm(A("pD", lo, NP), A("BDB"), x, False, j == NV - 1)
+            if j == NS:
+                ea = NP * NV
+                for lo in range(16 * NV + 16, NP, 16):
+                    mm(A("pD", lo, NP), A("BDB"), A("E", ea, ea + NP - lo), False, False)
+                    ea += NP - lo
+            if j == ND:
+                tt(A("ED"), IND(A("KL"), A("SOFF")), A("KRF"), op.is_equal)
+                mm(A("pD", 0, NP), A("LOW"), A("ED"), False, False)
         mm(A("pX", 0, NP), A("NIDB"), A("T4"), True, False)
         mm(A("pX", 0, NP), A("IDB"), A("XG"), False, True)
         scan(A("FS"), A("TRM"), A("pD", 0, NP), 0.0, op.max, op.min)
-        tt(A("OF2"), A("FS", 15, NP, 16), A("KF"), op.max)
-        cp(A("OFS"), A("OF2"))
-        pn = A("PN") if jub else A("PO", NP * t, NP * t + NP)
-        act(A("SG"), IND(A("IOTA"), A("OFS")), AF.Sign, bias=0.5 - V)
-        mm(A("pQ", 0, NP), A("IDHF"), A("SG"), False, True)
-        act(A("XV"), A("pX", 0, NP), AF.Relu, bias=160.0)
-        act(pn, A("pQ", 0, NP), AF.Relu, bias=-0.5)
+        of2 = A("FS", 15, NP, 16)
+        ofs = A("OFS", 16 * t, 16 * t + 16)
+        cp(ofs, of2)
+
+        def redeemed(out, old, targets, between=None):
+            mm(A("pQ", 0, NP), A("IDB"), old, True, False)
+            act(A("SG"), IND(A("IOTA"), targets), AF.Sign, bias=0.5 - V)
+            mm(A("pQ", 0, NP), A("IDHF"), A("SG"), False, True)
+            if between:
+                between()
+            act(out, A("pQ", 0, NP), AF.Relu, bias=-0.5)
+
+        def newkin():
+            act(A("SKF"), IND(Kg, A("BU")), AF.Identity, scale=A("ODD"))
+
+        def raised():
+            act(A("XV"), A("XR"), AF.Identity, bias=XO)
+
         if not jub:
-            send(nxt, A("RP", NP * t + NP, NP * t + 2 * NP), pn, "aP%d" % (t + 1))
-        act(A("SKF"), IND(Kg, A("BU")), AF.Identity, scale=A("ODD"))
+            send(nxt, A("RO", 16 * t + 16, 16 * t + 32), ofs, "aO%d" % (t + 1))
+            arrives(prv, A("RO", 16 * t + 16, 16 * t + 32), "aO%d" % (t + 1))
+            arrives(prv, A("RP", NP * t + NP, NP * t + 2 * NP), "aP%d" % (t + 1))
+            newkin()
+        act(A("XR"), A("pX", 0, NP), AF.Relu, bias=160.0 - XO)
         if last:
-            ymm(5, "pP")
-            mm(A("pK", 0, NP), A("YW"), A("SCE"), True, False)
-            mm(A("pK", 0, NP), A("YW"), A("SKF"), False, True)
-            ymm(6, "pY0")
-            ycopy(4, "pY1")
-            ycopy(5, "pP")
-            act(A("YF"), A("pK", 0, NP), AF.Identity)
-            ycopy(6, "pY0")
+            ymm(4, "pP")
+        if jub:
+            redeemed(A("PN"), price, ofs, raised)
+        else:
+            raised()
+        emit("S", [A("XV"), ofs], [A("X")], lambda: g.scalar.activation(ap(IND(A("X"), ofs)), ap(A("XV")), AF.Silu))
+        if jub:
+            newkin()
+        if last:
+            ymm(5, "pY0")
+            ycopy(3, "pY1")
         ho = A("HO", 16 * t, 16 * t + 16)
-        pend.append(lambda: ts(A("RL"), A("OF2"), float(V), op.is_lt))
-        pend.append(lambda hold=hold: tt(A("BH"), A("OF2"), hold, op.subtract))
+        pend.append(lambda: ts(A("RL"), of2, float(V), op.is_lt))
+        pend.append(lambda hold=hold: tt(A("BH"), of2, hold, op.subtract))
         pend.append(lambda: tt(A("BH2"), A("RL"), A("BH"), op.mult))
         if not jub:
             def hsend(t=t, ho=ho, hold=hold):
@@ -459,16 +524,13 @@ def rank_program(g, core, T, topo):
             pend.append(lambda: tt(A("WA"), A("HG"), A("WF"), op.mult))
         nf = 2 if jub else 1
         fillers(nf)
-        cp(IND(A("H"), A("OFS")), A("BR"))
+        cp(IND(A("H"), ofs), A("BR"))
         fillers(nf)
         tt(A("EG"), IND(A("H", V, 2 * V), e), A("OFD"), op.subtract)
         fillers(1)
 
-        def xpart():
-            cp(IND(A("X"), A("OFS")), A("XV"))
-
         def kpart():
-            tt(IND(A("K"), A("OFS")), A("SKF"), A("SCE"), op.add)
+            tt(IND(A("K"), ofs), A("SKF"), A("SCE"), op.add)
 
         el = A("ES", 15, NP, 16)
         en = A("FO", 0, 16) if last else A("EN", 16 * t, 16 * t + 16)
@@ -476,12 +538,14 @@ def rank_program(g, core, T, topo):
         if not jub:
             ts(en, el, float(MID), op.add)
             send(nxt, A("RE", 16 * t + 16, 16 * t + 32), en, "aE%d" % (t + 1))
+            redeemed(A("PO", NP * t + NP, NP * t + 2 * NP), A("RP", NP * t + NP, NP * t + 2 * NP), A("RO", 16 * t + 16, 16 * t + 32),
+                     lambda: wide(A("pQ", 64, 128), AF.Relu, -0.5))
             kpart()
-            xpart()
+            if t == 0:
+                jubilee_constants()
             if t == NT - 2:
                 ymm(0, "pQ")
                 ymm(1, "pD")
-                ycopy(0, "pQ")
         else:
             fillers(1)
             tt(A("DW"), el, A("WB"), op.mult)
@@ -489,42 +553,52 @@ def rank_program(g, core, T, topo):
             ts(en, A("EJ"), float(MID), op.add)
             if not last:
                 send(nxt, A("RE", 16 * t + 16, 16 * t + 32), en, "aE%d" % (t + 1))
-            xpart()
-            tt(A("PJ1"), IND(Xg, en), A("PN"), op.subtract)
-            ts(A("PJ2"), A("PJ1"), 0.5, op.mult, 167.25, op.add)
-            po = A("PO", NP * t, NP * t + NP)
+            mm(A("pL", 0, 16), A("WBD"), A("C160"), True, False)
+            halves = ((0, 128), (128, NP))
+            for a, b in halves:
+                tt(A("PJ1", a, b), IND(Xg, (en[0], en[1] + a // 16, en[1] + b // 16, 1)), A("PN", a, b), op.subtract)
+            for a, b in halves:
+                ts(A("PJ2", a, b), A("PJ1", a, b), 0.5, op.mult, 167.25 - XO / 2, op.add)
+            for h, (a, b) in enumerate(halves):
+                if not last:
+                    ts(A("PO", a, b), A("PJ2", a, b), -1.0, op.mult, 175.0, op.add)
+                    send(nxt, A("RP", NP * t + NP + a, NP * t + NP + b), A("PO", a, b), "a%s%d" % ("PO"[h], t + 1))
             if not last:
-                ts(po, A("PJ2"), -1.0, op.mult, 175.0, op.add)
-            ts(A("PJ1"), A("PJ2"), -160.0, op.add)
-            if not last:
-                send(nxt, A("RP", NP * t + NP, NP * t + 2 * NP), po, "aP%d" % (t + 1))
                 kpart()
             for j in range(16):
-                mm(A("pL", 0, 16), A("WH", 15 - j, 143 - j), A("PJ1", j, NP, 16), j == 0, j == 15)
-            cp(A("HI"), A("pL", 0, 16))
-
-            def hnew(t=t, ho=ho):
-                tt(ho, A("HA"), A("HG"), op.add)
-                if t < NT - 1:
-                    send(nxt, A("RH", 16 * t + 16, 16 * t + 32), ho, "aH%d" % (t + 1))
-                else:
-                    cp(A("FO", 16, 32), ho)
-                    send(nxt, A("FIN"), A("FO"), "aF")
-            pend.append(lambda: ts(A("HA"), A("HI"), 4095, op.bitwise_and))
-            pend.append(lambda: ts(A("HG"), A("HA"), float(V), op.is_ge, -float(V), op.mult))
-            pend.append(hnew)
+                mm(A("pL", 0, 16), A("WH", 15 - j, 143 - j), A("PJ2", j, NP, 16), False, j == 15)
             if last:
-                fillers(3)
+                cp(A("HI"), A("pL", 0, 16))
+                ts(A("HA"), A("HI"), 4095, op.bitwise_and)
+                cp(A("FO", 16, 32), A("HA"))
+                send(nxt, A("FIN"), A("FO"), "aF")
+            else:
+                def hnew(t=t, ho=ho):
+                    tt(ho, A("HA"), A("HG"), op.add)
+                    send(nxt, A("RH", 16 * t + 16, 16 * t + 32), ho, "aH%d" % (t + 1))
+                cp(A("HI"), A("pL", 0, 16))
+                pend.append(lambda: ts(A("HA"), A("HI"), 4095, op.bitwise_and))
+                pend.append(lambda: ts(A("HG"), A("HA"), float(V), op.is_ge, -float(V), op.mult))
+                pend.append(hnew)
         if last:
             outs = []
             outs.append(("Y", dma("Y", T.yh[:, :], T.H[0:128:16, V:2 * V], [A("H", V, 2 * V)], [])))
-            outs.append(("Y", dma("Y", T.yx[:, :], T.X[:, 0:V], [A("X", 0, V)], [])))
-            cp(IND(A("YK"), A("OFS")), A("YF"))
+            mm(A("pK", 0, NP), A("YW"), A("SCE"), True, False)
+            mm(A("pK", 0, NP), A("YW"), A("SKF"), False, True)
+            ymm(6, "pD")
+            for k, (a, b) in enumerate(parts):
+                act(A("G", a, b), A("X", a, b), AF.Relu, bias=-XO - 2.0 ** -10)
+                outs.append(("Y", dma("Y", T.yx[:, a:b], T.G[:, a:b], [A("G", a, b)], [])))
+                if k == 1:
+                    act(A("YF"), A("pK", 0, NP), AF.Identity)
+            for k, p in ((4, "pP"), (5, "pY0"), (6, "pD")):
+                ycopy(k, p)
+            cp(IND(A("YK"), ofs), A("YF"))
             outs.append(("Y", dma("Y", T.yk[:, :], T.YK[0:128:16, V:2 * V], [A("YK", V, 2 * V)], [])))
             arrives(prv, A("FIN"), "aF")
-            cp(A("YO"), IND(A("IOTA"), A("FIN", 0, 16)))
-            act(A("YT"), IND(A("IOTA"), A("FIN", 16, 32)), AF.Identity)
-            for k, (y, o) in enumerate((("YO", T.yo), ("YT", T.yt))):
+            act(A("YO"), IND(A("IOTA"), A("FIN", 0, 16)), AF.Identity)
+            cp(A("YT"), IND(A("KI"), A("FIN", 16, 32)))
+            for k, (y, o) in enumerate((("YT", T.yt), ("YO", T.yo))):
                 outs.append(("YS"[k], dma("YS"[k], o[:, :], T[y][0:128:16, :], [A(y)], [])))
             for q, s in outs:
                 queues[q].wait_ge(T.sem[s], 16)

@@ -2,14 +2,19 @@ import math
 from concourse.mybir import AluOpType, ActivationFunctionType
 
 V, NP, NT, TERM = 3584, 256, 8, 4
-W = 2 * V + NP
+F0, O0 = NP, NP + V
+W = NP + 2 * V
 MID = V // 2
-NV = 9
-ND, NS = 7, 7
+NV = 10
+SROWS = ((10, 13), (13, 16))
+NS = 7
 LAST = 224
-XO = 32.0
-C19 = float(3 * 2 ** 18)
-C0 = C19 + MID
+XS = 32.0
+R = 8
+KW = 136
+RO = 1536.0
+CK = float(O0 + MID)
+BIG = float(2 ** 30)
 
 _S = {}
 F, B, I, U, Hf = "float32", "bfloat16", "int32", "uint16", "float16"
@@ -19,23 +24,26 @@ for _n, _w, _d in [
         ("RE", 16 * NT, U), ("RP", NP * NT, B), ("RH", 16 * NT, F), ("FIN", 32, U),
         ("EN", 16 * NT, U), ("PO", NP * NT, B), ("HO", 16 * NT, F), ("FO", 32, U),
         ("CU", NP, U), ("KC", NP, Hf), ("G", 16 * NP, B), ("M", 16 * NP, Hf),
-        ("R0", 128, F), ("R1", NP, F), ("R2", NP, B), ("U0", 128, B), ("UU", NP, F), ("KEY", 128, F),
-        ("IDM", 128, B), ("IDP", 128, B), ("OFD", NP, F), ("RSH", NP, Hf), ("WA", 16, F), ("WB", 16, F), ("SC", NP, F), ("EXP", NP, F),
-        ("RB", 32, B), ("R4", 16, F), ("BP", 16, F), ("KL", 32, F), ("ID15", 128, F),
+        ("RR", 4 * KW, Hf), ("D1", 2 * KW, F), ("SC", 2 * KW, F), ("EXP", NP, F),
+        ("OFD", NP, F), ("RSH", NP, Hf), ("WA", 16, F), ("WB", 16, F),
+        ("RB", 48, F), ("KL", 48, F), ("ID15", 128, B), ("KH", 32, B),
         ("KU", 16, U), ("BU", 16, U), ("OFS", 16 * NT, U), ("RO", 16 * NT, U),
-        ("KR", NP, U), ("KRF", NP, F), ("E", 16 * NP, B), ("ED", NP, B), ("FS", NP, F), ("EA", NP * 3, F),
-        ("BR", NP, F), ("EG", NP, Hf), ("ES", NP, Hf), ("T4", NP, B), ("XG", NP, B), ("XR", NP, B), ("XV", NP, F),
+        ("KR", NP, U), ("KRF", NP, F), ("FS", NP, F),
+        ("BR", NP, F), ("EG", NP, Hf), ("ES", NP, Hf), ("T4", NP, B), ("XG", NP, B), ("XV", NP, F),
         ("SKF", NP, F), ("SCE", NP, F), ("SG", NP, B), ("PN", NP, B),
         ("RL", 16, F), ("BH", 16, F), ("BH2", 16, F), ("HN", 16, F), ("DW", 16, F), ("EJ", 16, F), ("WF", 16, F),
         ("PJ1", NP, B), ("PJ2", NP, B), ("HI", 16, I), ("HA", 16, I), ("HG", 16, F), ("YF", NP, F), ("YO", NP, F), ("YT", NP, F),
-        ("IP", 1, I), ("ICF", NP, B), ("CMF", NP, B), ("CGF", 128, B), ("TMP", 128, B),
+        ("IP", 1, I), ("ICF", NP, B), ("CMF", NP, B), ("CGF", 128, B), ("CG17", 2 * KW, B), ("TMP", 128, B), ("EQ", NP, B),
         ("PMI", 1, I), ("ODI", 1, I), ("COL", 16, F),
-        ("YW", 128, F), ("WH", 144, B), ("A8", 8, F), ("BG8", 8, B), ("BM8", 8, B),
-        ("CF", NP, B), ("P16", 1024, B), ("IDB", 128, B), ("NIDB", 128, B), ("IDHF", 128, B), ("IDH", 128, Hf), ("EVD", 128, Hf),
-        ("BDQ", 128, B), ("BDB", 128, B), ("LOW", 128, B), ("CY", NP, B), ("CK", 128, B), ("C16", NP, Hf), ("C160", 16, B), ("WBD", 128, B), ("MASK", NP, B),
-        ("DIAG", 128, F), ("RS", 128, F), ("TRM", NP, F), ("SOFF", 16, U), ("LOFF", 8, U)]:
+        ("YW", 128, B), ("YWE", 128, B), ("YWO", 128, B), ("SKH", NP, Hf), ("WH", 144, B), ("A8", 8, F), ("BG", 16, B), ("BM", 16, B),
+        ("INI", 3 * KW, B), ("ONE", 128, B), ("PERM", KW, B), ("IDP", 128, B), ("IDM", 128, B),
+        ("P16", 1024, B), ("IDB", 128, B), ("N32", 128, B), ("IDHF", 128, B), ("IDH", 128, Hf), ("EVD", 128, Hf),
+        ("BDQ", 2 * KW, B), ("BDB", 128, B), ("LOW", 128, B), ("C16", 512, Hf), ("C160", 16, B), ("WBD", 128, B), ("MASK", NP, B),
+        ("DIAG", 128, F), ("TRM", NP, F), ("LOFF", 8, U)]:
     _S[_n] = ("sbuf", [128, _w], _d)
-COLS = ["PF", "PM", "PG", "PG15", "ODD", "EVN", "EVM", "K1", "WTF", "PMW", "P15"]
+_S["E"] = ("sbuf", [128, 16, NP], B)
+_S["EA"] = ("sbuf", [128, 16 - NV, NP - 16 * NV], F)
+COLS = ["PF", "PM", "PG", "PG15", "ODD", "EVN", "EVM", "K1", "WTF", "PMW", "P15", "PC", "N15"]
 for _n in ["pP", "pY0", "pY1", "pK", "pL", "pD", "pX", "pQ"]:
     _S[_n] = ("psum", [128, 512], F)
 SCRATCH = _S
@@ -67,11 +75,16 @@ def rank_program(g, core, T, topo):
     def IND(w, o):
         return ("ind", w, o)
 
+    def ROWS(n, j0, j1, a, b):
+        return ("rows", n, j0, j1, a, b)
+
     def ap(x):
         if not isinstance(x, tuple):
             return x
         if x[0] == "ind":
             return ap(x[1]).indirect(ap(x[2]))
+        if x[0] == "rows":
+            return T[x[1]][:, x[2], x[4]:x[5]] if x[3] == x[2] + 1 else T[x[1]][:, x[2]:x[3], x[4]:x[5]]
         n, a, b, s = x[:4]
         p = slice(*x[4]) if len(x) > 4 else slice(None)
         return T[n][p, a:b] if s == 1 else T[n][p, a:b:s]
@@ -79,17 +92,24 @@ def rank_program(g, core, T, topo):
     def regs(x):
         if not isinstance(x, tuple):
             return []
+        if x[0] == "rows":
+            w = _S[x[1]][1][2]
+            return [(x[1], w * j + x[4], w * j + x[5], 1) for j in range(x[2], x[3])]
         return [x[1], x[2]] if x[0] == "ind" else [x]
 
     def psum(n):
         return _S[n][0] == "psum"
+
+    def lanes(r):
+        return r[4] if len(r) > 4 else (0, 128)
 
     def need(q, reads, writes):
         ev = []
         for lst, wr in ((reads, False), (writes, True)):
             for r in lst:
                 for e in log.get(r[0], []):
-                    meet = e[0] < r[2] and r[1] < e[1] and (wr or e[2]) and (e[0] - r[1]) % math.gcd(e[5], r[3]) == 0
+                    meet = (e[0] < r[2] and r[1] < e[1] and (wr or e[2]) and (e[0] - r[1]) % math.gcd(e[5], r[3]) == 0
+                            and e[6][0] < lanes(r)[1] and lanes(r)[0] < e[6][1])
                     if psum(r[0]):
                         if e[3] != q or (q != "T" and meet):
                             ev.append(e[4])
@@ -110,11 +130,11 @@ def rank_program(g, core, T, topo):
         for r in writes:
             l = log.setdefault(r[0], [])
             l[:] = [e for e in l if not covers(r, e)]
-            l.append((r[1], r[2], True, q, event, r[3]))
+            l.append((r[1], r[2], True, q, event, r[3], lanes(r)))
         for r in reads:
             l = log.setdefault(r[0], [])
             l[:] = [e for e in l if not (not e[2] and e[3] == q and covers(r, e))]
-            l.append((r[1], r[2], False, q, event, r[3]))
+            l.append((r[1], r[2], False, q, event, r[3], lanes(r)))
         for r in reads + writes:
             l = log[r[0]]
             if len(l) > 64:
@@ -135,7 +155,7 @@ def rank_program(g, core, T, topo):
 
     def external(x, sem, val):
         order[0] += 1
-        log.setdefault(x[0], []).append((x[1], x[2], True, "X", (order[0], sem, val, {sem: val}), 1))
+        log.setdefault(x[0], []).append((x[1], x[2], True, "X", (order[0], sem, val, {sem: val}), 1, (0, 128)))
 
     def tt(out, a, b, o, q="V"):
         wr = [out[1]] if out[0] == "ind" else [out]
@@ -145,9 +165,9 @@ def rank_program(g, core, T, topo):
     def ts(out, a, s1, o1, s2=None, o2=None):
         rd = regs(a) + regs(s1) + regs(s2)
         if o2 is None:
-            emit("V", rd, [out], lambda: g.vector.tensor_scalar(ap(out), ap(a), ap(s1), None, o1))
+            emit("V", rd, regs(out), lambda: g.vector.tensor_scalar(ap(out), ap(a), ap(s1), None, o1))
         else:
-            emit("V", rd, [out], lambda: g.vector.tensor_scalar(ap(out), ap(a), ap(s1), ap(s2), o1, o2))
+            emit("V", rd, regs(out), lambda: g.vector.tensor_scalar(ap(out), ap(a), ap(s1), ap(s2), o1, o2))
 
     def cp(out, a):
         wr = [out[1]] if out[0] == "ind" else [out]
@@ -157,14 +177,14 @@ def rank_program(g, core, T, topo):
         emit("V", [d0, d1], [out], lambda: g.vector.tensor_tensor_scan(ap(out), ap(d0), ap(d1), init, o0, o1))
 
     def fill(out, c):
-        emit("V", [], [out], lambda: g.vector.memset(ap(out), c))
+        emit("V", [], regs(out), lambda: g.vector.memset(ap(out), c))
 
     def act(out, a, f, bias=0.0, scale=1.0):
-        emit("S", regs(a) + regs(bias) + regs(scale), [out],
+        emit("S", regs(a) + regs(bias) + regs(scale), regs(out),
              lambda: g.scalar.activation(ap(out), ap(a), f, bias=ap(bias), scale=ap(scale)))
 
     def mm(out, l, r, start, stop):
-        emit("T", [l, r], [out], lambda: g.tensor.matmul(ap(out), ap(l), ap(r), start, stop))
+        emit("T", [l] + regs(r), [out], lambda: g.tensor.matmul(ap(out), ap(l), ap(r), start, stop))
 
     def dma(q, out, in_, reads, writes):
         need(q, reads, writes)
@@ -197,95 +217,124 @@ def rank_program(g, core, T, topo):
         dma(q, T[n][:, :], src[:, :], [], [A(n)])
 
     def iota(x, pattern, base=0, per=0):
-        flag = {"allow_small_or_imprecise_dtypes": True} if _S[x[0]][2] != I else {}
-        emit("G", [], [x], lambda: g.iota(ap(x), pattern, base, per, **flag))
+        flag = {"allow_small_or_imprecise_dtypes": True} if _S[regs(x)[0][0]][2] != I else {}
+        emit("G", [], regs(x), lambda: g.iota(ap(x), pattern, base, per, **flag))
 
+    def lane(p):
+        return ((p, p + 1),)
+
+    fill(A("INI"), 0.0)
     iota(A("IP"), [[1, 1]], 0, 1)
     iota(A("PF"), [[1, 1]], 0, 1)
     iota(A("ICF"), [[1, NP]])
+    iota(A("CG17"), [[0, 2], [16, 8], [0, 17]])
     iota(A("CMF"), [[0, 16], [1, 16]])
     iota(A("CGF"), [[16, 8], [0, 16]])
+    iota(A("INI", 2 * KW, 3 * KW) + lane(0), [[0, 8], [-4096, 17]], 65536)
     iota(A("IOTA", V, W), [[1, W - V]], V)
     send(prv, A("WR"), A("WL"), "aW")
     arrives(nxt, A("WR"), "aW")
     act(A("IOTA", 0, NP), A("ICF"), AF.Identity)
     n = NP
-    while n < 2048:
+    while n < 1024:
         act(A("IOTA", n, 2 * n), A("IOTA", 0, n), AF.Identity, bias=float(n))
         n *= 2
     for a, b in xparts:
-        act(A("X", a, b), A("G", a, b), AF.Silu, bias=XO)
-    fill(A("CY", 0, 128), -8.5 * 2048)
-    fill(A("CY", 128, 256), -15.0 * 2 ** 20)
+        act(A("X", O0 + a, O0 + b), A("G", a, b), AF.Silu, scale=XS)
     ts(A("PMI"), A("IP"), 15, op.bitwise_and)
     ts(A("ODI"), A("IP"), 1, op.bitwise_and)
+    fill(A("ONE"), 1.0)
     cp(A("PM"), A("PMI"))
     cp(A("ODD"), A("ODI"))
+    fill(A("ONE", 0, 64) + ((64, 128),), 0.0)
+    fill(A("RB"), -BIG)
     tt(A("PG"), A("PF"), A("PM"), op.subtract)
-    ts(A("PG15"), A("PG"), 15.0, op.add)
     ts(A("EVN"), A("ODD"), -1.0, op.mult, 1.0, op.add)
-    ts(A("PMW"), A("PM"), float(2 * V), op.add)
-    ts(A("K1"), A("PM"), 1.0, op.add)
-    ts(A("EVM"), A("EVN"), float(MID), op.mult)
-    ts(A("SOFF"), A("ICF", 0, 16), 2.0, op.mult, 1.0, op.add)
-    fill(A("RB"), -float(2 ** 30))
+    ts(A("PMW"), A("PM"), -1.0, op.mult, NP - 1.0, op.add)
     ts(A("P15"), A("PM"), 15.0, op.is_equal)
-    ts(A("ID15"), A("ICF", 0, 128), A("PF"), op.is_equal, A("P15"), op.mult)
-    ts(A("LOFF"), A("ICF", 0, 8), 16.0, op.mult, 15.0, op.add)
-    ts(A("RP", 0, NP), A("PN"), -1.0, op.mult, 15.0, op.add)
-    cp(A("RE", 0, 16), A("OWN"))
+    ts(A("PC"), A("PG"), 17.0 / 16, op.mult, 16.0, op.add)
+    ts(A("N15"), A("PM"), 15.0, op.not_equal, 8192.0, op.mult)
+    ts(A("EVM"), A("EVN"), float(MID), op.mult)
+    fill(A("pL", 0, 48), -BIG)
+    tt(A("PC"), A("PC"), A("PM"), op.subtract)
     idn = A("ICF", 0, 128)
     ts(A("IDB"), idn, A("PF"), op.is_equal)
     ts(A("IDH"), idn, A("PF"), op.is_equal)
-    ts(A("NIDB"), idn, A("PF"), op.is_equal, -1.0, op.mult)
-    ts(A("IDHF"), idn, A("PF"), op.is_equal, 0.5, op.mult)
+    ts(A("N32"), idn, A("PF"), op.is_equal, -XS, op.mult)
+    ts(A("IDP"), idn, A("PF"), op.is_equal, 256.0 * 65536, op.mult)
+    ts(A("IDM"), idn, A("PF"), op.is_equal, -255.0 * 65536, op.mult)
     ts(A("EVD"), idn, A("PF"), op.is_equal, A("EVN"), op.mult)
-    ts(A("BDQ"), A("CGF"), A("PG"), op.is_equal, 65536.0, op.mult)
-    ts(A("BDB"), A("CGF"), A("PG"), op.is_equal, 8192.0, op.mult)
-    cg8 = A("CGF", 0, 128, 16)
-    ts(A("A8"), cg8, A("PG"), op.is_equal)
-    ts(A("BG8"), cg8, A("PG"), op.is_equal, -65536.0, op.mult)
-    ts(A("BM8"), cg8, A("PG"), op.is_equal, 131072.0, op.mult)
-    ts(A("C16"), A("CMF"), 0.0, op.mult, 15 - 1.0 / 64, op.add)
-    fill(A("CF", 0, 128), (30 + XO) * 2 ** 20)
-    fill(A("CF", 128, 256), -32768.0)
-    ts(A("CK"), A("CMF", 0, 128), 4096.0, op.mult)
-    ts(A("DIAG"), A("CMF", 0, 128), A("PM"), op.is_equal)
-    ts(A("MASK"), A("CMF"), A("PM"), op.not_equal, 8192.0, op.mult)
-    ts(A("RS"), A("CMF", 0, 128), 0.0, op.is_equal, float(2 ** 25), op.mult)
-    ts(A("RSH"), A("CMF"), 0.0, op.is_equal, -32768.0, op.mult)
-    ts(A("IDM"), idn, A("PF"), op.is_equal, -255.0, op.mult)
-    ts(A("IDP"), idn, A("PF"), op.is_equal, 256.0, op.mult)
+    ts(A("PERM"), A("ICF", 0, KW), A("PC"), op.is_equal)
+    ts(A("LOFF"), A("ICF", 0, 8), 17.0, op.mult, 16.0, op.add)
+    ts(A("RP", 0, NP), A("PN"), -1.0, op.mult, 15.0, op.add)
+    fill(A("C16"), (15 - 1.0 / 64) * XS)
+    for p, c in ((32, -15.0 * 2 ** 20), (64, 30.0 * 2 ** 20), (96, -32768.0)):
+        fill(A("INI", 0, 2 * KW) + lane(p), c)
+    fill(A("INI", 0, KW) + lane(0), -8.5 * 2048)
+    fill(A("INI", KW, 2 * KW) + lane(0), 8.0 * 2048)
+    fill(A("INI", 2 * KW, 3 * KW) + lane(32), -(256 + RO) * 65536.0)
+
+    def doubled(s):
+        cp(A("P16", s // 2, 1024, s), A("P16", 0, 1024, s))
+
+    for k in range(0, 16, 4):
+        ts(A("P16", k, 1024, 16), A("RP", 64, 128), XS, op.mult)
+    ts(A("BDQ"), A("CG17"), A("PG"), op.is_equal, 65536.0, op.mult)
+    doubled(4)
+    ts(A("BG"), A("CG17", 0, 2 * KW, 17), A("PG"), op.is_equal, -65536.0 / XS, op.mult)
+    ts(A("BM"), A("CG17", 0, 2 * KW, 17), A("PG"), op.is_equal, 131072.0 / XS, op.mult)
+    ts(A("A8"), A("CG17", 0, KW, 17), A("PG"), op.is_equal)
+    doubled(2)
+    cp(A("RE", 0, 16), A("OWN"))
+    ts(A("EQ"), A("CMF"), A("PM"), op.is_equal)
+    fill(A("INI", 2 * KW, 3 * KW, 17) + lane(0), float(2 ** 25))
+    ts(A("BDB"), A("CGF"), A("PG"), op.is_equal, -8192.0, op.mult)
     ts(A("TMP"), A("CMF", 0, 128), A("PM"), op.is_gt)
-    fill(A("TRM"), 0.0)
-    tt(A("LOW"), A("TMP"), A("BDB"), op.mult)
-    ts(A("TRM", 0, NP, 16), A("ICF", 0, NP, 16), A("PMW"), op.add)
     for a, b in parts[:3]:
-        cp(A("K", V + a, V + b), A("KI", a, b))
+        cp(A("K", F0 + a, F0 + b), A("KI", a, b))
 
     def jubilee_constants():
-        cp(A("WTF"), A("WTI"))
-        cp(A("WF"), A("WR"))
-        ts(A("YW"), A("CGF"), A("PG"), op.is_equal, A("K1"), op.mult)
-        ts(A("WH"), A("ICF", 0, 144), A("PG15"), op.is_equal, A("WTF"), op.mult)
-        ts(A("WBD"), A("CGF"), A("PG"), op.is_equal, A("WTF"), op.mult)
-        ts(A("WB"), A("WF"), -1.0, op.mult, 1.0, op.add)
-        fill(A("C160"), -160.0)
+        return [lambda: cp(A("WTF"), A("WTI")),
+                lambda: cp(A("WF"), A("WR")),
+                lambda: ts(A("K1"), A("PM"), 1.0, op.add),
+                lambda: ts(A("PG15"), A("PG"), 15.0, op.add),
+                lambda: fill(A("C160"), -160.0),
+                lambda: ts(A("YW"), A("CGF"), A("PG"), op.is_equal, A("K1"), op.mult),
+                lambda: ts(A("WH"), A("ICF", 0, 144), A("PG15"), op.is_equal, A("WTF"), op.mult),
+                lambda: ts(A("WBD"), A("CGF"), A("PG"), op.is_equal, A("WTF"), op.mult),
+                lambda: ts(A("WB"), A("WF"), -1.0, op.mult, 1.0, op.add),
+                lambda: ts(A("YWE"), A("YW"), A("EVN"), op.mult),
+                lambda: ts(A("YWO"), A("YW"), A("ODD"), op.mult)]
 
-    def ymm(k, p):
-        mm(A(p), A("YW"), A("K", V + 512 * k, V + 512 * k + 512), True, True)
+    YB = ("pX", "pP", "pK", "pY0", "pY1", "pP", "pD")
 
-    def ycopy(k, p):
-        if k < 4:
-            act(A("YK", V + 512 * k, V + 512 * k + 512), A(p), AF.Identity)
+    def yhalf(k):
+        act(A("M", 512 * k, 512 * k + 512), A("K", F0 + 512 * k, F0 + 512 * k + 512), AF.Identity, bias=-float(MID))
+
+    def ymm(k):
+        mm(A(YB[k]), A("YW"), A("M", 512 * k, 512 * k + 512), True, True)
+
+    def ycopy(k, q):
+        if q == "S":
+            act(A("YK", F0 + 512 * k, F0 + 512 * k + 512), A(YB[k]), AF.Identity, bias=136.0 * MID)
         else:
-            cp(A("YK", V + 512 * k, V + 512 * k + 512), A(p))
+            ts(A("YK", F0 + 512 * k, F0 + 512 * k + 512), A(YB[k]), 136.0 * MID, op.add)
 
-    def wide(x, f, bias):
-        for k in range(16):
-            act(A("P16", k, 1024, 16), x, f, bias=bias)
+    BANK = ("pD", "pQ", "pX", "pP")
+
+    def pieces(t):
+        return (0, 1, 2, 3) if t == TERM else (0, 2, 3)
+
+    def prepare(t):
+        for h in range(2):
+            p = ((0, 128 if h == 0 and t != TERM else 64),)
+            mm(A("pY%d" % h, 0, 2 * KW), A("ONE") + p, A("INI", 0, 2 * KW) + p, True, False)
+        for c in pieces(t):
+            mm(A(BANK[c], 0, 64 * R), A("IDH"), A("C16", 0, 64 * R), True, False)
 
     pend = []
+    spare = []
+    prepare(0)
     for t in range(NT):
         e = A("RE", 16 * t, 16 * t + 16)
         pb = "PO" if t % TERM else "RP"
@@ -303,231 +352,252 @@ def rank_program(g, core, T, topo):
             need("G", [e], [])
             send(nxt, A("RP", NP * t + NP, NP * t + 2 * NP), price, "aP%d" % (t + 1))
         if t == 0:
-            iota(A("H", V, 2 * V), [[1, V]])
+            iota(ROWS("EA", 0, 16 - NV, 0, NP - 16 * NV), [[0, 16 - NV], [0, NP - 16 * NV]], 1)
+            iota(A("TRM"), [[0, NP]], 16384)
+            iota(A("H", F0 + 1024, O0), [[1, V - 1024]], 1024)
+            need("Y", [A("WTI")], [])
+            dma("Y", T.H[:, F0:F0 + 1024], T.IOTA[:, 0:1024], [A("IOTA", 0, 1024)], [A("H", F0, F0 + 1024)])
         if t == 1:
             iota(A("KI", 0, V), [[1, V]])
             iota(A("KI", V, 4096), [[1, 4096 - V]])
-        pP = lambda a, b, s=1: A("pQ" if t == TERM and a >= 256 else "pP", a, b, s)
-        Kg, Xg = A("K", V, 2 * V), A("X", 0, V)
+            spare += jubilee_constants()
+        Kg, Xg = A("K", F0, O0), A("X", O0, W)
 
         def kin(a, b):
             cp(A("CU", a, b), IND(Kg if t else A("KI", 0, V), A("RE", 16 * t + a // 16, 16 * t + b // 16)))
 
         def wealth(a, b):
-            act(A("G", 16 * a, 16 * b), IND(Xg, A("CU", a, b)), AF.Identity, bias=-XO)
+            act(A("G", 16 * a, 16 * b), IND(Xg, A("CU", a, b)), AF.Identity)
+
+        def span(a, b):
+            return ((a % 128, (b - 1) % 128 + 1),)
 
         def ysum(k, a, b):
-            return A("pY%d" % (a // 128), k, 128, 16) + ((a % 128, (b - 1) % 128 + 1),)
+            return A("pY%d" % (a // 128), 16 - k, 2 * KW, 17) + span(a, b)
 
-        def gsum(a, b, ks=range(16)):
-            for k in ks:
-                mm(ysum(k, a, b), A("G", 16 * a + k, 16 * b, 16), A("BG8"), False, False)
+        def gsum(a, b):
+            for k in range(16):
+                mm(ysum(k, a, b), A("G", 16 * a + k, 16 * b, 16), A("BG"), False, False)
 
         def least(a, b, sums=None):
-            for s in range(8):
-                tt(A("M", 16 * a + s, 16 * b, 8), A("G", 16 * a + s, 16 * b, 8), pP(2 * a, 2 * b), op.max)
-                if b == NP:
-                    gsum(a, b, (s, s + 8))
+            n = 16 // R
+            for s in range(n):
+                tt(A("M", 16 * a + s, 16 * b, n), A("G", 16 * a + s, 16 * b, n), A(BANK[a // 64], R * (a % 64), R * ((b - 1) % 64 + 1)), op.max)
                 if sums:
-                    for k in (s, s + 8):
-                        mm(ysum(k, *sums), A("M", 16 * sums[0] + k, 16 * sums[1], 16), A("BM8"), False, k == 15)
+                    for k in range(s, 16, n):
+                        mm(ysum(k, *sums), A("M", 16 * sums[0] + k, 16 * sums[1], 16), A("BM"), False, k == 15)
 
-        big = 1.5 * 2.0 ** 39
-        keys = (A("pX", 256, 384), A("pK", 0, 128))
+        keys = (A("pY0", 2 * KW, 3 * KW), A("pK", 2 * KW, 3 * KW))
 
-        def least_key(h, key):
-            scan(A("SC", 128 * h, 128 * h + 128), A("RS"), key, float(2 ** 25), op.add, op.min)
+        def half(n, h):
+            return A(n, KW * h, KW * h + KW)
+
+        def ranks(x, rows):
+            mm(x, A("ONE") + ((0, rows),), A("INI", 2 * KW, 3 * KW) + ((0, rows),), True, False)
+
+        def persons(x, h):
+            mm(x, A("KC", 128 * h, 128 * h + 128), A("PERM"), False, True)
+
+        def scored(h):
+            mm(keys[h], A("IDP"), half("RR", 2 * h + 1), False, False)
+            mm(keys[h], A("IDM"), half("RR", 2 * h), False, False)
+            persons(keys[h], h)
+
+        def least_key(h):
+            scan(half("SC", h), keys[h], half("D1", h), 0.0, op.min, op.max)
 
         def to_list(h):
             lo, hi = 128 * h, 128 * h + 128
-            tt(A("EXP", lo, hi), IND(A("SC", lo, hi), A("LOFF")), A("DIAG", 0, 128), op.mult)
-            mm(A("pL", 16 * h, 16 * h + 16, 2), A("EXP", lo, hi), A("A8"), True, True)
+            tt(A("EXP", lo, hi), IND(half("SC", h), A("LOFF")), A("DIAG", 0, 128), op.mult)
+            mm(A("pL", 24 * h, 24 * h + 24, 3), A("EXP", lo, hi), A("A8"), True, True)
 
         def fillers(n):
-            for _ in range(min(n, len(pend))):
-                pend.pop(0)()
+            for _ in range(n):
+                if pend or spare:
+                    (pend or spare).pop(0)()
 
-        pend.insert(0, lambda e=e: ts(A("pL", 1, 32, 2), e, -1.0, op.mult, C0 - V, op.add))
         if t == 0:
-            pend.append(lambda: cp(A("RH", 0, 16), A("HI0")))
+            pend.append(lambda: tt(A("LOW"), A("TMP"), A("BDB"), op.mult))
+            pend.append(lambda: ts(A("TRM", 0, NP, 16), A("ICF", 0, NP, 16), -1.0, op.mult, A("PMW"), op.add))
+            pend.append(lambda: ts(A("RSH"), A("CMF"), 0.0, op.is_equal, -32768.0, op.mult))
+            pend.append(lambda: ts(A("RH", 0, 16), A("HI0"), float(O0), op.add))
         early = t != TERM
 
-        def prices(h):
-            n = 64 if early and h == 0 else 128
-            x = A(pb, NP * t + 128 * h, NP * t + 128 * h + n)
-            mm(pP(256 * h, 256 * h + 2 * n), A("IDH"), A("C16", 0, 2 * n), True, False)
-            for u in range(2):
-                mm(pP(256 * h + u, 256 * h + 2 * n, 2), A("NIDB"), x, False, u == 1)
-            mm(A("pY%d" % h, 0, 128) + ((0, n),), x, A("BDQ"), False, False)
+        def prices(c):
+            x = A(pb, NP * t + 64 * c, NP * t + 64 * c + 64)
+            for u in range(R):
+                mm(A(BANK[c], u, 64 * R, R), A("N32"), x, False, u == R - 1)
 
-        for h in range(2):
-            mm(A("pY%d" % h, 0, 128), A("IDB"), A("CY", 0, 128), True, False)
-            mm(A("pY%d" % h, 0, 128), A("IDB"), A("CY", 128, 256), False, False)
-            mm(keys[h], A("IDB"), A("CK"), True, False)
+        def qsum(a, b):
+            mm(A("pY%d" % (a // 128), 0, 2 * KW) + span(a, b), A(pb, NP * t + a, NP * t + b), A("BDQ"), False, False)
+
         if early:
-            for c in range(2):
-                mm(A("pY0", 0, 128) + ((64, 128),), A("IDB", 0, 64), A("CF", 128 * c, 128 * c + 128), False, False)
-        if t == 0:
-            wide(A(pb, 64, 128), AF.Identity, 0.0)
-        prices(0)
-        if early:
+            for c in pieces(t):
+                prices(c)
+            qsum(0, 64)
+            qsum(128, NP)
+        else:
+            prices(0)
             prices(1)
+            qsum(0, 128)
         kin(0, 64)
         wealth(0, 64)
-        kin(64, NP)
+        kin(64, 128)
+        kin(128, NP)
         if early:
             tt(A("G", 1024, 2048), IND(Xg, A("CU", 64, 128)), A("P16"), op.add)
             ts(A("KC"), A("CU"), -float(MID), op.add)
-            ts(A("M", 1024, 2048), A("G", 1024, 2048), 1.0 / 64 - 15 - XO, op.add, 0.0, op.max)
+            ts(A("M", 1024, 2048), A("G", 1024, 2048), (1.0 / 64 - 15) * XS, op.add, 0.0, op.max)
         else:
-            ts(A("G", 1024, 2048), IND(Xg, A("CU", 64, 128)), -XO, op.add)
+            cp(A("G", 1024, 2048), IND(Xg, A("CU", 64, 128)))
             ts(A("KC"), A("CU"), -float(MID), op.add)
         wealth(128, 192)
         gsum(0, 128)
         for h in range(2):
-            mm(keys[h], A("KC", 128 * h, 128 * h + 128), A("IDH"), False, h == 1)
+            ranks(half("pK", h), 32)
+            persons(half("pK", h), h)
         mm(A("pL", 256, 512), A("EVD"), A("KC"), True, True)
         if early:
             least(0, 64, (0, 128))
         else:
+            prices(2)
+            prices(3)
+            qsum(128, NP)
             least(0, 64)
             least(64, 128, (0, 128))
-            prices(1)
         wealth(192, LAST)
         wealth(LAST, NP)
-        gsum(128, 192)
         least(128, 192)
-        act(A("R0"), A("pY0", 0, 128), AF.Identity, bias=16.5 * 2048)
-        act(A("R1", 0, 128), A("pY0", 0, 128), AF.Identity, bias=big)
-        act(A("R1", 128, 256), A("R0"), AF.Identity, bias=big)
-        act(A("R2"), A("R1"), AF.Identity, bias=-big)
-        gsum(192, LAST)
-        least(192, LAST, (128, LAST))
-        least(LAST, NP, (LAST, NP))
-        mm(A("pY0", 128, 256), A("IDM"), A("R2", 0, 128), True, False)
-        mm(A("pY0", 128, 256), A("IDP"), A("R2", 128, 256), False, True)
-        act(A("U0"), A("pY0", 128, 256), AF.Relu, bias=-float(2 ** 24))
-        mm(keys[0], A("IDB"), A("U0"), False, True)
-        if last:
-            ymm(2, "pY0")
-        y1 = A("pY1", 0, 128)
-        fillers(1)
-        act(A("SCE"), A("pL", 256, 512), AF.Identity, bias=A("EVM"))
-        ts(A("UU", 0, 128), y1, big, op.add, -big, op.add)
-        fillers(1)
-        tt(A("pY1", 128, 256), y1, A("UU", 0, 128), op.is_gt)
-        fillers(1)
-        tt(A("UU", 128, 256), A("pY1", 128, 256), A("UU", 0, 128), op.mult)
-        fillers(1)
-        tt(A("KEY", 0, 128), keys[1], A("UU", 128, 256), op.add)
-        least_key(0, keys[0])
-        least_key(1, A("KEY", 0, 128))
-        to_list(0)
-        to_list(1)
-        act(A("T4"), price, AF.Identity, bias=163.375, scale=-0.25)
-        if last:
-            ycopy(1, "pD")
-            ycopy(0, "pQ")
-            ycopy(2, "pY0")
-            ymm(3, "pY1")
-        mm(A("pD", 0, NP), A("IDB"), A("MASK"), True, False)
+        act(A("RR", 0, 2 * KW), A("pY0", 0, 2 * KW), AF.Identity, bias=RO, scale=1.0 / 65536)
+        act(A("D1"), A("pK", 0, 2 * KW), AF.Identity)
         if t == 0:
+            act(A("DIAG"), A("EQ", 0, 128), AF.Identity)
+        gsum(128, LAST)
+        least(192, LAST)
+        gsum(LAST, NP)
+        ranks(keys[0], 64)
+        least(LAST, NP, (128, NP))
+        scored(0)
+        ranks(keys[1], 64)
+        act(A("SCE"), A("pL", 256, 512), AF.Identity, bias=A("EVM"))
+        act(A("T4"), price, AF.Identity, bias=163.375, scale=-0.25)
+        if t == 0:
+            act(A("MASK"), A("EQ"), AF.Identity, scale=A("N15"))
+            act(A("ID15"), A("IDB"), AF.Identity, scale=A("P15"))
+            act(A("IOTA", 1024, 2048), A("IOTA", 0, 1024), AF.Identity, bias=1024.0)
             act(A("IOTA", 2048, V), A("IOTA", 0, V - 2048), AF.Identity, bias=2048.0)
-            act(A("OFD"), A("MASK"), AF.Identity, bias=float(MID))
-            cp(A("K", V + parts[3][0], 2 * V), A("KI", *parts[3]))
-        fillers(99)
-        key = A("pL", 0, 32, 2)
+            cp(A("K", F0 + parts[3][0], O0), A("KI", *parts[3]))
+        else:
+            fillers(4)
+        ts(A("RR", 2 * KW, 4 * KW), A("pY1", 0, 2 * KW), 1.0 / 65536, op.mult, RO, op.add)
+        scored(1)
+        least_key(0)
+        ts(A("pL", 2, 48, 3), e, F0 - CK, op.add)
+        fillers(1)
+        to_list(0)
+        least_key(1)
+        fillers(2)
+        to_list(1)
+        mm(A("pD", 0, NP), A("IDB"), A("MASK"), True, False)
+        if last:
+            for k in range(4):
+                yhalf(k)
+            ymm(0)
+            ymm(1)
+        fillers(4)
+        key = A("pL", 0, 48, 3)
         big = 1.5 * 2.0 ** 35
         kf = A("TRM", 15, NP, 16)
-        ts(A("RB", 1, 32, 2), key, 131072.0, op.min, C19, op.add)
-        ts(A("R4"), key, big, op.add, -big, op.add)
-        scan(A("KL"), A("RB"), A("pL", 0, 32), 0.0, op.subtract, op.max)
-        tt(A("BP"), key, A("R4"), op.subtract)
-        ts(A("KU"), A("KL", 1, 32, 2), -1.0, op.mult, C0, op.add)
-        ts(kf, A("KL", 1, 32, 2), -1.0, op.mult, C0, op.add)
-        act(A("KRF"), IND(A("IOTA"), A("KU")), AF.Identity, bias=C0, scale=-1.0)
+        kl = A("KL", 2, 48, 3)
+        ts(A("RB", 1, 48, 3), key, big, op.add, -big, op.add)
+        ts(A("RB", 2, 48, 3), key, 131072.0, op.is_ge, -BIG, op.mult)
+        scan(A("KL"), A("RB"), A("pL", 0, 48), 0.0, op.subtract, op.max)
+        ts(A("KU"), kl, CK, op.add)
+        ts(A("BU"), A("KL", 1, 48, 3), -1.0, op.mult, float(MID), op.add)
+        act(A("KH", 0, 16), kl, AF.Identity, bias=CK)
+        act(kf, kl, AF.Identity, bias=CK)
+        act(A("KRF", 16 * NV, NP), IND(A("IOTA"), A("KU", NV, 16)), AF.Identity, bias=-CK)
         cp(A("KR"), IND(A("IOTA"), A("KU")))
-        ts(A("BU"), A("BP"), float(MID), op.add)
-        mm(A("pD", 15, NP, 16), A("ID15"), kf, False, False)
-        ea = 0
-        for j in range(NV, 15):
-            lo = 16 * j + 16
-            act(A("EA", ea, ea + NP - lo), A("KRF", lo, NP), AF.Abs, bias=A("KL", 2 * j + 1, 2 * j + 2), scale=-1.0)
-            ea += NP - lo
-        act(A("E", NP * NV, NP * NV + ea), A("EA", 0, ea), AF.Relu, bias=1.0, scale=-1.0)
+        tt(A("KH", 16, 32), kf, A("KH", 0, 16), op.subtract)
+        for u in range(2):
+            mm(A("pD", 15, NP, 16), A("ID15"), A("KH", 16 * u, 16 * u + 16), False, False)
+        for j in range(NV, 16):
+            act(ROWS("EA", j - NV, j - NV + 1, 0, NP - 16 * j), A("KRF", 16 * j, NP), AF.Abs, bias=A("KL", 3 * j + 2, 3 * j + 3), scale=-1.0)
+        for j0, j1 in SROWS:
+            act(ROWS("E", j0, j1, 0, NP - 16 * j0), ROWS("EA", j0 - NV, j1 - NV, 0, NP - 16 * j0), AF.Relu, bias=1.0, scale=-1.0)
+
+        def tail(j):
+            mm(A("pD", 16 * j + 16, NP), A("BDB"), ROWS("E", j, j + 1, 16, NP - 16 * j), False, False)
+
+        def heads(j0, j1, stop=False):
+            mm(A("pD", 16 * j0, 16 * j1), A("LOW"), ROWS("E", j0, j1, 0, 16), False, stop)
+
+        for j in range(NV):
+            ts(ROWS("E", j, j + 1, 0, NP - 16 * j), A("KR", 16 * j, NP), A("KH", j, j + 1), op.subtract, A("KH", 16 + j, 17 + j), op.is_equal)
+            tail(j)
+            if j == NS:
+                for i in range(NV, 15):
+                    tail(i)
+                heads(NV, 16)
+        heads(0, NV, True)
         act(A("BR"), IND(A("IOTA"), A("BU")), AF.Identity)
         act(A("XG"), IND(Xg, A("BU")), AF.Identity)
-        for j in range(NV):
-            lo = 16 * j + 16
-            x = A("E", NP * j + lo, NP * j + NP)
-            ts(x, A("KR", lo, NP), A("TRM", lo - 1, lo), op.is_equal)
-            mm(A("pD", lo, NP), A("BDB"), x, False, j == NV - 1)
-            if j == NS:
-                ea = NP * NV
-                for lo in range(16 * NV + 16, NP, 16):
-                    mm(A("pD", lo, NP), A("BDB"), A("E", ea, ea + NP - lo), False, False)
-                    ea += NP - lo
-            if j == ND:
-                tt(A("ED"), IND(A("KL"), A("SOFF")), A("KRF"), op.is_equal)
-                mm(A("pD", 0, NP), A("LOW"), A("ED"), False, False)
-        mm(A("pX", 0, NP), A("NIDB"), A("T4"), True, False)
+        if t == 0:
+            act(A("OFD"), A("EQ"), AF.Identity, bias=8192.0 + MID, scale=-8192.0)
+            act(A("IDHF"), A("IDB"), AF.Identity, scale=0.5)
+        if last:
+            ycopy(0, "V")
+        mm(A("pX", 0, NP), A("N32"), A("T4"), True, False)
         mm(A("pX", 0, NP), A("IDB"), A("XG"), False, True)
-        scan(A("FS"), A("TRM"), A("pD", 0, NP), 0.0, op.max, op.min)
+        fillers(len(pend) + 3)
+        scan(A("FS"), A("TRM"), A("pD", 0, NP), 16384.0, op.min, op.max)
         of2 = A("FS", 15, NP, 16)
         ofs = A("OFS", 16 * t, 16 * t + 16)
         cp(ofs, of2)
 
-        def redeemed(out, old, targets, between=None):
+        def redeemed(out, old, targets, scale, before, after):
             mm(A("pQ", 0, NP), A("IDB"), old, True, False)
-            act(A("SG"), IND(A("IOTA"), targets), AF.Sign, bias=0.5 - V)
+            act(A("SG"), IND(A("IOTA"), targets), AF.Sign, bias=O0 - 0.5, scale=-1.0)
+            before()
             mm(A("pQ", 0, NP), A("IDHF"), A("SG"), False, True)
-            if between:
-                between()
-            act(out, A("pQ", 0, NP), AF.Relu, bias=-0.5)
+            after()
+            act(out, A("pQ", 0, NP), AF.Relu, bias=-0.5 * scale, scale=scale)
 
         def newkin():
             act(A("SKF"), IND(Kg, A("BU")), AF.Identity, scale=A("ODD"))
 
-        def raised():
-            act(A("XV"), A("XR"), AF.Identity, bias=XO)
-
+        if not jub:
+            newkin()
+        act(A("XV"), A("pX", 0, NP), AF.Identity, bias=160.0 * XS)
         if not jub:
             send(nxt, A("RO", 16 * t + 16, 16 * t + 32), ofs, "aO%d" % (t + 1))
             arrives(prv, A("RO", 16 * t + 16, 16 * t + 32), "aO%d" % (t + 1))
             arrives(prv, A("RP", NP * t + NP, NP * t + 2 * NP), "aP%d" % (t + 1))
-            newkin()
-        act(A("XR"), A("pX", 0, NP), AF.Relu, bias=160.0 - XO)
-        if last:
-            ymm(4, "pP")
-        if jub:
-            redeemed(A("PN"), price, ofs, raised)
         else:
-            raised()
-        emit("S", [A("XV"), ofs], [A("X")], lambda: g.scalar.activation(ap(IND(A("X"), ofs)), ap(A("XV")), AF.Silu))
-        if jub:
+            redeemed(A("PN"), price, ofs, XS, lambda: None,
+                     lambda: emit("S", [A("XV"), ofs], [A("X")], lambda: g.scalar.activation(ap(IND(A("X"), ofs)), ap(A("XV")), AF.Silu)))
             newkin()
+        if not jub:
+            emit("S", [A("XV"), ofs], [A("X")], lambda: g.scalar.activation(ap(IND(A("X"), ofs)), ap(A("XV")), AF.Silu))
         if last:
-            ymm(5, "pY0")
-            ycopy(3, "pY1")
+            act(A("SKH"), A("SKF"), AF.Identity, bias=-float(MID))
+            for k in (4, 5, 6):
+                yhalf(k)
+            ymm(2)
+            ymm(3)
         ho = A("HO", 16 * t, 16 * t + 16)
-        pend.append(lambda: ts(A("RL"), of2, float(V), op.is_lt))
+        pend.append(lambda: ts(A("RL"), of2, float(O0), op.is_ge))
         pend.append(lambda hold=hold: tt(A("BH"), of2, hold, op.subtract))
         pend.append(lambda: tt(A("BH2"), A("RL"), A("BH"), op.mult))
-        if not jub:
-            def hsend(t=t, ho=ho, hold=hold):
-                tt(ho, A("BH2"), hold, op.add)
-                send(nxt, A("RH", 16 * t + 16, 16 * t + 32), ho, "aH%d" % (t + 1))
-            pend.append(hsend)
-        else:
+        if jub:
             pend.append(lambda: tt(A("HN"), A("BH2"), hold, op.add))
-            pend.append(lambda: ts(A("HG"), A("HN"), -float(MID), op.add))
+            pend.append(lambda: ts(A("HG"), A("HN"), -CK, op.add))
             pend.append(lambda: tt(A("WA"), A("HG"), A("WF"), op.mult))
-        nf = 2 if jub else 1
-        fillers(nf)
+        fillers(2)
         cp(IND(A("H"), ofs), A("BR"))
-        fillers(nf)
-        tt(A("EG"), IND(A("H", V, 2 * V), e), A("OFD"), op.subtract)
         fillers(1)
+        tt(A("EG"), IND(A("H", F0, O0), e), A("OFD"), op.subtract)
+        fillers(1 if jub else 0)
 
         def kpart():
             tt(IND(A("K"), ofs), A("SKF"), A("SCE"), op.add)
@@ -538,27 +608,36 @@ def rank_program(g, core, T, topo):
         if not jub:
             ts(en, el, float(MID), op.add)
             send(nxt, A("RE", 16 * t + 16, 16 * t + 32), en, "aE%d" % (t + 1))
+
+            def wide():
+                for k in range(0, 16, 4):
+                    act(A("P16", k, 1024, 16), A("pQ", 64, 128), AF.Relu, bias=-0.5 * XS, scale=XS)
+
             redeemed(A("PO", NP * t + NP, NP * t + 2 * NP), A("RP", NP * t + NP, NP * t + 2 * NP), A("RO", 16 * t + 16, 16 * t + 32),
-                     lambda: wide(A("pQ", 64, 128), AF.Relu, -0.5))
+                     1.0, lambda: prepare(t + 1), wide)
             kpart()
-            if t == 0:
-                jubilee_constants()
-            if t == NT - 2:
-                ymm(0, "pQ")
-                ymm(1, "pD")
+            doubled(4)
+            tt(ho, A("BH2"), hold, op.add)
+            send(nxt, A("RH", 16 * t + 16, 16 * t + 32), ho, "aH%d" % (t + 1))
+            doubled(2)
         else:
             fillers(1)
             tt(A("DW"), el, A("WB"), op.mult)
+            fillers(1)
             tt(A("EJ"), A("DW"), A("WA"), op.add)
             ts(en, A("EJ"), float(MID), op.add)
             if not last:
                 send(nxt, A("RE", 16 * t + 16, 16 * t + 32), en, "aE%d" % (t + 1))
-            mm(A("pL", 0, 16), A("WBD"), A("C160"), True, False)
+                prepare(t + 1)
+            else:
+                ycopy(1, "V")
+            sums = A("pL", 64, 80)
+            mm(sums, A("WBD"), A("C160"), True, False)
             halves = ((0, 128), (128, NP))
             for a, b in halves:
                 tt(A("PJ1", a, b), IND(Xg, (en[0], en[1] + a // 16, en[1] + b // 16, 1)), A("PN", a, b), op.subtract)
             for a, b in halves:
-                ts(A("PJ2", a, b), A("PJ1", a, b), 0.5, op.mult, 167.25 - XO / 2, op.add)
+                ts(A("PJ2", a, b), A("PJ1", a, b), 0.5 / XS, op.mult, 167.25, op.add)
             for h, (a, b) in enumerate(halves):
                 if not last:
                     ts(A("PO", a, b), A("PJ2", a, b), -1.0, op.mult, 175.0, op.add)
@@ -566,9 +645,14 @@ def rank_program(g, core, T, topo):
             if not last:
                 kpart()
             for j in range(16):
-                mm(A("pL", 0, 16), A("WH", 15 - j, 143 - j), A("PJ2", j, NP, 16), False, j == 15)
+                mm(sums, A("WH", 15 - j, 143 - j), A("PJ2", j, NP, 16), False, j == 15)
             if last:
-                cp(A("HI"), A("pL", 0, 16))
+                mm(A("pX", 0, NP), A("YWE"), A("KC"), True, False)
+                mm(A("pX", 0, NP), A("YWO"), A("SKH"), False, True)
+                for k in (4, 5, 6):
+                    ymm(k)
+                ycopy(2, "V")
+                cp(A("HI"), sums)
                 ts(A("HA"), A("HI"), 4095, op.bitwise_and)
                 cp(A("FO", 16, 32), A("HA"))
                 send(nxt, A("FIN"), A("FO"), "aF")
@@ -576,25 +660,23 @@ def rank_program(g, core, T, topo):
                 def hnew(t=t, ho=ho):
                     tt(ho, A("HA"), A("HG"), op.add)
                     send(nxt, A("RH", 16 * t + 16, 16 * t + 32), ho, "aH%d" % (t + 1))
-                cp(A("HI"), A("pL", 0, 16))
+                cp(A("HI"), sums)
                 pend.append(lambda: ts(A("HA"), A("HI"), 4095, op.bitwise_and))
-                pend.append(lambda: ts(A("HG"), A("HA"), float(V), op.is_ge, -float(V), op.mult))
+                pend.append(lambda: ts(A("HG"), A("HA"), float(V), op.is_lt, float(V), op.mult))
+                pend.append(lambda: ts(A("HG"), A("HG"), float(NP), op.add))
                 pend.append(hnew)
         if last:
             outs = []
-            outs.append(("Y", dma("Y", T.yh[:, :], T.H[0:128:16, V:2 * V], [A("H", V, 2 * V)], [])))
-            mm(A("pK", 0, NP), A("YW"), A("SCE"), True, False)
-            mm(A("pK", 0, NP), A("YW"), A("SKF"), False, True)
-            ymm(6, "pD")
+            outs.append(("Y", dma("Y", T.yh[:, :], T.H[0:128:16, F0:O0], [A("H", F0, O0)], [])))
             for k, (a, b) in enumerate(parts):
-                act(A("G", a, b), A("X", a, b), AF.Relu, bias=-XO - 2.0 ** -10)
+                act(A("G", a, b), A("X", O0 + a, O0 + b), AF.Relu, bias=-2.0 ** -10, scale=1.0 / XS)
                 outs.append(("Y", dma("Y", T.yx[:, a:b], T.G[:, a:b], [A("G", a, b)], [])))
                 if k == 1:
-                    act(A("YF"), A("pK", 0, NP), AF.Identity)
-            for k, p in ((4, "pP"), (5, "pY0"), (6, "pD")):
-                ycopy(k, p)
+                    act(A("YF"), A("pX", 0, NP), AF.Identity, bias=136.0 * MID)
+            for k in (3, 4, 5, 6):
+                ycopy(k, "V")
             cp(IND(A("YK"), ofs), A("YF"))
-            outs.append(("Y", dma("Y", T.yk[:, :], T.YK[0:128:16, V:2 * V], [A("YK", V, 2 * V)], [])))
+            outs.append(("Y", dma("Y", T.yk[:, :], T.YK[0:128:16, F0:O0], [A("YK", F0, O0)], [])))
             arrives(prv, A("FIN"), "aF")
             act(A("YO"), IND(A("IOTA"), A("FIN", 0, 16)), AF.Identity)
             cp(A("YT"), IND(A("KI"), A("FIN", 16, 32)))

@@ -2,48 +2,53 @@ import math
 from concourse.mybir import AluOpType, ActivationFunctionType
 
 V, NP, NT, TERM = 3584, 256, 8, 4
-F0, O0 = NP, NP + V
+F0, SP = V, 2 * V
 W = NP + 2 * V
 MID = V // 2
-NV = 10
-SROWS = ((10, 13), (13, 16))
-NS = 7
-LAST = 224
+V0 = 192
+LAST = 96
+NV = 12
+KV, KS = 1152, 896
 XS = 32.0
 R = 8
 KW = 136
 RO = 1536.0
-CK = float(O0 + MID)
 BIG = float(2 ** 30)
+FAR = 16384.0
+OFF = (15 - 1.0 / 64) * XS
+NB = V // 128
+NF = 19
+PW = 16 * (NP - V0)
 
 _S = {}
 F, B, I, U, Hf = "float32", "bfloat16", "int32", "uint16", "float16"
 for _n, _w, _d in [
-        ("K", W, F), ("KI", 4096, I), ("X", W, F), ("H", W, F), ("YK", W, F), ("IOTA", W, F),
+        ("K", W, F), ("KI", 4096, I), ("X", W, F), ("H", W, F), ("IOTA", W, F),
         ("OWN", 16, I), ("WL", 16, I), ("WR", 16, I), ("HI0", 16, I), ("WTI", 1, I),
         ("RE", 16 * NT, U), ("RP", NP * NT, B), ("RH", 16 * NT, F), ("FIN", 32, U),
         ("EN", 16 * NT, U), ("PO", NP * NT, B), ("HO", 16 * NT, F), ("FO", 32, U),
-        ("CU", NP, U), ("KC", NP, Hf), ("G", 16 * NP, B), ("M", 16 * NP, Hf),
+        ("CU", NP, U), ("KC", NP, Hf), ("G", 16 * NP, Hf), ("XB", V, B), ("M", 16 * NP, Hf),
         ("RR", 4 * KW, Hf), ("D1", 2 * KW, F), ("SC", 2 * KW, F), ("EXP", NP, F),
-        ("OFD", NP, F), ("RSH", NP, Hf), ("WA", 16, F), ("WB", 16, F),
-        ("RB", 48, F), ("KL", 48, F), ("ID15", 128, B), ("KH", 32, B),
+        ("OFD", NP, F), ("RSH", NP, Hf), ("JA", 48, F), ("JB", 48, F), ("JC", 48, F), ("CAP", NP, F), ("RSJ", NP, F), ("WU", 16, U),
+        ("RB", 48, F), ("KL", 48, F), ("ID15", 128, F), ("KH", 32, B),
         ("KU", 16, U), ("BU", 16, U), ("OFS", 16 * NT, U), ("RO", 16 * NT, U),
-        ("KR", NP, U), ("KRF", NP, F), ("FS", NP, F),
+        ("KR", NP, U), ("FS", NP, F),
         ("BR", NP, F), ("EG", NP, Hf), ("ES", NP, Hf), ("T4", NP, B), ("XG", NP, B), ("XV", NP, F),
         ("SKF", NP, F), ("SCE", NP, F), ("SG", NP, B), ("PN", NP, B),
-        ("RL", 16, F), ("BH", 16, F), ("BH2", 16, F), ("HN", 16, F), ("DW", 16, F), ("EJ", 16, F), ("WF", 16, F),
-        ("PJ1", NP, B), ("PJ2", NP, B), ("HI", 16, I), ("HA", 16, I), ("HG", 16, F), ("YF", NP, F), ("YO", NP, F), ("YT", NP, F),
+        ("RL", 16, F), ("BH", 16, F), ("BH2", 16, F),
+        ("PJ1", NP, B), ("PJ2", NP, B), ("HI", 16, I), ("HA", 16, I), ("HG", 16, F), ("YO", NP, F), ("YT", NP, F),
+        ("YA", 8 * NB, F), ("YB", NP, F),
         ("IP", 1, I), ("ICF", NP, B), ("CMF", NP, B), ("CGF", 128, B), ("CG17", 2 * KW, B), ("TMP", 128, B), ("EQ", NP, B),
         ("PMI", 1, I), ("ODI", 1, I), ("COL", 16, F),
-        ("YW", 128, B), ("YWE", 128, B), ("YWO", 128, B), ("SKH", NP, Hf), ("WH", 144, B), ("A8", 8, F), ("BG", 16, B), ("BM", 16, B),
-        ("INI", 3 * KW, B), ("ONE", 128, B), ("PERM", KW, B), ("IDP", 128, B), ("IDM", 128, B),
-        ("P16", 1024, B), ("IDB", 128, B), ("N32", 128, B), ("IDHF", 128, B), ("IDH", 128, Hf), ("EVD", 128, Hf),
-        ("BDQ", 2 * KW, B), ("BDB", 128, B), ("LOW", 128, B), ("C16", 512, Hf), ("C160", 16, B), ("WBD", 128, B), ("MASK", NP, B),
+        ("YW", 8, B), ("YF", 8, F), ("YC", 8 * NB, B), ("IDF", 128, F), ("WH", 144, B), ("A8", 8, F), ("BG", 16, B), ("BM", 16, B),
+        ("INI", 4 * KW, B), ("ONE", 128, B), ("PERM", KW, B), ("IDP", 128, B), ("IDM", 128, B),
+        ("P16", PW, B), ("IDB", 128, B), ("N32", 128, B), ("IDHF", 128, B),
+        ("BDQ", 2 * KW, B), ("BDB", 128, B), ("LOW", 128, B), ("C160", 16, B), ("WBD", 128, B), ("MASK", NP, B),
         ("DIAG", 128, F), ("TRM", NP, F), ("LOFF", 8, U)]:
     _S[_n] = ("sbuf", [128, _w], _d)
 _S["E"] = ("sbuf", [128, 16, NP], B)
 _S["EA"] = ("sbuf", [128, 16 - NV, NP - 16 * NV], F)
-COLS = ["PF", "PM", "PG", "PG15", "ODD", "EVN", "EVM", "K1", "WTF", "PMW", "P15", "PC", "N15"]
+COLS = ["PF", "PM", "PG", "PG15", "ODD", "EVN", "EVM", "K1", "WTF", "PMS", "P15", "PC"]
 for _n in ["pP", "pY0", "pY1", "pK", "pL", "pD", "pX", "pQ"]:
     _S[_n] = ("psum", [128, 512], F)
 SCRATCH = _S
@@ -205,15 +210,15 @@ def rank_program(g, core, T, topo):
     def arrives(src, x, sem):
         external(x, sem, len(topo.engines(src, core)[:8]))
 
-    parts = ((0, 1024), (1024, 2048), (2048, 3072), (3072, V))
+    parts = ((0, KV), (KV, 2304), (2304, V))
     xparts = ((0, MID), (MID, V))
-    for q, n, src in (("S", "PN", T.price), ("S", "OWN", T.own)):
+    for q, n, src in (("S", "PN", T.price), ("S", "WL", T.wall), ("S", "OWN", T.own)):
         dma(q, T[n][:, :], src[:, :], [], [A(n)])
     for a, b in xparts:
-        dma("Y", T.G[:, a:b], T.x[:, a:b], [], [A("G", a, b)])
+        dma("Y", T.XB[:, a:b], T.x[:, a:b], [], [A("XB", a, b)])
     for a, b in parts:
         dma("Y", T.KI[:, a:b], T.kin[:, a:b], [], [A("KI", a, b)])
-    for q, n, src in (("Y", "WL", T.wall), ("Y", "HI0", T.hold), ("Y", "WTI", T.wt)):
+    for q, n, src in (("Y", "HI0", T.hold), ("Y", "WTI", T.wt)):
         dma(q, T[n][:, :], src[:, :], [], [A(n)])
 
     def iota(x, pattern, base=0, per=0):
@@ -230,55 +235,56 @@ def rank_program(g, core, T, topo):
     iota(A("CG17"), [[0, 2], [16, 8], [0, 17]])
     iota(A("CMF"), [[0, 16], [1, 16]])
     iota(A("CGF"), [[16, 8], [0, 16]])
-    iota(A("INI", 2 * KW, 3 * KW) + lane(0), [[0, 8], [-4096, 17]], 65536)
-    iota(A("IOTA", V, W), [[1, W - V]], V)
-    send(prv, A("WR"), A("WL"), "aW")
-    arrives(nxt, A("WR"), "aW")
+    iota(A("INI", 2 * KW, 4 * KW) + lane(0), [[0, 16], [-4096, 17]], 65536)
+    act(A("TRM"), A("ICF"), AF.Silu, scale=0.0)
     act(A("IOTA", 0, NP), A("ICF"), AF.Identity)
-    n = NP
-    while n < 1024:
-        act(A("IOTA", n, 2 * n), A("IOTA", 0, n), AF.Identity, bias=float(n))
-        n *= 2
+    iota(A("IOTA", MID, V), [[1, MID]], MID)
+    iota(A("IOTA", V, W), [[1, W - V]], V)
     for a, b in xparts:
-        act(A("X", O0 + a, O0 + b), A("G", a, b), AF.Silu, scale=XS)
+        act(A("X", a, b), A("XB", a, b), AF.Identity, scale=XS)
+    for n in (NP, 2 * NP):
+        act(A("IOTA", n, 2 * n), A("IOTA", 0, n), AF.Identity, bias=float(n))
+
+    def first_heirs(a, b):
+        dma("Y", T.H[:, F0 + a:F0 + b], T.IOTA[:, a:b], [A("IOTA", a, b)], [A("H", F0 + a, F0 + b)])
+
+    need("Y", [A("WTI")], [])
+    first_heirs(MID, V)
+    first_heirs(0, 1024)
     ts(A("PMI"), A("IP"), 15, op.bitwise_and)
     ts(A("ODI"), A("IP"), 1, op.bitwise_and)
     fill(A("ONE"), 1.0)
     cp(A("PM"), A("PMI"))
     cp(A("ODD"), A("ODI"))
-    fill(A("ONE", 0, 64) + ((64, 128),), 0.0)
-    fill(A("RB"), -BIG)
+    fill(A("ONE", 0, V0 - 128) + ((64, 128),), 0.0)
+    fill(A("RB"), BIG)
     tt(A("PG"), A("PF"), A("PM"), op.subtract)
     ts(A("EVN"), A("ODD"), -1.0, op.mult, 1.0, op.add)
-    ts(A("PMW"), A("PM"), -1.0, op.mult, NP - 1.0, op.add)
+    ts(A("PMS"), A("PM"), float(SP), op.add)
     ts(A("P15"), A("PM"), 15.0, op.is_equal)
     ts(A("PC"), A("PG"), 17.0 / 16, op.mult, 16.0, op.add)
-    ts(A("N15"), A("PM"), 15.0, op.not_equal, 8192.0, op.mult)
     ts(A("EVM"), A("EVN"), float(MID), op.mult)
-    fill(A("pL", 0, 48), -BIG)
+    fill(A("pL", 0, 48), BIG)
     tt(A("PC"), A("PC"), A("PM"), op.subtract)
+    ts(A("RP", 0, NP), A("PN"), -1.0, op.mult, 15.0, op.add)
+    send(nxt, A("RP", NP, 2 * NP), A("RP", 0, NP), "aP1")
     idn = A("ICF", 0, 128)
     ts(A("IDB"), idn, A("PF"), op.is_equal)
-    ts(A("IDH"), idn, A("PF"), op.is_equal)
     ts(A("N32"), idn, A("PF"), op.is_equal, -XS, op.mult)
     ts(A("IDP"), idn, A("PF"), op.is_equal, 256.0 * 65536, op.mult)
     ts(A("IDM"), idn, A("PF"), op.is_equal, -255.0 * 65536, op.mult)
-    ts(A("EVD"), idn, A("PF"), op.is_equal, A("EVN"), op.mult)
     ts(A("PERM"), A("ICF", 0, KW), A("PC"), op.is_equal)
     ts(A("LOFF"), A("ICF", 0, 8), 17.0, op.mult, 16.0, op.add)
-    ts(A("RP", 0, NP), A("PN"), -1.0, op.mult, 15.0, op.add)
-    fill(A("C16"), (15 - 1.0 / 64) * XS)
-    for p, c in ((32, -15.0 * 2 ** 20), (64, 30.0 * 2 ** 20), (96, -32768.0)):
+    for p, c in ((64, 15.0 * 2 ** 20), (96, -16384.0)):
         fill(A("INI", 0, 2 * KW) + lane(p), c)
-    fill(A("INI", 0, KW) + lane(0), -8.5 * 2048)
-    fill(A("INI", KW, 2 * KW) + lane(0), 8.0 * 2048)
+    fill(A("INI", 0, KW) + lane(0), -16.5 * 2048)
     fill(A("INI", 2 * KW, 3 * KW) + lane(32), -(256 + RO) * 65536.0)
 
     def doubled(s):
-        cp(A("P16", s // 2, 1024, s), A("P16", 0, 1024, s))
+        cp(A("P16", s // 2, PW, s), A("P16", 0, PW, s))
 
     for k in range(0, 16, 4):
-        ts(A("P16", k, 1024, 16), A("RP", 64, 128), XS, op.mult)
+        ts(A("P16", k, PW, 16), A("RP", V0, NP), XS, op.mult)
     ts(A("BDQ"), A("CG17"), A("PG"), op.is_equal, 65536.0, op.mult)
     doubled(4)
     ts(A("BG"), A("CG17", 0, 2 * KW, 17), A("PG"), op.is_equal, -65536.0 / XS, op.mult)
@@ -287,53 +293,52 @@ def rank_program(g, core, T, topo):
     doubled(2)
     cp(A("RE", 0, 16), A("OWN"))
     ts(A("EQ"), A("CMF"), A("PM"), op.is_equal)
-    fill(A("INI", 2 * KW, 3 * KW, 17) + lane(0), float(2 ** 25))
-    ts(A("BDB"), A("CGF"), A("PG"), op.is_equal, -8192.0, op.mult)
+    fill(A("INI", 2 * KW, 4 * KW, 17) + lane(0), float(2 ** 25))
+    ts(A("BDB"), A("CGF"), A("PG"), op.is_equal, FAR, op.mult)
     ts(A("TMP"), A("CMF", 0, 128), A("PM"), op.is_gt)
-    for a, b in parts[:3]:
-        cp(A("K", F0 + a, F0 + b), A("KI", a, b))
+    ts(A("PG15"), A("PG"), 15.0, op.add)
+    ts(A("WBD"), A("CGF"), A("PG"), op.is_equal)
+    ts(A("WH"), A("ICF", 0, 144), A("PG15"), op.is_equal)
+    cp(A("DIAG"), A("EQ", 0, 128))
+    ts(A("MASK"), A("EQ"), -FAR, op.mult, FAR, op.add)
+    tt(A("LOW"), A("TMP"), A("BDB"), op.mult)
+    ts(A("TRM", 0, NP, 16), A("ICF", 0, NP, 16), A("PMS"), op.add)
+    ts(A("ID15"), idn, A("PF"), op.is_equal, A("P15"), op.mult)
+    ts(A("RSH"), A("CMF"), 0.0, op.is_equal, -32768.0, op.mult)
+    cp(A("K", F0, F0 + KV), A("KI", 0, KV))
 
     def jubilee_constants():
-        return [lambda: cp(A("WTF"), A("WTI")),
-                lambda: cp(A("WF"), A("WR")),
-                lambda: ts(A("K1"), A("PM"), 1.0, op.add),
-                lambda: ts(A("PG15"), A("PG"), 15.0, op.add),
-                lambda: fill(A("C160"), -160.0),
-                lambda: ts(A("YW"), A("CGF"), A("PG"), op.is_equal, A("K1"), op.mult),
-                lambda: ts(A("WH"), A("ICF", 0, 144), A("PG15"), op.is_equal, A("WTF"), op.mult),
-                lambda: ts(A("WBD"), A("CGF"), A("PG"), op.is_equal, A("WTF"), op.mult),
-                lambda: ts(A("WB"), A("WF"), -1.0, op.mult, 1.0, op.add),
-                lambda: ts(A("YWE"), A("YW"), A("EVN"), op.mult),
-                lambda: ts(A("YWO"), A("YW"), A("ODD"), op.mult)]
+        ID = AF.Identity
+        return [lambda: act(A("WTF"), A("WTI"), ID),
+                lambda: act(A("JA"), A("RB"), ID, scale=0.0),
+                lambda: act(A("JB"), A("RB"), ID, scale=0.0),
+                lambda: act(A("RSJ"), A("RSH"), ID),
+                lambda: act(A("K1"), A("PM"), ID, bias=1.0),
+                lambda: act(A("C160"), A("ICF", 0, 16), ID, bias=-160.0, scale=0.0),
+                lambda: act(A("JC", 0, 2), A("ICF", 0, 2), ID, bias=4096.0, scale=-4096.0),
+                lambda: act(A("IDF"), A("IDB"), ID),
+                lambda: act(A("WU"), A("WR"), ID),
+                lambda: act(A("JA", 2, 48, 3), A("WR"), ID),
+                lambda: act(A("YW"), A("A8"), ID, scale=A("K1")),
+                lambda: act(A("YF"), A("A8"), ID, scale=A("K1")),
+                lambda: act(A("WH"), A("WH"), ID, scale=A("WTF")),
+                lambda: act(A("WBD"), A("WBD"), ID, scale=A("WTF")),
+                lambda: longer.append(lambda: tt(A("CAP"), IND(A("JC", 0, 2), A("WU")), A("EQ"), op.mult))]
 
-    YB = ("pX", "pP", "pK", "pY0", "pY1", "pP", "pD")
+    BANK = ("pX", "pP", "pD", "pQ")
 
-    def yhalf(k):
-        act(A("M", 512 * k, 512 * k + 512), A("K", F0 + 512 * k, F0 + 512 * k + 512), AF.Identity, bias=-float(MID))
-
-    def ymm(k):
-        mm(A(YB[k]), A("YW"), A("M", 512 * k, 512 * k + 512), True, True)
-
-    def ycopy(k, q):
-        if q == "S":
-            act(A("YK", F0 + 512 * k, F0 + 512 * k + 512), A(YB[k]), AF.Identity, bias=136.0 * MID)
-        else:
-            ts(A("YK", F0 + 512 * k, F0 + 512 * k + 512), A(YB[k]), 136.0 * MID, op.add)
-
-    BANK = ("pD", "pQ", "pX", "pP")
-
-    def pieces(t):
-        return (0, 1, 2, 3) if t == TERM else (0, 2, 3)
+    def ranks(x, rows):
+        mm(x, A("ONE") + ((0, rows),), A("INI", 2 * KW, 2 * KW + x[2] - x[1]) + ((0, rows),), True, False)
 
     def prepare(t):
-        for h in range(2):
-            p = ((0, 128 if h == 0 and t != TERM else 64),)
+        for h in (1, 0):
+            p = ((0, 128 if h == 1 and t != TERM else 64),)
             mm(A("pY%d" % h, 0, 2 * KW), A("ONE") + p, A("INI", 0, 2 * KW) + p, True, False)
-        for c in pieces(t):
-            mm(A(BANK[c], 0, 64 * R), A("IDH"), A("C16", 0, 64 * R), True, False)
+        ranks(A("pK", 0, 2 * KW), 32)
 
     pend = []
-    spare = []
+    spare = [lambda: act(A("IOTA", 1024, MID), A("IOTA", 0, MID - 1024), AF.Identity, bias=1024.0), lambda: first_heirs(1024, MID)]
+    longer = []
     prepare(0)
     for t in range(NT):
         e = A("RE", 16 * t, 16 * t + 16)
@@ -348,26 +353,24 @@ def rank_program(g, core, T, topo):
                     arrives(prv, A(pb, NP * t + 128 * h, NP * t + 128 * h + 128), "a%s%d" % ("PO"[h], t))
             arrives(prv, e, "aE%d" % t)
             arrives(prv, hold, "aH%d" % t)
-        if not jub:
+        if t and not jub:
             need("G", [e], [])
             send(nxt, A("RP", NP * t + NP, NP * t + 2 * NP), price, "aP%d" % (t + 1))
-        if t == 0:
-            iota(ROWS("EA", 0, 16 - NV, 0, NP - 16 * NV), [[0, 16 - NV], [0, NP - 16 * NV]], 1)
-            iota(A("TRM"), [[0, NP]], 16384)
-            iota(A("H", F0 + 1024, O0), [[1, V - 1024]], 1024)
-            need("Y", [A("WTI")], [])
-            dma("Y", T.H[:, F0:F0 + 1024], T.IOTA[:, 0:1024], [A("IOTA", 0, 1024)], [A("H", F0, F0 + 1024)])
         if t == 1:
+            send(prv, A("WR"), A("WL"), "aW")
+            arrives(nxt, A("WR"), "aW")
+            iota(A("YC"), [[0, 8], [1, NB]])
             iota(A("KI", 0, V), [[1, V]])
             iota(A("KI", V, 4096), [[1, 4096 - V]])
+            longer.append(lambda: ts(A("YC"), A("YC"), float(NF), op.is_ge, 136.0 * MID, op.mult))
             spare += jubilee_constants()
-        Kg, Xg = A("K", F0, O0), A("X", O0, W)
+        Kg, Xg = A("K", F0, SP), A("X", 0, V)
 
         def kin(a, b):
             cp(A("CU", a, b), IND(Kg if t else A("KI", 0, V), A("RE", 16 * t + a // 16, 16 * t + b // 16)))
 
         def wealth(a, b):
-            act(A("G", 16 * a, 16 * b), IND(Xg, A("CU", a, b)), AF.Identity)
+            act(A("G", 16 * a, 16 * b), IND(Xg, A("CU", a, b)), AF.Identity, bias=-OFF)
 
         def span(a, b):
             return ((a % 128, (b - 1) % 128 + 1),)
@@ -379,24 +382,23 @@ def rank_program(g, core, T, topo):
             for k in range(16):
                 mm(ysum(k, a, b), A("G", 16 * a + k, 16 * b, 16), A("BG"), False, False)
 
-        def least(a, b, sums=None):
+        def least(a, b, sums=None, between=None):
             n = 16 // R
             for s in range(n):
                 tt(A("M", 16 * a + s, 16 * b, n), A("G", 16 * a + s, 16 * b, n), A(BANK[a // 64], R * (a % 64), R * ((b - 1) % 64 + 1)), op.max)
+                if between and s:
+                    between()
                 if sums:
                     for k in range(s, 16, n):
                         mm(ysum(k, *sums), A("M", 16 * sums[0] + k, 16 * sums[1], 16), A("BM"), False, k == 15)
 
-        keys = (A("pY0", 2 * KW, 3 * KW), A("pK", 2 * KW, 3 * KW))
+        keys = (A("pK", 2 * KW, 3 * KW), A("pL", 2 * KW, 3 * KW))
 
         def half(n, h):
             return A(n, KW * h, KW * h + KW)
 
-        def ranks(x, rows):
-            mm(x, A("ONE") + ((0, rows),), A("INI", 2 * KW, 3 * KW) + ((0, rows),), True, False)
-
-        def persons(x, h):
-            mm(x, A("KC", 128 * h, 128 * h + 128), A("PERM"), False, True)
+        def persons(x, h, stop=True):
+            mm(x, A("KC", 128 * h, 128 * h + 128), A("PERM"), False, stop)
 
         def scored(h):
             mm(keys[h], A("IDP"), half("RR", 2 * h + 1), False, False)
@@ -413,118 +415,113 @@ def rank_program(g, core, T, topo):
 
         def fillers(n):
             for _ in range(n):
-                if pend or spare:
-                    (pend or spare).pop(0)()
+                if pend:
+                    pend.pop(0)()
 
         if t == 0:
-            pend.append(lambda: tt(A("LOW"), A("TMP"), A("BDB"), op.mult))
-            pend.append(lambda: ts(A("TRM", 0, NP, 16), A("ICF", 0, NP, 16), -1.0, op.mult, A("PMW"), op.add))
-            pend.append(lambda: ts(A("RSH"), A("CMF"), 0.0, op.is_equal, -32768.0, op.mult))
-            pend.append(lambda: ts(A("RH", 0, 16), A("HI0"), float(O0), op.add))
+            pend.append(lambda: fill(ROWS("EA", 0, 16 - NV, 0, NP - 16 * NV), 1.0))
+            pend.append(lambda: cp(A("RH", 0, 16), A("HI0")))
+            for a in range(KV, V - KS, 128):
+                pend.append(lambda a=a: cp(A("K", F0 + a, F0 + a + 128), A("KI", a, a + 128)))
         early = t != TERM
 
         def prices(c):
             x = A(pb, NP * t + 64 * c, NP * t + 64 * c + 64)
             for u in range(R):
-                mm(A(BANK[c], u, 64 * R, R), A("N32"), x, False, u == R - 1)
+                mm(A(BANK[c], u, 64 * R, R), A("N32"), x, True, True)
 
         def qsum(a, b):
             mm(A("pY%d" % (a // 128), 0, 2 * KW) + span(a, b), A(pb, NP * t + a, NP * t + b), A("BDQ"), False, False)
 
+        def rounded(h):
+            act(A("RR", 2 * KW * h, 2 * KW * h + 2 * KW), A("pY%d" % h, 0, 2 * KW), AF.Identity, bias=RO, scale=1.0 / 65536)
+
         if early:
-            for c in pieces(t):
+            for c in (2, 0, 1):
                 prices(c)
-            qsum(0, 64)
-            qsum(128, NP)
-        else:
-            prices(0)
-            prices(1)
+            qsum(128, V0)
             qsum(0, 128)
-        kin(0, 64)
-        wealth(0, 64)
-        kin(64, 128)
-        kin(128, NP)
-        if early:
-            tt(A("G", 1024, 2048), IND(Xg, A("CU", 64, 128)), A("P16"), op.add)
-            ts(A("KC"), A("CU"), -float(MID), op.add)
-            ts(A("M", 1024, 2048), A("G", 1024, 2048), (1.0 / 64 - 15) * XS, op.add, 0.0, op.max)
-        else:
-            cp(A("G", 1024, 2048), IND(Xg, A("CU", 64, 128)))
-            ts(A("KC"), A("CU"), -float(MID), op.add)
-        wealth(128, 192)
-        gsum(0, 128)
-        for h in range(2):
-            ranks(half("pK", h), 32)
-            persons(half("pK", h), h)
-        mm(A("pL", 256, 512), A("EVD"), A("KC"), True, True)
-        if early:
-            least(0, 64, (0, 128))
         else:
             prices(2)
             prices(3)
             qsum(128, NP)
-            least(0, 64)
-            least(64, 128, (0, 128))
-        wealth(192, LAST)
-        wealth(LAST, NP)
-        least(128, 192)
-        act(A("RR", 0, 2 * KW), A("pY0", 0, 2 * KW), AF.Identity, bias=RO, scale=1.0 / 65536)
-        act(A("D1"), A("pK", 0, 2 * KW), AF.Identity)
-        if t == 0:
-            act(A("DIAG"), A("EQ", 0, 128), AF.Identity)
-        gsum(128, LAST)
-        least(192, LAST)
-        gsum(LAST, NP)
-        ranks(keys[0], 64)
-        least(LAST, NP, (128, NP))
-        scored(0)
         ranks(keys[1], 64)
-        act(A("SCE"), A("pL", 256, 512), AF.Identity, bias=A("EVM"))
-        act(A("T4"), price, AF.Identity, bias=163.375, scale=-0.25)
-        if t == 0:
-            act(A("MASK"), A("EQ"), AF.Identity, scale=A("N15"))
-            act(A("ID15"), A("IDB"), AF.Identity, scale=A("P15"))
-            act(A("IOTA", 1024, 2048), A("IOTA", 0, 1024), AF.Identity, bias=1024.0)
-            act(A("IOTA", 2048, V), A("IOTA", 0, V - 2048), AF.Identity, bias=2048.0)
-            cp(A("K", F0 + parts[3][0], O0), A("KI", *parts[3]))
+        kin(128, V0)
+        wealth(128, V0)
+        kin(V0, NP)
+        kin(0, 128)
+        if early:
+            tt(A("G", 16 * V0, 16 * NP), IND(Xg, A("CU", V0, NP)), A("P16"), op.add)
+            ts(A("KC"), A("CU"), -float(MID), op.add)
+            ts(A("M", 16 * V0, 16 * NP), A("G", 16 * V0, 16 * NP), -OFF, op.add, 0.0, op.max)
         else:
-            fillers(4)
-        ts(A("RR", 2 * KW, 4 * KW), A("pY1", 0, 2 * KW), 1.0 / 65536, op.mult, RO, op.add)
-        scored(1)
-        least_key(0)
-        ts(A("pL", 2, 48, 3), e, F0 - CK, op.add)
-        fillers(1)
-        to_list(0)
-        least_key(1)
-        fillers(2)
-        to_list(1)
+            ts(A("G", 16 * V0, 16 * NP), IND(Xg, A("CU", V0, NP)), -OFF, op.add)
+            ts(A("KC"), A("CU"), -float(MID), op.add)
+        wealth(0, 64)
+        gsum(128, NP)
+        for h in (1, 0):
+            persons(half("pK", h), h, h == 0)
+        if early:
+            least(128, V0, (128, NP))
+        else:
+            prices(0)
+            prices(1)
+            qsum(0, 128)
+            least(128, 192)
+            least(192, NP, (128, NP))
         mm(A("pD", 0, NP), A("IDB"), A("MASK"), True, False)
-        if last:
-            for k in range(4):
-                yhalf(k)
-            ymm(0)
-            ymm(1)
-        fillers(4)
-        key = A("pL", 0, 48, 3)
+        wealth(64, LAST)
+        wealth(LAST, 128)
+        least(0, 64)
+        rounded(1)
+        act(A("D1"), A("pK", 0, 2 * KW), AF.Identity)
+        gsum(0, LAST)
+        least(64, LAST)
+        gsum(LAST, 128)
+        scored(1)
+        least(LAST, 128, (0, 128))
+        ranks(keys[0], 64)
+        least_key(1)
+        ts(A("pL", 2, 48, 3), e, float(F0), op.add)
+        to_list(1)
+        for _ in range(min(len(spare), 8)):
+            spare.pop(0)()
+        rounded(0)
+        scored(0)
+        act(A("T4"), price, AF.Identity, bias=163.375, scale=-0.25)
+        act(A("SCE"), A("KC"), AF.Identity, bias=A("EVM"), scale=A("EVN"))
+
         big = 1.5 * 2.0 ** 35
-        kf = A("TRM", 15, NP, 16)
-        kl = A("KL", 2, 48, 3)
-        ts(A("RB", 1, 48, 3), key, big, op.add, -big, op.add)
-        ts(A("RB", 2, 48, 3), key, 131072.0, op.is_ge, -BIG, op.mult)
-        scan(A("KL"), A("RB"), A("pL", 0, 48), 0.0, op.subtract, op.max)
-        ts(A("KU"), kl, CK, op.add)
-        ts(A("BU"), A("KL", 1, 48, 3), -1.0, op.mult, float(MID), op.add)
-        act(A("KH", 0, 16), kl, AF.Identity, bias=CK)
-        act(kf, kl, AF.Identity, bias=CK)
-        act(A("KRF", 16 * NV, NP), IND(A("IOTA"), A("KU", NV, 16)), AF.Identity, bias=-CK)
-        cp(A("KR"), IND(A("IOTA"), A("KU")))
-        tt(A("KH", 16, 32), kf, A("KH", 0, 16), op.subtract)
-        for u in range(2):
-            mm(A("pD", 15, NP, 16), A("ID15"), A("KH", 16 * u, 16 * u + 16), False, False)
-        for j in range(NV, 16):
-            act(ROWS("EA", j - NV, j - NV + 1, 0, NP - 16 * j), A("KRF", 16 * j, NP), AF.Abs, bias=A("KL", 3 * j + 2, 3 * j + 3), scale=-1.0)
-        for j0, j1 in SROWS:
+
+        def third(n, h, k):
+            return A(n, 24 * h + k, 24 * h + 24, 3)
+
+        def decode(h):
+            ts(third("RB", h, 1), third("pL", h, 0), big, op.add, -big, op.add)
+            ts(third("RB", h, 2), third("pL", h, 0), -65536.0, op.add, float(MID), op.max)
+
+        def keyed(h):
+            scan(A("KL", 24 * h, 24 * h + 24), A("RB", 24 * h, 24 * h + 24), A("pL", 24 * h, 24 * h + 24), 0.0, op.subtract, op.min)
+
+        def keyrow(q, a, b):
+            x, y = A("KR", a, b), IND(A("IOTA"), A("KU", a // 16, b // 16))
+            cp(x, y) if q == "V" else act(x, y, AF.Identity)
+
+        def first(h):
+            cp(A("KH", 8 * h, 8 * h + 8), third("KL", h, 2))
+
+        def second(h):
+            tt(A("KH", 16 + 8 * h, 24 + 8 * h), third("KL", h, 2), A("KH", 8 * h, 8 * h + 8), op.subtract)
+
+        def distances(j0, j1):
+            for j in range(j0, j1):
+                act(ROWS("EA", j - NV, j - NV + 1, 0, NP - 16 * j), A("KR", 16 * j, NP), AF.Abs, bias=A("KL", 3 * j + 2, 3 * j + 3), scale=-1.0)
+
+        def clipped(j0, j1):
             act(ROWS("E", j0, j1, 0, NP - 16 * j0), ROWS("EA", j0 - NV, j1 - NV, 0, NP - 16 * j0), AF.Relu, bias=1.0, scale=-1.0)
+
+        def row(j):
+            ts(ROWS("E", j, j + 1, 0, NP - 16 * j), A("KR", 16 * j, NP), A("KH", j, j + 1), op.subtract, A("KH", 16 + j, 17 + j), op.is_equal)
 
         def tail(j):
             mm(A("pD", 16 * j + 16, NP), A("BDB"), ROWS("E", j, j + 1, 16, NP - 16 * j), False, False)
@@ -532,154 +529,210 @@ def rank_program(g, core, T, topo):
         def heads(j0, j1, stop=False):
             mm(A("pD", 16 * j0, 16 * j1), A("LOW"), ROWS("E", j0, j1, 0, 16), False, stop)
 
-        for j in range(NV):
-            ts(ROWS("E", j, j + 1, 0, NP - 16 * j), A("KR", 16 * j, NP), A("KH", j, j + 1), op.subtract, A("KH", 16 + j, 17 + j), op.is_equal)
+        high = list(range(8, NV))
+
+        def ahead(n):
+            for _ in range(n):
+                row(high[0])
+                tail(high.pop(0))
+
+        fillers(2)
+        decode(1)
+        least_key(0)
+        keyed(1)
+        act(A("KU", 8, 16), third("KL", 1, 2), AF.Identity)
+        keyrow("S", 128, NP)
+        to_list(0)
+        first(1)
+        fillers(1)
+        second(1)
+        distances(NV, 16)
+        clipped(NV, 16)
+        fillers(1)
+        decode(0)
+        ahead(2)
+        keyed(0)
+        ahead(2)
+        cp(A("KU", 0, 8), third("KL", 0, 2))
+        first(0)
+        keyrow("S", 64, 128)
+        fillers(1)
+        keyrow("V", 0, 64)
+        second(0)
+        act(A("BU"), A("KL", 1, 48, 3), AF.Identity, bias=float(MID), scale=-1.0)
+        act(A("TRM", 15, NP, 16), A("KL", 2, 48, 3), AF.Identity)
+        mm(A("pD", 15, NP, 16), A("ID15"), A("KL", 2, 48, 3), False, False)
+        for j in range(NV, 15):
             tail(j)
-            if j == NS:
-                for i in range(NV, 15):
-                    tail(i)
-                heads(NV, 16)
-        heads(0, NV, True)
+        heads(8, 16)
+        fillers(1)
+        for j in range(8):
+            row(j)
+            tail(j)
+            if j == 5:
+                heads(0, 6)
+        heads(6, 8, True)
+
+        def newkin():
+            act(A("SKF"), IND(Kg if t else A("KI", 0, V), A("BU")), AF.Identity, scale=A("ODD"))
+            if t == 0:
+                act(A("OFD"), A("EQ"), AF.Identity, bias=8192.0 + MID, scale=-8192.0)
+                act(A("K", SP - KS, SP), A("KI", V - KS, V), AF.Identity)
+                act(A("IDHF"), A("IDB"), AF.Identity, scale=0.5)
+
         act(A("BR"), IND(A("IOTA"), A("BU")), AF.Identity)
         act(A("XG"), IND(Xg, A("BU")), AF.Identity)
-        if t == 0:
-            act(A("OFD"), A("EQ"), AF.Identity, bias=8192.0 + MID, scale=-8192.0)
-            act(A("IDHF"), A("IDB"), AF.Identity, scale=0.5)
-        if last:
-            ycopy(0, "V")
         mm(A("pX", 0, NP), A("N32"), A("T4"), True, False)
         mm(A("pX", 0, NP), A("IDB"), A("XG"), False, True)
-        fillers(len(pend) + 3)
-        scan(A("FS"), A("TRM"), A("pD", 0, NP), 16384.0, op.min, op.max)
+        if jub:
+            cp(A("JB", 1, 48, 3), hold)
+        fillers(3)
+        while longer:
+            longer.pop(0)()
+        scan(A("FS"), A("TRM"), A("pD", 0, NP), 0.0, op.max, op.min)
         of2 = A("FS", 15, NP, 16)
         ofs = A("OFS", 16 * t, 16 * t + 16)
         cp(ofs, of2)
 
-        def redeemed(out, old, targets, scale, before, after):
-            mm(A("pQ", 0, NP), A("IDB"), old, True, False)
-            act(A("SG"), IND(A("IOTA"), targets), AF.Sign, bias=O0 - 0.5, scale=-1.0)
-            before()
-            mm(A("pQ", 0, NP), A("IDHF"), A("SG"), False, True)
-            after()
-            act(out, A("pQ", 0, NP), AF.Relu, bias=-0.5 * scale, scale=scale)
+        def flags(a, b, targets):
+            act(A("SG", a, b), IND(A("IOTA"), A(targets[0], targets[1] + a // 16, targets[1] + b // 16)), AF.Sign, bias=0.5 - V)
 
-        def newkin():
-            act(A("SKF"), IND(Kg, A("BU")), AF.Identity, scale=A("ODD"))
+        def newwealth():
+            emit("S", [A("XV"), ofs], [A("X")], lambda: g.scalar.activation(ap(IND(A("X"), ofs)), ap(A("XV")), AF.Silu))
 
-        if not jub:
-            newkin()
+        newkin()
         act(A("XV"), A("pX", 0, NP), AF.Identity, bias=160.0 * XS)
         if not jub:
             send(nxt, A("RO", 16 * t + 16, 16 * t + 32), ofs, "aO%d" % (t + 1))
             arrives(prv, A("RO", 16 * t + 16, 16 * t + 32), "aO%d" % (t + 1))
             arrives(prv, A("RP", NP * t + NP, NP * t + 2 * NP), "aP%d" % (t + 1))
+            newwealth()
         else:
-            redeemed(A("PN"), price, ofs, XS, lambda: None,
-                     lambda: emit("S", [A("XV"), ofs], [A("X")], lambda: g.scalar.activation(ap(IND(A("X"), ofs)), ap(A("XV")), AF.Silu)))
-            newkin()
-        if not jub:
-            emit("S", [A("XV"), ofs], [A("X")], lambda: g.scalar.activation(ap(IND(A("X"), ofs)), ap(A("XV")), AF.Silu))
-        if last:
-            act(A("SKH"), A("SKF"), AF.Identity, bias=-float(MID))
-            for k in (4, 5, 6):
-                yhalf(k)
-            ymm(2)
-            ymm(3)
+            mm(A("pQ", 0, NP), A("IDB"), price, True, False)
+            flags(0, NP, ofs)
+            mm(A("pQ", 0, NP), A("IDHF"), A("SG"), False, True)
+            newwealth()
+            act(A("PN"), A("pQ", 0, NP), AF.Relu, bias=-0.5 * XS, scale=XS)
         ho = A("HO", 16 * t, 16 * t + 16)
-        pend.append(lambda: ts(A("RL"), of2, float(O0), op.is_ge))
-        pend.append(lambda hold=hold: tt(A("BH"), of2, hold, op.subtract))
-        pend.append(lambda: tt(A("BH2"), A("RL"), A("BH"), op.mult))
         if jub:
-            pend.append(lambda: tt(A("HN"), A("BH2"), hold, op.add))
-            pend.append(lambda: ts(A("HG"), A("HN"), -CK, op.add))
-            pend.append(lambda: tt(A("WA"), A("HG"), A("WF"), op.mult))
-        fillers(2)
-        cp(IND(A("H"), ofs), A("BR"))
-        fillers(1)
-        tt(A("EG"), IND(A("H", F0, O0), e), A("OFD"), op.subtract)
-        fillers(1 if jub else 0)
+            ts(A("JA", 1, 48, 3), of2, float(V), op.is_lt)
+            tt(A("JB", 0, 48, 3), of2, hold, op.subtract)
+            cp(IND(A("H"), ofs), A("BR"))
+            scan(A("JC"), A("JA"), A("JB"), 0.0, op.mult, op.add)
+            tt(A("BR"), IND(A("H", F0, SP), e), A("CAP"), op.min)
+            cp(A("RSJ", 1, NP, 16), A("JC", 2, 48, 3))
+        else:
+            ts(A("RL"), of2, float(V), op.is_lt)
+            tt(A("BH"), of2, hold, op.subtract)
+            cp(IND(A("H"), ofs), A("BR"))
+            tt(A("BH2"), A("RL"), A("BH"), op.mult)
+            fillers(1)
+            tt(A("EG"), IND(A("H", F0, SP), e), A("OFD"), op.subtract)
+            tt(ho, A("BH2"), hold, op.add)
+            fillers(1)
 
         def kpart():
             tt(IND(A("K"), ofs), A("SKF"), A("SCE"), op.add)
 
         el = A("ES", 15, NP, 16)
         en = A("FO", 0, 16) if last else A("EN", 16 * t, 16 * t + 16)
-        scan(A("ES"), A("RSH"), A("EG"), -32768.0, op.add, op.max)
         if not jub:
+            scan(A("ES"), A("RSH"), A("EG"), -32768.0, op.add, op.max)
+            fillers(1)
             ts(en, el, float(MID), op.add)
             send(nxt, A("RE", 16 * t + 16, 16 * t + 32), en, "aE%d" % (t + 1))
-
-            def wide():
-                for k in range(0, 16, 4):
-                    act(A("P16", k, 1024, 16), A("pQ", 64, 128), AF.Relu, bias=-0.5 * XS, scale=XS)
-
-            redeemed(A("PO", NP * t + NP, NP * t + 2 * NP), A("RP", NP * t + NP, NP * t + 2 * NP), A("RO", 16 * t + 16, 16 * t + 32),
-                     1.0, lambda: prepare(t + 1), wide)
+            n0 = NP * t + NP
+            shares = (("pP", V0, NP), ("pQ", 0, V0))
+            for x, a, b in shares:
+                mm(A(x, a, b), A("IDB"), A("RP", n0 + a, n0 + b), True, False)
+            prepare(t + 1)
+            for x, a, b in shares:
+                flags(a, b, A("RO", 16 * t + 16, 16 * t + 32))
+                mm(A(x, a, b), A("IDHF"), A("SG", a, b), False, True)
+            for k in range(0, 16, 4):
+                act(A("P16", k, PW, 16), A("pP", V0, NP), AF.Relu, bias=-0.5 * XS, scale=XS)
+            for x, a, b in shares[::-1]:
+                act(A("PO", n0 + a, n0 + b), A(x, a, b), AF.Relu, bias=-0.5)
+            fillers(len(pend))
             kpart()
             doubled(4)
-            tt(ho, A("BH2"), hold, op.add)
             send(nxt, A("RH", 16 * t + 16, 16 * t + 32), ho, "aH%d" % (t + 1))
             doubled(2)
         else:
-            fillers(1)
-            tt(A("DW"), el, A("WB"), op.mult)
-            fillers(1)
-            tt(A("EJ"), A("DW"), A("WA"), op.add)
-            ts(en, A("EJ"), float(MID), op.add)
+            scan(A("EXP"), A("RSJ"), A("BR"), 0.0, op.add, op.max)
+            cp(en, A("EXP", 15, NP, 16))
             if not last:
                 send(nxt, A("RE", 16 * t + 16, 16 * t + 32), en, "aE%d" % (t + 1))
                 prepare(t + 1)
-            else:
-                ycopy(1, "V")
             sums = A("pL", 64, 80)
             mm(sums, A("WBD"), A("C160"), True, False)
-            halves = ((0, 128), (128, NP))
-            for a, b in halves:
-                tt(A("PJ1", a, b), IND(Xg, (en[0], en[1] + a // 16, en[1] + b // 16, 1)), A("PN", a, b), op.subtract)
-            for a, b in halves:
-                ts(A("PJ2", a, b), A("PJ1", a, b), 0.5 / XS, op.mult, 167.25, op.add)
-            for h, (a, b) in enumerate(halves):
-                if not last:
-                    ts(A("PO", a, b), A("PJ2", a, b), -1.0, op.mult, 175.0, op.add)
-                    send(nxt, A("RP", NP * t + NP + a, NP * t + NP + b), A("PO", a, b), "a%s%d" % ("PO"[h], t + 1))
-            if not last:
+            todo = list(range(NF, NB))
+
+            def halved(n):
+                b0, b1 = todo[0], min(todo[0] + n, NB)
+                del todo[:n]
+                ts(A("M", 128 * b0, 128 * b1), A("K", F0 + 128 * b0, F0 + 128 * b1), -float(MID), op.add)
+
+            def whole(b0, b1):
+                for b in range(b0, b1):
+                    mm(A("pP", b, 8 * NB, NB), A("K", F0 + 128 * b, F0 + 128 * b + 128), A("YF"), False, False)
+
+            if last:
                 kpart()
+                mm(A("pP", 0, 8 * NB), A("ONE") + lane(0), A("YC") + lane(0), True, False)
+                whole(0, 8)
+            halves = ((0, 0, NP),) if last else ((1, 128, NP), (0, 0, 128))
+            for h, a, b in halves:
+                tt(A("PJ1", a, b), IND(Xg, (en[0], en[1] + a // 16, en[1] + b // 16, 1)), A("PN", a, b), op.subtract)
+            if last:
+                halved(1)
+            for h, a, b in halves:
+                ts(A("PJ2", a, b), A("PJ1", a, b), 0.5 / XS, op.mult, 167.25, op.add)
+                if not last:
+                    act(A("PO", a, b), A("PJ2", a, b), AF.Identity, bias=175.0, scale=-1.0)
+                    send(nxt, A("RP", NP * t + NP + a, NP * t + NP + b), A("PO", a, b), "a%s%d" % ("PO"[h], t + 1))
             for j in range(16):
                 mm(sums, A("WH", 15 - j, 143 - j), A("PJ2", j, NP, 16), False, j == 15)
             if last:
-                mm(A("pX", 0, NP), A("YWE"), A("KC"), True, False)
-                mm(A("pX", 0, NP), A("YWO"), A("SKH"), False, True)
-                for k in (4, 5, 6):
-                    ymm(k)
-                ycopy(2, "V")
+                whole(8, NF)
+                halved(4)
                 cp(A("HI"), sums)
+                halved(1)
                 ts(A("HA"), A("HI"), 4095, op.bitwise_and)
+                halved(1)
                 cp(A("FO", 16, 32), A("HA"))
                 send(nxt, A("FIN"), A("FO"), "aF")
+                halved(NB)
             else:
+                kpart()
+                act(A("HI"), sums, AF.Identity)
+
                 def hnew(t=t, ho=ho):
                     tt(ho, A("HA"), A("HG"), op.add)
                     send(nxt, A("RH", 16 * t + 16, 16 * t + 32), ho, "aH%d" % (t + 1))
-                cp(A("HI"), sums)
                 pend.append(lambda: ts(A("HA"), A("HI"), 4095, op.bitwise_and))
-                pend.append(lambda: ts(A("HG"), A("HA"), float(V), op.is_lt, float(V), op.mult))
-                pend.append(lambda: ts(A("HG"), A("HG"), float(NP), op.add))
+                pend.append(lambda: ts(A("HG"), A("HA"), float(V), op.is_ge, -float(V), op.mult))
                 pend.append(hnew)
         if last:
             outs = []
-            outs.append(("Y", dma("Y", T.yh[:, :], T.H[0:128:16, F0:O0], [A("H", F0, O0)], [])))
-            for k, (a, b) in enumerate(parts):
-                act(A("G", a, b), A("X", O0 + a, O0 + b), AF.Relu, bias=-2.0 ** -10, scale=1.0 / XS)
-                outs.append(("Y", dma("Y", T.yx[:, a:b], T.G[:, a:b], [A("G", a, b)], [])))
-                if k == 1:
-                    act(A("YF"), A("pX", 0, NP), AF.Identity, bias=136.0 * MID)
-            for k in (3, 4, 5, 6):
-                ycopy(k, "V")
-            cp(IND(A("YK"), ofs), A("YF"))
-            outs.append(("Y", dma("Y", T.yk[:, :], T.YK[0:128:16, F0:O0], [A("YK", F0, O0)], [])))
+            outs.append(("Y", dma("Y", T.yh[:, :], T.H[0:128:16, F0:SP], [A("H", F0, SP)], [])))
+
+            for a in range(0, V, V // 4):
+                b = a + V // 4
+                act(A("XB", a, b), A("X", a, b), AF.Relu, bias=-2.0 ** -10, scale=1.0 / XS)
+                outs.append(("Y", dma("Y", T.yx[:, a:b], T.XB[:, a:b], [A("XB", a, b)], [])))
+            for b in range(NF, NB):
+                mm(A("pP", b, 8 * NB, NB), A("M", 128 * b, 128 * b + 128), A("YW"), False, b == NB - 1)
             arrives(prv, A("FIN"), "aF")
+            cp(A("YA"), A("pP", 0, 8 * NB))
             act(A("YO"), IND(A("IOTA"), A("FIN", 0, 16)), AF.Identity)
+            rows = ((0, 4 * NB),)
+            for u in range(2):
+                mm(A("pK", 128 * u, 128 * u + 128) + rows, A("YA", 4 * NB * u, 4 * NB * u + 4 * NB), A("IDF"), True, True)
+            cp(A("YB") + rows, A("pK", 0, NP) + rows)
             cp(A("YT"), IND(A("KI"), A("FIN", 16, 32)))
+            for u in range(2):
+                outs.append(("Y", dma("Y", T.yk[4 * u:4 * u + 4, :], T.YB[0:4 * NB, 128 * u:128 * u + 128], [A("YB")], [])))
             for k, (y, o) in enumerate((("YT", T.yt), ("YO", T.yo))):
                 outs.append(("YS"[k], dma("YS"[k], o[:, :], T[y][0:128:16, :], [A(y)], [])))
             for q, s in outs:

import math
from concourse.mybir import AluOpType, ActivationFunctionType

V, NP, NT, TERM = 3584, 256, 8, 4
F0, SP = V, 2 * V
W = NP + 2 * V
MID = V // 2
V0 = 192
LAST = 96
NV = 12
KV, KS = 1152, 896
XS = 32.0
R = 8
KW = 136
RO = 1536.0
BIG = float(2 ** 30)
FAR = 16384.0
OFF = (15 - 1.0 / 64) * XS
NB = V // 128
NF = 19
PW = 16 * (NP - V0)

_S = {}
F, B, I, U, Hf = "float32", "bfloat16", "int32", "uint16", "float16"
for _n, _w, _d in [
        ("K", W, F), ("KI", 4096, I), ("X", W, F), ("H", W, F), ("IOTA", W, F),
        ("OWN", 16, I), ("WL", 16, I), ("WR", 16, I), ("HI0", 16, I), ("WTI", 1, I),
        ("RE", 16 * NT, U), ("RP", NP * NT, B), ("RH", 16 * NT, F), ("FIN", 32, U),
        ("EN", 16 * NT, U), ("PO", NP * NT, B), ("HO", 16 * NT, F), ("FO", 32, U),
        ("CU", NP, U), ("KC", NP, Hf), ("G", 16 * NP, Hf), ("XB", V, B), ("M", 16 * NP, Hf),
        ("RR", 4 * KW, Hf), ("D1", 2 * KW, F), ("SC", 2 * KW, F), ("EXP", NP, F),
        ("OFD", NP, F), ("RSH", NP, Hf), ("JA", 48, F), ("JB", 48, F), ("JC", 48, F), ("CAP", NP, F), ("RSJ", NP, F), ("WU", 16, U),
        ("RB", 48, F), ("KL", 48, F), ("ID15", 128, F), ("KH", 32, B),
        ("KU", 16, U), ("BU", 16, U), ("OFS", 16 * NT, U), ("RO", 16 * NT, U),
        ("KR", NP, U), ("FS", NP, F),
        ("BR", NP, F), ("EG", NP, Hf), ("ES", NP, Hf), ("T4", NP, B), ("XG", NP, B), ("XV", NP, F),
        ("SKF", NP, F), ("SCE", NP, F), ("SG", NP, B), ("PN", NP, B),
        ("RL", 16, F), ("BH", 16, F), ("BH2", 16, F),
        ("PJ1", NP, B), ("PJ2", NP, B), ("HI", 16, I), ("HA", 16, I), ("HG", 16, F), ("YO", NP, F), ("YT", NP, F),
        ("YA", 8 * NB, F), ("YB", NP, F),
        ("IP", 1, I), ("ICF", NP, B), ("CMF", NP, B), ("CGF", 128, B), ("CG17", 2 * KW, B), ("TMP", 128, B), ("EQ", NP, B),
        ("PMI", 1, I), ("ODI", 1, I), ("COL", 16, F),
        ("YW", 8, B), ("YF", 8, F), ("YC", 8 * NB, B), ("IDF", 128, F), ("WH", 144, B), ("A8", 8, F), ("BG", 16, B), ("BM", 16, B),
        ("INI", 4 * KW, B), ("ONE", 128, B), ("PERM", KW, B), ("IDP", 128, B), ("IDM", 128, B),
        ("P16", PW, B), ("IDB", 128, B), ("N32", 128, B), ("IDHF", 128, B),
        ("BDQ", 2 * KW, B), ("BDB", 128, B), ("LOW", 128, B), ("C160", 16, B), ("WBD", 128, B), ("MASK", NP, B),
        ("DIAG", 128, F), ("TRM", NP, F), ("LOFF", 8, U)]:
    _S[_n] = ("sbuf", [128, _w], _d)
_S["E"] = ("sbuf", [128, 16, NP], B)
_S["EA"] = ("sbuf", [128, 16 - NV, NP - 16 * NV], F)
COLS = ["PF", "PM", "PG", "PG15", "ODD", "EVN", "EVM", "K1", "WTF", "PMS", "P15", "PC"]
for _n in ["pP", "pY0", "pY1", "pK", "pL", "pD", "pX", "pQ"]:
    _S[_n] = ("psum", [128, 512], F)
SCRATCH = _S
NDMA = 24
SEMAPHORES = (["qV", "qS", "qT", "qG", "loc", "aW", "aF"] + ["aE%d" % t for t in range(NT)] + ["aP%d" % t for t in range(NT)]
              + ["aH%d" % t for t in range(NT)] + ["aO%d" % t for t in range(NT)] + ["d%d" % k for k in range(NDMA)])


def rank_program(g, core, T, topo):
    rank = T.rank_of(core)
    if rank is None:
        return
    nxt, prv = T.cores[(rank + 1) % 4], T.cores[(rank + 3) % 4]
    op = AluOpType
    AF = ActivationFunctionType
    queues = {"V": g.vector, "S": g.scalar, "T": g.tensor, "G": g, "Y": g.sync}
    count = {}
    known = {q: {} for q in queues}
    log = {}
    order = [0]
    ndma = [0]
    nloc = [0]

    def A(n, a=0, b=None, s=1):
        if n in COLS:
            return ("COL", COLS.index(n), COLS.index(n) + 1, 1)
        return (n, a, _S[n][1][1] if b is None else b, s)

    def IND(w, o):
        return ("ind", w, o)

    def ROWS(n, j0, j1, a, b):
        return ("rows", n, j0, j1, a, b)

    def ap(x):
        if not isinstance(x, tuple):
            return x
        if x[0] == "ind":
            return ap(x[1]).indirect(ap(x[2]))
        if x[0] == "rows":
            return T[x[1]][:, x[2], x[4]:x[5]] if x[3] == x[2] + 1 else T[x[1]][:, x[2]:x[3], x[4]:x[5]]
        n, a, b, s = x[:4]
        p = slice(*x[4]) if len(x) > 4 else slice(None)
        return T[n][p, a:b] if s == 1 else T[n][p, a:b:s]

    def regs(x):
        if not isinstance(x, tuple):
            return []
        if x[0] == "rows":
            w = _S[x[1]][1][2]
            return [(x[1], w * j + x[4], w * j + x[5], 1) for j in range(x[2], x[3])]
        return [x[1], x[2]] if x[0] == "ind" else [x]

    def psum(n):
        return _S[n][0] == "psum"

    def lanes(r):
        return r[4] if len(r) > 4 else (0, 128)

    def need(q, reads, writes):
        ev = []
        for lst, wr in ((reads, False), (writes, True)):
            for r in lst:
                for e in log.get(r[0], []):
                    meet = (e[0] < r[2] and r[1] < e[1] and (wr or e[2]) and (e[0] - r[1]) % math.gcd(e[5], r[3]) == 0
                            and e[6][0] < lanes(r)[1] and lanes(r)[0] < e[6][1])
                    if psum(r[0]):
                        if e[3] != q or (q != "T" and meet):
                            ev.append(e[4])
                    elif meet:
                        ev.append(e[4])
        ev.sort(key=lambda e: -e[0])
        for e in ev:
            if known[q].get(e[1], 0) >= e[2]:
                continue
            queues[q].wait_ge(T.sem[e[1]], e[2])
            for k, v in e[3].items():
                known[q][k] = max(known[q].get(k, 0), v)

    def covers(r, e):
        return len(r) == 4 and r[1] <= e[0] and e[1] <= r[2] and e[5] % r[3] == 0 and (e[0] - r[1]) % r[3] == 0

    def note(q, reads, writes, event):
        for r in writes:
            l = log.setdefault(r[0], [])
            l[:] = [e for e in l if not covers(r, e)]
            l.append((r[1], r[2], True, q, event, r[3], lanes(r)))
        for r in reads:
            l = log.setdefault(r[0], [])
            l[:] = [e for e in l if not (not e[2] and e[3] == q and covers(r, e))]
            l.append((r[1], r[2], False, q, event, r[3], lanes(r)))
        for r in reads + writes:
            l = log[r[0]]
            if len(l) > 64:
                l[:] = [e for e in l if not all(known[k].get(e[4][1], 0) >= e[4][2] for k in "VST")] if psum(r[0]) else l

    def event(q, sem, val):
        order[0] += 1
        c = dict(known[q])
        c[sem] = val
        return (order[0], sem, val, c)

    def emit(q, reads, writes, fn):
        need(q, reads, writes)
        sem = "q" + q
        count[sem] = count.get(sem, 0) + 1
        fn().then_inc(T.sem[sem], 1)
        note(q, reads, writes, event(q, sem, count[sem]))

    def external(x, sem, val):
        order[0] += 1
        log.setdefault(x[0], []).append((x[1], x[2], True, "X", (order[0], sem, val, {sem: val}), 1, (0, 128)))

    def tt(out, a, b, o, q="V"):
        wr = [out[1]] if out[0] == "ind" else [out]
        rd = regs(a) + regs(b) + ([out[2]] if out[0] == "ind" else [])
        emit(q, rd, wr, lambda: g.vector.tensor_tensor(ap(out), ap(a), ap(b), o))

    def ts(out, a, s1, o1, s2=None, o2=None):
        rd = regs(a) + regs(s1) + regs(s2)
        if o2 is None:
            emit("V", rd, regs(out), lambda: g.vector.tensor_scalar(ap(out), ap(a), ap(s1), None, o1))
        else:
            emit("V", rd, regs(out), lambda: g.vector.tensor_scalar(ap(out), ap(a), ap(s1), ap(s2), o1, o2))

    def cp(out, a):
        wr = [out[1]] if out[0] == "ind" else [out]
        emit("V", regs(a) + ([out[2]] if out[0] == "ind" else []), wr, lambda: g.vector.tensor_copy(ap(out), ap(a)))

    def scan(out, d0, d1, init, o0, o1):
        emit("V", [d0, d1], [out], lambda: g.vector.tensor_tensor_scan(ap(out), ap(d0), ap(d1), init, o0, o1))

    def fill(out, c):
        emit("V", [], regs(out), lambda: g.vector.memset(ap(out), c))

    def act(out, a, f, bias=0.0, scale=1.0):
        emit("S", regs(a) + regs(bias) + regs(scale), regs(out),
             lambda: g.scalar.activation(ap(out), ap(a), f, bias=ap(bias), scale=ap(scale)))

    def mm(out, l, r, start, stop):
        emit("T", [l] + regs(r), [out], lambda: g.tensor.matmul(ap(out), ap(l), ap(r), start, stop))

    def dma(q, out, in_, reads, writes):
        need(q, reads, writes)
        sem = "d%d" % ndma[0]
        ndma[0] += 1
        queues[q].dma_start(out, in_).then_inc(T.sem[sem], 16)
        note(q, reads, writes, event(q, sem, 16))
        return sem

    def send(dst, out, in_, sem):
        need("G", [in_], [])
        rid, pid = topo.addr(dst)[:2]
        m = topo.engines(core, dst)[:8]
        mask = sum(1 << e for e in m)
        g.remote_dma(ap(out), ap(in_), T.sem[sem], T.sem.loc, pid, rid, mask)
        nloc[0] += len(m)

    def arrives(src, x, sem):
        external(x, sem, len(topo.engines(src, core)[:8]))

    parts = ((0, KV), (KV, 2304), (2304, V))
    xparts = ((0, MID), (MID, V))
    for q, n, src in (("S", "PN", T.price), ("S", "WL", T.wall), ("S", "OWN", T.own)):
        dma(q, T[n][:, :], src[:, :], [], [A(n)])
    for a, b in xparts:
        dma("Y", T.XB[:, a:b], T.x[:, a:b], [], [A("XB", a, b)])
    for a, b in parts:
        dma("Y", T.KI[:, a:b], T.kin[:, a:b], [], [A("KI", a, b)])
    for q, n, src in (("Y", "HI0", T.hold), ("Y", "WTI", T.wt)):
        dma(q, T[n][:, :], src[:, :], [], [A(n)])

    def iota(x, pattern, base=0, per=0):
        flag = {"allow_small_or_imprecise_dtypes": True} if _S[regs(x)[0][0]][2] != I else {}
        emit("G", [], regs(x), lambda: g.iota(ap(x), pattern, base, per, **flag))

    def lane(p):
        return ((p, p + 1),)

    fill(A("INI"), 0.0)
    iota(A("IP"), [[1, 1]], 0, 1)
    iota(A("PF"), [[1, 1]], 0, 1)
    iota(A("ICF"), [[1, NP]])
    iota(A("CG17"), [[0, 2], [16, 8], [0, 17]])
    iota(A("CMF"), [[0, 16], [1, 16]])
    iota(A("CGF"), [[16, 8], [0, 16]])
    iota(A("INI", 2 * KW, 4 * KW) + lane(0), [[0, 16], [-4096, 17]], 65536)
    act(A("TRM"), A("ICF"), AF.Silu, scale=0.0)
    act(A("IOTA", 0, NP), A("ICF"), AF.Identity)
    iota(A("IOTA", MID, V), [[1, MID]], MID)
    iota(A("IOTA", V, W), [[1, W - V]], V)
    for a, b in xparts:
        act(A("X", a, b), A("XB", a, b), AF.Identity, scale=XS)
    for n in (NP, 2 * NP):
        act(A("IOTA", n, 2 * n), A("IOTA", 0, n), AF.Identity, bias=float(n))

    def first_heirs(a, b):
        dma("Y", T.H[:, F0 + a:F0 + b], T.IOTA[:, a:b], [A("IOTA", a, b)], [A("H", F0 + a, F0 + b)])

    need("Y", [A("WTI")], [])
    first_heirs(MID, V)
    first_heirs(0, 1024)
    ts(A("PMI"), A("IP"), 15, op.bitwise_and)
    ts(A("ODI"), A("IP"), 1, op.bitwise_and)
    fill(A("ONE"), 1.0)
    cp(A("PM"), A("PMI"))
    cp(A("ODD"), A("ODI"))
    fill(A("ONE", 0, V0 - 128) + ((64, 128),), 0.0)
    fill(A("RB"), BIG)
    tt(A("PG"), A("PF"), A("PM"), op.subtract)
    ts(A("EVN"), A("ODD"), -1.0, op.mult, 1.0, op.add)
    ts(A("PMS"), A("PM"), float(SP), op.add)
    ts(A("P15"), A("PM"), 15.0, op.is_equal)
    ts(A("PC"), A("PG"), 17.0 / 16, op.mult, 16.0, op.add)
    ts(A("EVM"), A("EVN"), float(MID), op.mult)
    fill(A("pL", 0, 48), BIG)
    tt(A("PC"), A("PC"), A("PM"), op.subtract)
    ts(A("RP", 0, NP), A("PN"), -1.0, op.mult, 15.0, op.add)
    send(nxt, A("RP", NP, 2 * NP), A("RP", 0, NP), "aP1")
    idn = A("ICF", 0, 128)
    ts(A("IDB"), idn, A("PF"), op.is_equal)
    ts(A("N32"), idn, A("PF"), op.is_equal, -XS, op.mult)
    ts(A("IDP"), idn, A("PF"), op.is_equal, 256.0 * 65536, op.mult)
    ts(A("IDM"), idn, A("PF"), op.is_equal, -255.0 * 65536, op.mult)
    ts(A("PERM"), A("ICF", 0, KW), A("PC"), op.is_equal)
    ts(A("LOFF"), A("ICF", 0, 8), 17.0, op.mult, 16.0, op.add)
    for p, c in ((64, 15.0 * 2 ** 20), (96, -16384.0)):
        fill(A("INI", 0, 2 * KW) + lane(p), c)
    fill(A("INI", 0, KW) + lane(0), -16.5 * 2048)
    fill(A("INI", 2 * KW, 3 * KW) + lane(32), -(256 + RO) * 65536.0)

    def doubled(s):
        cp(A("P16", s // 2, PW, s), A("P16", 0, PW, s))

    for k in range(0, 16, 4):
        ts(A("P16", k, PW, 16), A("RP", V0, NP), XS, op.mult)
    ts(A("BDQ"), A("CG17"), A("PG"), op.is_equal, 65536.0, op.mult)
    doubled(4)
    ts(A("BG"), A("CG17", 0, 2 * KW, 17), A("PG"), op.is_equal, -65536.0 / XS, op.mult)
    ts(A("BM"), A("CG17", 0, 2 * KW, 17), A("PG"), op.is_equal, 131072.0 / XS, op.mult)
    ts(A("A8"), A("CG17", 0, KW, 17), A("PG"), op.is_equal)
    doubled(2)
    cp(A("RE", 0, 16), A("OWN"))
    ts(A("EQ"), A("CMF"), A("PM"), op.is_equal)
    fill(A("INI", 2 * KW, 4 * KW, 17) + lane(0), float(2 ** 25))
    ts(A("BDB"), A("CGF"), A("PG"), op.is_equal, FAR, op.mult)
    ts(A("TMP"), A("CMF", 0, 128), A("PM"), op.is_gt)
    ts(A("PG15"), A("PG"), 15.0, op.add)
    ts(A("WBD"), A("CGF"), A("PG"), op.is_equal)
    ts(A("WH"), A("ICF", 0, 144), A("PG15"), op.is_equal)
    cp(A("DIAG"), A("EQ", 0, 128))
    ts(A("MASK"), A("EQ"), -FAR, op.mult, FAR, op.add)
    tt(A("LOW"), A("TMP"), A("BDB"), op.mult)
    ts(A("TRM", 0, NP, 16), A("ICF", 0, NP, 16), A("PMS"), op.add)
    ts(A("ID15"), idn, A("PF"), op.is_equal, A("P15"), op.mult)
    ts(A("RSH"), A("CMF"), 0.0, op.is_equal, -32768.0, op.mult)
    cp(A("K", F0, F0 + KV), A("KI", 0, KV))

    def jubilee_constants():
        ID = AF.Identity
        return [lambda: act(A("WTF"), A("WTI"), ID),
                lambda: act(A("JA"), A("RB"), ID, scale=0.0),
                lambda: act(A("JB"), A("RB"), ID, scale=0.0),
                lambda: act(A("RSJ"), A("RSH"), ID),
                lambda: act(A("K1"), A("PM"), ID, bias=1.0),
                lambda: act(A("C160"), A("ICF", 0, 16), ID, bias=-160.0, scale=0.0),
                lambda: act(A("JC", 0, 2), A("ICF", 0, 2), ID, bias=4096.0, scale=-4096.0),
                lambda: act(A("IDF"), A("IDB"), ID),
                lambda: act(A("WU"), A("WR"), ID),
                lambda: act(A("JA", 2, 48, 3), A("WR"), ID),
                lambda: act(A("YW"), A("A8"), ID, scale=A("K1")),
                lambda: act(A("YF"), A("A8"), ID, scale=A("K1")),
                lambda: act(A("WH"), A("WH"), ID, scale=A("WTF")),
                lambda: act(A("WBD"), A("WBD"), ID, scale=A("WTF")),
                lambda: longer.append(lambda: tt(A("CAP"), IND(A("JC", 0, 2), A("WU")), A("EQ"), op.mult))]

    BANK = ("pX", "pP", "pD", "pQ")

    def ranks(x, rows):
        mm(x, A("ONE") + ((0, rows),), A("INI", 2 * KW, 2 * KW + x[2] - x[1]) + ((0, rows),), True, False)

    def prepare(t):
        for h in (1, 0):
            p = ((0, 128 if h == 1 and t != TERM else 64),)
            mm(A("pY%d" % h, 0, 2 * KW), A("ONE") + p, A("INI", 0, 2 * KW) + p, True, False)
        ranks(A("pK", 0, 2 * KW), 32)

    pend = []
    spare = [lambda: act(A("IOTA", 1024, MID), A("IOTA", 0, MID - 1024), AF.Identity, bias=1024.0), lambda: first_heirs(1024, MID)]
    longer = []
    prepare(0)
    for t in range(NT):
        e = A("RE", 16 * t, 16 * t + 16)
        pb = "PO" if t % TERM else "RP"
        price = A(pb, NP * t, NP * t + NP)
        hold = A("RH", 16 * t, 16 * t + 16)
        jub = t % TERM == TERM - 1
        last = t == NT - 1
        if t:
            if t % TERM == 0:
                for h in range(2):
                    arrives(prv, A(pb, NP * t + 128 * h, NP * t + 128 * h + 128), "a%s%d" % ("PO"[h], t))
            arrives(prv, e, "aE%d" % t)
            arrives(prv, hold, "aH%d" % t)
        if t and not jub:
            need("G", [e], [])
            send(nxt, A("RP", NP * t + NP, NP * t + 2 * NP), price, "aP%d" % (t + 1))
        if t == 1:
            send(prv, A("WR"), A("WL"), "aW")
            arrives(nxt, A("WR"), "aW")
            iota(A("YC"), [[0, 8], [1, NB]])
            iota(A("KI", 0, V), [[1, V]])
            iota(A("KI", V, 4096), [[1, 4096 - V]])
            longer.append(lambda: ts(A("YC"), A("YC"), float(NF), op.is_ge, 136.0 * MID, op.mult))
            spare += jubilee_constants()
        Kg, Xg = A("K", F0, SP), A("X", 0, V)

        def kin(a, b):
            cp(A("CU", a, b), IND(Kg if t else A("KI", 0, V), A("RE", 16 * t + a // 16, 16 * t + b // 16)))

        def wealth(a, b):
            act(A("G", 16 * a, 16 * b), IND(Xg, A("CU", a, b)), AF.Identity, bias=-OFF)

        def span(a, b):
            return ((a % 128, (b - 1) % 128 + 1),)

        def ysum(k, a, b):
            return A("pY%d" % (a // 128), 16 - k, 2 * KW, 17) + span(a, b)

        def gsum(a, b):
            for k in range(16):
                mm(ysum(k, a, b), A("G", 16 * a + k, 16 * b, 16), A("BG"), False, False)

        def least(a, b, sums=None, between=None):
            n = 16 // R
            for s in range(n):
                tt(A("M", 16 * a + s, 16 * b, n), A("G", 16 * a + s, 16 * b, n), A(BANK[a // 64], R * (a % 64), R * ((b - 1) % 64 + 1)), op.max)
                if between and s:
                    between()
                if sums:
                    for k in range(s, 16, n):
                        mm(ysum(k, *sums), A("M", 16 * sums[0] + k, 16 * sums[1], 16), A("BM"), False, k == 15)

        keys = (A("pK", 2 * KW, 3 * KW), A("pL", 2 * KW, 3 * KW))

        def half(n, h):
            return A(n, KW * h, KW * h + KW)

        def persons(x, h, stop=True):
            mm(x, A("KC", 128 * h, 128 * h + 128), A("PERM"), False, stop)

        def scored(h):
            mm(keys[h], A("IDP"), half("RR", 2 * h + 1), False, False)
            mm(keys[h], A("IDM"), half("RR", 2 * h), False, False)
            persons(keys[h], h)

        def least_key(h):
            scan(half("SC", h), keys[h], half("D1", h), 0.0, op.min, op.max)

        def to_list(h):
            lo, hi = 128 * h, 128 * h + 128
            tt(A("EXP", lo, hi), IND(half("SC", h), A("LOFF")), A("DIAG", 0, 128), op.mult)
            mm(A("pL", 24 * h, 24 * h + 24, 3), A("EXP", lo, hi), A("A8"), True, True)

        def fillers(n):
            for _ in range(n):
                if pend:
                    pend.pop(0)()

        if t == 0:
            pend.append(lambda: fill(ROWS("EA", 0, 16 - NV, 0, NP - 16 * NV), 1.0))
            pend.append(lambda: cp(A("RH", 0, 16), A("HI0")))
            for a in range(KV, V - KS, 128):
                pend.append(lambda a=a: cp(A("K", F0 + a, F0 + a + 128), A("KI", a, a + 128)))
        early = t != TERM

        def prices(c):
            x = A(pb, NP * t + 64 * c, NP * t + 64 * c + 64)
            for u in range(R):
                mm(A(BANK[c], u, 64 * R, R), A("N32"), x, True, True)

        def qsum(a, b):
            mm(A("pY%d" % (a // 128), 0, 2 * KW) + span(a, b), A(pb, NP * t + a, NP * t + b), A("BDQ"), False, False)

        def rounded(h):
            act(A("RR", 2 * KW * h, 2 * KW * h + 2 * KW), A("pY%d" % h, 0, 2 * KW), AF.Identity, bias=RO, scale=1.0 / 65536)

        if early:
            for c in (2, 0, 1):
                prices(c)
            qsum(128, V0)
            qsum(0, 128)
        else:
            prices(2)
            prices(3)
            qsum(128, NP)
        ranks(keys[1], 64)
        kin(128, V0)
        wealth(128, V0)
        kin(V0, NP)
        kin(0, 128)
        if early:
            tt(A("G", 16 * V0, 16 * NP), IND(Xg, A("CU", V0, NP)), A("P16"), op.add)
            ts(A("KC"), A("CU"), -float(MID), op.add)
            ts(A("M", 16 * V0, 16 * NP), A("G", 16 * V0, 16 * NP), -OFF, op.add, 0.0, op.max)
        else:
            ts(A("G", 16 * V0, 16 * NP), IND(Xg, A("CU", V0, NP)), -OFF, op.add)
            ts(A("KC"), A("CU"), -float(MID), op.add)
        wealth(0, 64)
        gsum(128, NP)
        for h in (1, 0):
            persons(half("pK", h), h, h == 0)
        if early:
            least(128, V0, (128, NP))
        else:
            prices(0)
            prices(1)
            qsum(0, 128)
            least(128, 192)
            least(192, NP, (128, NP))
        mm(A("pD", 0, NP), A("IDB"), A("MASK"), True, False)
        wealth(64, LAST)
        wealth(LAST, 128)
        least(0, 64)
        rounded(1)
        act(A("D1"), A("pK", 0, 2 * KW), AF.Identity)
        gsum(0, LAST)
        least(64, LAST)
        gsum(LAST, 128)
        scored(1)
        least(LAST, 128, (0, 128))
        ranks(keys[0], 64)
        least_key(1)
        ts(A("pL", 2, 48, 3), e, float(F0), op.add)
        to_list(1)
        for _ in range(min(len(spare), 8)):
            spare.pop(0)()
        rounded(0)
        scored(0)
        act(A("T4"), price, AF.Identity, bias=163.375, scale=-0.25)
        act(A("SCE"), A("KC"), AF.Identity, bias=A("EVM"), scale=A("EVN"))

        big = 1.5 * 2.0 ** 35

        def third(n, h, k):
            return A(n, 24 * h + k, 24 * h + 24, 3)

        def decode(h):
            ts(third("RB", h, 1), third("pL", h, 0), big, op.add, -big, op.add)
            ts(third("RB", h, 2), third("pL", h, 0), -65536.0, op.add, float(MID), op.max)

        def keyed(h):
            scan(A("KL", 24 * h, 24 * h + 24), A("RB", 24 * h, 24 * h + 24), A("pL", 24 * h, 24 * h + 24), 0.0, op.subtract, op.min)

        def keyrow(q, a, b):
            x, y = A("KR", a, b), IND(A("IOTA"), A("KU", a // 16, b // 16))
            cp(x, y) if q == "V" else act(x, y, AF.Identity)

        def first(h):
            cp(A("KH", 8 * h, 8 * h + 8), third("KL", h, 2))

        def second(h):
            tt(A("KH", 16 + 8 * h, 24 + 8 * h), third("KL", h, 2), A("KH", 8 * h, 8 * h + 8), op.subtract)

        def distances(j0, j1):
            for j in range(j0, j1):
                act(ROWS("EA", j - NV, j - NV + 1, 0, NP - 16 * j), A("KR", 16 * j, NP), AF.Abs, bias=A("KL", 3 * j + 2, 3 * j + 3), scale=-1.0)

        def clipped(j0, j1):
            act(ROWS("E", j0, j1, 0, NP - 16 * j0), ROWS("EA", j0 - NV, j1 - NV, 0, NP - 16 * j0), AF.Relu, bias=1.0, scale=-1.0)

        def row(j):
            ts(ROWS("E", j, j + 1, 0, NP - 16 * j), A("KR", 16 * j, NP), A("KH", j, j + 1), op.subtract, A("KH", 16 + j, 17 + j), op.is_equal)

        def tail(j):
            mm(A("pD", 16 * j + 16, NP), A("BDB"), ROWS("E", j, j + 1, 16, NP - 16 * j), False, False)

        def heads(j0, j1, stop=False):
            mm(A("pD", 16 * j0, 16 * j1), A("LOW"), ROWS("E", j0, j1, 0, 16), False, stop)

        high = list(range(8, NV))

        def ahead(n):
            for _ in range(n):
                row(high[0])
                tail(high.pop(0))

        fillers(2)
        decode(1)
        least_key(0)
        keyed(1)
        act(A("KU", 8, 16), third("KL", 1, 2), AF.Identity)
        keyrow("S", 128, NP)
        to_list(0)
        first(1)
        fillers(1)
        second(1)
        distances(NV, 16)
        clipped(NV, 16)
        fillers(1)
        decode(0)
        ahead(2)
        keyed(0)
        ahead(2)
        cp(A("KU", 0, 8), third("KL", 0, 2))
        first(0)
        keyrow("S", 64, 128)
        fillers(1)
        keyrow("V", 0, 64)
        second(0)
        act(A("BU"), A("KL", 1, 48, 3), AF.Identity, bias=float(MID), scale=-1.0)
        act(A("TRM", 15, NP, 16), A("KL", 2, 48, 3), AF.Identity)
        mm(A("pD", 15, NP, 16), A("ID15"), A("KL", 2, 48, 3), False, False)
        for j in range(NV, 15):
            tail(j)
        heads(8, 16)
        fillers(1)
        for j in range(8):
            row(j)
            tail(j)
            if j == 5:
                heads(0, 6)
        heads(6, 8, True)

        def newkin():
            act(A("SKF"), IND(Kg if t else A("KI", 0, V), A("BU")), AF.Identity, scale=A("ODD"))
            if t == 0:
                act(A("OFD"), A("EQ"), AF.Identity, bias=8192.0 + MID, scale=-8192.0)
                act(A("K", SP - KS, SP), A("KI", V - KS, V), AF.Identity)
                act(A("IDHF"), A("IDB"), AF.Identity, scale=0.5)

        act(A("BR"), IND(A("IOTA"), A("BU")), AF.Identity)
        act(A("XG"), IND(Xg, A("BU")), AF.Identity)
        mm(A("pX", 0, NP), A("N32"), A("T4"), True, False)
        mm(A("pX", 0, NP), A("IDB"), A("XG"), False, True)
        if jub:
            cp(A("JB", 1, 48, 3), hold)
        fillers(3)
        while longer:
            longer.pop(0)()
        scan(A("FS"), A("TRM"), A("pD", 0, NP), 0.0, op.max, op.min)
        of2 = A("FS", 15, NP, 16)
        ofs = A("OFS", 16 * t, 16 * t + 16)
        cp(ofs, of2)

        def flags(a, b, targets):
            act(A("SG", a, b), IND(A("IOTA"), A(targets[0], targets[1] + a // 16, targets[1] + b // 16)), AF.Sign, bias=0.5 - V)

        def newwealth():
            emit("S", [A("XV"), ofs], [A("X")], lambda: g.scalar.activation(ap(IND(A("X"), ofs)), ap(A("XV")), AF.Silu))

        newkin()
        act(A("XV"), A("pX", 0, NP), AF.Identity, bias=160.0 * XS)
        if not jub:
            send(nxt, A("RO", 16 * t + 16, 16 * t + 32), ofs, "aO%d" % (t + 1))
            arrives(prv, A("RO", 16 * t + 16, 16 * t + 32), "aO%d" % (t + 1))
            arrives(prv, A("RP", NP * t + NP, NP * t + 2 * NP), "aP%d" % (t + 1))
            newwealth()
        else:
            mm(A("pQ", 0, NP), A("IDB"), price, True, False)
            flags(0, NP, ofs)
            mm(A("pQ", 0, NP), A("IDHF"), A("SG"), False, True)
            newwealth()
            act(A("PN"), A("pQ", 0, NP), AF.Relu, bias=-0.5 * XS, scale=XS)
        ho = A("HO", 16 * t, 16 * t + 16)
        if jub:
            ts(A("JA", 1, 48, 3), of2, float(V), op.is_lt)
            tt(A("JB", 0, 48, 3), of2, hold, op.subtract)
            cp(IND(A("H"), ofs), A("BR"))
            scan(A("JC"), A("JA"), A("JB"), 0.0, op.mult, op.add)
            tt(A("BR"), IND(A("H", F0, SP), e), A("CAP"), op.min)
            cp(A("RSJ", 1, NP, 16), A("JC", 2, 48, 3))
        else:
            ts(A("RL"), of2, float(V), op.is_lt)
            tt(A("BH"), of2, hold, op.subtract)
            cp(IND(A("H"), ofs), A("BR"))
            tt(A("BH2"), A("RL"), A("BH"), op.mult)
            fillers(1)
            tt(A("EG"), IND(A("H", F0, SP), e), A("OFD"), op.subtract)
            tt(ho, A("BH2"), hold, op.add)
            fillers(1)

        def kpart():
            tt(IND(A("K"), ofs), A("SKF"), A("SCE"), op.add)

        el = A("ES", 15, NP, 16)
        en = A("FO", 0, 16) if last else A("EN", 16 * t, 16 * t + 16)
        if not jub:
            scan(A("ES"), A("RSH"), A("EG"), -32768.0, op.add, op.max)
            fillers(1)
            ts(en, el, float(MID), op.add)
            send(nxt, A("RE", 16 * t + 16, 16 * t + 32), en, "aE%d" % (t + 1))
            n0 = NP * t + NP
            shares = (("pP", V0, NP), ("pQ", 0, V0))
            for x, a, b in shares:
                mm(A(x, a, b), A("IDB"), A("RP", n0 + a, n0 + b), True, False)
            prepare(t + 1)
            for x, a, b in shares:
                flags(a, b, A("RO", 16 * t + 16, 16 * t + 32))
                mm(A(x, a, b), A("IDHF"), A("SG", a, b), False, True)
            for k in range(0, 16, 4):
                act(A("P16", k, PW, 16), A("pP", V0, NP), AF.Relu, bias=-0.5 * XS, scale=XS)
            for x, a, b in shares[::-1]:
                act(A("PO", n0 + a, n0 + b), A(x, a, b), AF.Relu, bias=-0.5)
            fillers(len(pend))
            kpart()
            doubled(4)
            send(nxt, A("RH", 16 * t + 16, 16 * t + 32), ho, "aH%d" % (t + 1))
            doubled(2)
        else:
            scan(A("EXP"), A("RSJ"), A("BR"), 0.0, op.add, op.max)
            cp(en, A("EXP", 15, NP, 16))
            if not last:
                send(nxt, A("RE", 16 * t + 16, 16 * t + 32), en, "aE%d" % (t + 1))
                prepare(t + 1)
            sums = A("pL", 64, 80)
            mm(sums, A("WBD"), A("C160"), True, False)
            todo = list(range(NF, NB))

            def halved(n):
                b0, b1 = todo[0], min(todo[0] + n, NB)
                del todo[:n]
                ts(A("M", 128 * b0, 128 * b1), A("K", F0 + 128 * b0, F0 + 128 * b1), -float(MID), op.add)

            def whole(b0, b1):
                for b in range(b0, b1):
                    mm(A("pP", b, 8 * NB, NB), A("K", F0 + 128 * b, F0 + 128 * b + 128), A("YF"), False, False)

            if last:
                kpart()
                mm(A("pP", 0, 8 * NB), A("ONE") + lane(0), A("YC") + lane(0), True, False)
                whole(0, 8)
            halves = ((0, 0, NP),) if last else ((1, 128, NP), (0, 0, 128))
            for h, a, b in halves:
                tt(A("PJ1", a, b), IND(Xg, (en[0], en[1] + a // 16, en[1] + b // 16, 1)), A("PN", a, b), op.subtract)
            if last:
                halved(1)
            for h, a, b in halves:
                ts(A("PJ2", a, b), A("PJ1", a, b), 0.5 / XS, op.mult, 167.25, op.add)
                if not last:
                    act(A("PO", a, b), A("PJ2", a, b), AF.Identity, bias=175.0, scale=-1.0)
                    send(nxt, A("RP", NP * t + NP + a, NP * t + NP + b), A("PO", a, b), "a%s%d" % ("PO"[h], t + 1))
            for j in range(16):
                mm(sums, A("WH", 15 - j, 143 - j), A("PJ2", j, NP, 16), False, j == 15)
            if last:
                whole(8, NF)
                halved(4)
                cp(A("HI"), sums)
                halved(1)
                ts(A("HA"), A("HI"), 4095, op.bitwise_and)
                halved(1)
                cp(A("FO", 16, 32), A("HA"))
                send(nxt, A("FIN"), A("FO"), "aF")
                halved(NB)
            else:
                kpart()
                act(A("HI"), sums, AF.Identity)

                def hnew(t=t, ho=ho):
                    tt(ho, A("HA"), A("HG"), op.add)
                    send(nxt, A("RH", 16 * t + 16, 16 * t + 32), ho, "aH%d" % (t + 1))
                pend.append(lambda: ts(A("HA"), A("HI"), 4095, op.bitwise_and))
                pend.append(lambda: ts(A("HG"), A("HA"), float(V), op.is_ge, -float(V), op.mult))
                pend.append(hnew)
        if last:
            outs = []
            outs.append(("Y", dma("Y", T.yh[:, :], T.H[0:128:16, F0:SP], [A("H", F0, SP)], [])))

            for a in range(0, V, V // 4):
                b = a + V // 4
                act(A("XB", a, b), A("X", a, b), AF.Relu, bias=-2.0 ** -10, scale=1.0 / XS)
                outs.append(("Y", dma("Y", T.yx[:, a:b], T.XB[:, a:b], [A("XB", a, b)], [])))
            for b in range(NF, NB):
                mm(A("pP", b, 8 * NB, NB), A("M", 128 * b, 128 * b + 128), A("YW"), False, b == NB - 1)
            arrives(prv, A("FIN"), "aF")
            cp(A("YA"), A("pP", 0, 8 * NB))
            act(A("YO"), IND(A("IOTA"), A("FIN", 0, 16)), AF.Identity)
            rows = ((0, 4 * NB),)
            for u in range(2):
                mm(A("pK", 128 * u, 128 * u + 128) + rows, A("YA", 4 * NB * u, 4 * NB * u + 4 * NB), A("IDF"), True, True)
            cp(A("YB") + rows, A("pK", 0, NP) + rows)
            cp(A("YT"), IND(A("KI"), A("FIN", 16, 32)))
            for u in range(2):
                outs.append(("Y", dma("Y", T.yk[4 * u:4 * u + 4, :], T.YB[0:4 * NB, 128 * u:128 * u + 128], [A("YB")], [])))
            for k, (y, o) in enumerate((("YT", T.yt), ("YO", T.yo))):
                outs.append(("YS"[k], dma("YS"[k], o[:, :], T[y][0:128:16, :], [A(y)], [])))
            for q, s in outs:
                queues[q].wait_ge(T.sem[s], 16)
            g.wait_ge(T.sem.loc, nloc[0])
            for s, n in count.items():
                g.wait_ge(T.sem[s], n)
